import numpy as np, ml_dtypes
CORES = [2,6,10,14,18,22,26,30]
N = 8
BF = ml_dtypes.bfloat16
P, D, SI, CAP, RO, PM, CM, LM = 768, 5, 3840, 256, 2, 1280, 6400, 49
DIST = np.array([0, 0, 0, 1, 3])
def home(r, s):
    return (r - DIST[s // P]) % N
def lengths(rng, pw, big):
    e = np.zeros(P, np.int64); e[rng.permutation(P)[:big]] = LM - 1; t = (D - 1) * P - big * (LM - 1)
    e = e + np.bincount(rng.permutation(P)[np.minimum((P * rng.random(t) ** pw).astype(np.int64), P - 1)], minlength=P)
    e = np.minimum(e, LM - 1); o = rng.permutation(P); room = LM - 1 - e[o]
    e[o] += np.clip((D - 1) * P - np.sum(e) - (np.add.accumulate(room) - room), 0, room)
    return e + 1
def lists(rng, pw, big):
    calls = np.argsort(rng.random((N, 8, SI)), axis=-1)
    lens = np.array([[lengths(rng, pw, big) for g in range(8)] for r in range(N)])
    rid = np.array([[np.repeat(np.arange(P), lens[r, g]) for g in range(8)] for r in range(N)])
    return calls, lens, rid
def change(rng, b, k):
    m = np.argsort(rng.random(b.shape), axis=1) < k[:, None]
    return np.where(m, (b + rng.integers(1, 15, b.shape)) % 15, b)
def paint(rng, rid, share, loose):
    base = rng.integers(0, 15, (P, 16)); other = change(rng, base, rng.choice(np.array([0, 2, 4, 9]), P))
    n = rng.choice(np.array([7, 8, 9, 10, 16]), P); two = rng.random(P) < share; pick = (rng.random(SI) < 0.4) & two[rid]; out = []
    for b in (base, other):
        c = np.where(pick[:, None], change(rng, b, n)[rid], b[rid])
        c = np.where(rng.random(c.shape) < 0.03, rng.integers(0, 15, c.shape), c)
        out.append(np.where(rng.random(c.shape) < loose, 15, c))
    return np.stack(out).astype(np.int8)
def formals(rng):
    return np.where(rng.random((N, 8, 16, P)) < 0.4, 15, rng.integers(0, 15, (N, 8, 16, P)))
def mixed(rng, a):
    return rng.permuted(np.tile(np.array(a), (N, 2)), axis=1)
def pack(calls, lens, c, v):
    jump = np.zeros((N, 8, 16, 2 * SI), np.int8)
    for r in range(N):
        for g in range(8):
            s = calls[r, g]; q = home(r, s)
            jump[q, g, :, s] = c[r, g, 0]; jump[q, g, :, SI + s] = c[r, g, 1]
    return {"jump": jump.reshape(N, 128, 2 * SI).astype(np.float32).astype(BF), "form": np.ascontiguousarray(v).reshape(N, 128, P).astype(np.float32).astype(BF),
            "calls": calls.astype(np.int32), "runs": lens.astype(np.int32)}
def setup_inputs(rng):
    calls, lens, rid = lists(rng, 1.5, 0); share = mixed(rng, [0.05, 0.2, 0.5, 0.9]); loose = mixed(rng, [0.03, 0.06, 0.12, 0.2])
    c = np.stack([np.stack([paint(rng, rid[r, g], share[r, g], loose[r, g]) for g in range(8)]) for r in range(N)])
    return pack(calls, lens, c, formals(rng))
def setup_inputs_spread(rng):
    calls, lens, rid = lists(rng, 3.0, 0); q = mixed(rng, [0.2, 0.5, 0.8, 0.95])
    ex = np.where(rng.random((N, 8, 16)) < q[:, :, None], 12.0, rng.choice(np.array([0.25, 1.0, 3.0]), (N, 8, 16)))
    c = np.minimum((16 * rng.random((N, 8, 2, SI, 16)) ** ex[:, :, None, None, :]).astype(np.int8), 15)
    v = np.minimum((16 * rng.random((N, 8, 16, P)) ** ex[:, :, :, None]).astype(np.int8), 15)
    return pack(calls, lens, c, v)
def setup_inputs_ends(rng):
    n = (D - 1) * P // (LM - 1); half = np.arange(SI // 2); zig = np.stack([half, SI - 1 - half], axis=1).reshape(-1)
    calls = np.argsort(rng.random((N, 8, SI)), axis=-1)
    for r in range(N):
        for g in range(1, 8, 2): calls[r, g] = np.roll(zig, int(rng.integers(0, SI)))
    big = np.concatenate([np.argsort(rng.random((N, 8, P - 1)), axis=-1) < n - 1, np.ones((N, 8, 1), bool)], axis=-1); lens = np.where(big, LM, 1)
    lane = np.arange(16); m = np.stack([lane < 0, lane >= 0, lane >= 7, lane >= 8])
    kind = np.stack([rng.choice(5, (N, 8, SI), p=[0.06, 0.7, 0.1, 0.08, 0.06]), rng.choice(5, (N, 8, SI), p=[0.3, 0.3, 0.15, 0.15, 0.1])], axis=2)
    kind[..., SI - LM] = 0; kind[..., SI - 2] = 3; kind[..., SI - 1] = 2
    c = np.where((kind == 4)[..., None], rng.random(kind.shape + (16,)) < 0.5, m[np.minimum(kind, 3)]).astype(np.int8) * 15
    kv = rng.choice(5, (N, 8, P), p=[0.25, 0.5, 0.1, 0.1, 0.05])
    v = np.where((kv == 4)[..., None], rng.random(kv.shape + (16,)) < 0.5, m[np.minimum(kv, 3)]).astype(np.int8).transpose(0, 1, 3, 2) * 15
    for r in range(N):
        for g in range(8):
            for k in (SI - 2, SI - 1):
                s = int(calls[r, g, k]); v[int(home(r, s)), g, :, s % P] = 15
    return pack(calls, lens, c, v)
def setup_inputs_corners(rng):
    calls, lens, rid = lists(rng, 1.0, 4); c = np.zeros((N, 8, 2, SI, 16), np.int8)
    v = formals(rng); v[:, :, 0] = 15
    for r in range(N):
        for g in range(8):
            n = (CAP, CAP + 1, P, CAP - 1, 1, 0, CAP, CAP - 1)[(g + r) % 8]; L = lens[r, g]; d = rid[r, g]
            hot = np.zeros(P, bool); hot[rng.permutation(np.flatnonzero(L >= 2))[:n]] = True
            pos = np.arange(SI) - (np.add.accumulate(L) - L)[d]; how = rng.integers(0, 3, P)[d]
            m = hot[d] & (pos > 0) & np.where(how == 0, pos == L[d] - 1, np.where(how == 1, pos == 1, True))
            b = rng.integers(0, 15, (P, 16))[d]; x = change(rng, b, np.full(SI, 8)); x = np.where((x != b) & (rng.random(x.shape) < 0.3), 15, x)
            c[r, g, 0] = np.where((pos == 0)[:, None], b, np.where(m[:, None], change(rng, b, np.full(SI, 9)), x))
            c[r, g, 1] = paint(rng, d, 0.5, 0.1)[1]
    return pack(calls, lens, c, v)
def long_lists(rng, calls, lens, rid, r, g):
    L = lens[r, g]; two = np.flatnonzero(L == 2)[:min(LM - 1, CAP // 4)]; n = len(two)
    front = np.concatenate([np.flatnonzero(L == LM)[:1], two, np.flatnonzero(L == 1)[:3]])
    lens[r, g] = np.concatenate([L[front], np.delete(L, front)]); rid[r, g] = np.repeat(np.arange(P), lens[r, g])
    p = np.arange(1, n + 1); u = LM + 2 * n
    at = np.concatenate([rng.permutation(LM - 1)[:n], LM + 2 * p - 2, LM + 2 * p - 1, np.array([LM - 1, u, u + 1, u + 2])])
    s = np.concatenate([2 * P + p, p, P + p, np.array([n + 1, n + 2, n + 3, P + n + 3])])
    a = np.full(SI, -1, np.int64); a[at] = s; a[a < 0] = rng.permutation(np.setdiff1d(np.arange(SI), s)); calls[r, g] = a
    return n
def long_values(rng, c, v, r, g, n):
    b = rng.integers(0, 15, 16); A = rng.integers(0, 15, (n, 16)); u = LM + 2 * n; k = LM + 2 * np.arange(n)
    z = np.concatenate([change(rng, np.tile(b[:15], (LM - 2, 1)), np.full(LM - 2, 7)), np.full((LM - 2, 1), (b[15] + 1) % 15)], axis=1)
    c[r, g, :, 0] = b; c[r, g, :, 1:LM - 1] = z; c[r, g, :, LM - 1] = np.where(rng.permutation(16) < 9, 15, b)
    c[r, g, 0, k] = A; c[r, g, 0, k + 1] = (A + 1) % 15; c[r, g, 1, LM:u] = 15
    c[r, g, :, u:u + 2] = 15; c[r, g, :, u + 2] = (b + 1) % 15
    v[r, g, 0] = 15; v[r, g, :, n + 1:n + 4] = b[:, None]
def deep_lists(rng, calls, lens, rid, r, g):
    m = (0, 1, 1, 3)[r % 4]; L = lens[r, g]; n = LM // 2; h = n + 9; p = np.arange(7, h)
    front = np.concatenate([np.flatnonzero(L == x)[:y] for x, y in ((LM, 6), (3, 1), (2, n + 2), (1, 2))])
    lens[r, g] = np.concatenate([L[front], np.delete(L, front)]); rid[r, g] = np.repeat(np.arange(P), lens[r, g])
    quiet = rng.permutation((np.arange(4)[:, None] * P + np.arange(h + 2, h + 66)).reshape(-1))[:5 * LM + m]
    grow = rng.permutation(np.concatenate([2 * P + p[2:], 3 * P + p[2:]]))[:LM - 1 - m]
    s = np.concatenate([quiet[:5 * LM], np.array([6]), grow, quiet[5 * LM:], np.array([2 * P + 7, 2 * P + 8, h]), np.stack([p, P + p], axis=1).reshape(-1), np.array([h + 1, P + h + 1])])
    calls[r, g] = np.concatenate([s, rng.permutation(np.setdiff1d(np.arange(SI), s))])
def deep_values(rng, c, v, lens, rid, r, g):
    w = r % 4; m = (0, 1, 1, 3)[w]; some = (0, LM - 33, 0, LM - 16)[w]; n = LM // 2; h = n + 9; u = 5 * LM; k = u + LM; e = k + 3 + 2 * (n + 2)
    b = rng.integers(0, 15, 16); star = (b + 7) % 15; o = rng.permutation(16)
    stay = np.concatenate([np.array([False]), rng.permutation(np.arange(LM - 3 - m) < some), np.array([False]), np.full(m, w == 3)])
    z = np.tile(b, (LM - 1, 1)); z[:, o[:4]] = (z[:, o[:4]] + rng.integers(0, 2, (LM - 1, 4))) % 15
    half = b.copy(); half[o[8:]] = star[o[8:]]; z[stay] = half
    if w == 1 or w == 2: z[-1, o[4:8]] = (b[o[4:8]] + 1) % 15
    if w == 3: z[-1, o[8]] = b[o[8]]; z[-1, o[0]] = star[o[0]]
    c[r, g, :, :u] = b; c[r, g, 0, u] = star; c[r, g, 1, u] = b; c[r, g, :, u + 1:k] = z
    a = rng.integers(0, 15, 16); A = rng.integers(0, 15, (n + 2, 16)); A[0] = a; t = k + 3 + 2 * np.arange(n + 2)
    c[r, g, 0, k] = a; c[r, g, 0, k + 1] = (a + 1) % 15; c[r, g, 1, k:k + 2] = 15; c[r, g, :, k + 2] = np.where(np.arange(16) == 0, 15, a)
    c[r, g, 0, t] = A; c[r, g, 0, t + 1] = (A + 1) % 15; c[r, g, 1, k + 3:e] = 15
    c[r, g, :, e] = 15; c[r, g, :, e + 1] = (a + 1) % 15
    top = int(np.sum(lens[r, g, :h + 66])); c[r, g, :, e + 2:top] = rng.integers(0, 15, (P, 16))[rid[r, g, e + 2:top]]
    v[r, g, 0] = 15; v[r, g, 0, 6] = a[0]; v[r, g, :, h:h + 2] = a[:, None]
def setup_inputs_crowd(rng):
    calls, lens, rid = lists(rng, 1.0, (D - 1) * P // (LM - 1) // 2); c = np.zeros((N, 8, 2, SI, 16), np.int8); v = formals(rng)
    for r in range(N):
        for g in range(8):
            grow = RO == 4 and g == 7; n = long_lists(rng, calls, lens, rid, r, g) if grow else 0
            deep = RO == 4 and g == 3
            if deep: deep_lists(rng, calls, lens, rid, r, g)
            L = lens[r, g]; d = rid[r, g]; pos = np.arange(SI) - (np.add.accumulate(L) - L)[d]; last = (pos == L[d] - 1)[:, None]
            hot = np.zeros(P, bool); hot[rng.permutation(np.flatnonzero(L >= 2))[:CAP - 1]] = True
            for i in range(2):
                b = rng.integers(0, 15, (P, 16))[d]; x = (b + pos[:, None]) % 15
                if g % 4 == 1: x = np.where(last, b, x)
                if g % 4 == 2 and i == 0: x = np.where(hot[d][:, None], x, b)
                if g % 4 == 3 and i == 0: x = b
                x[:, 13:] = np.where(rng.random((SI, 3)) < 0.5, 15, x[:, 13:])
                c[r, g, i] = x
            if g % 4 >= 2: v[r, g, 0] = 15
            if grow: long_values(rng, c, v, r, g, n)
            if deep: deep_values(rng, c, v, lens, rid, r, g)
    return pack(calls, lens, c, v)
def setup_inputs_calm(rng):
    calls, lens, rid = lists(rng, 3.0, 0); c = np.zeros((N, 8, 2, SI, 16), np.int8); v = formals(rng)
    for r in range(N):
        for g in range(8):
            L = lens[r, g]; d = rid[r, g]; first = np.add.accumulate(L) - L; cs = calls[r, g]
            base = rng.integers(0, 15, (P, 16)); o = np.argsort(rng.random((P, 16)), axis=1)
            one = np.where(o < 6, 15, base); two = np.where((o == 6) | (o == 7), (base + 1) % 15, one)
            c[r, g, 0] = one[d]; c[r, g, 1] = two[d]
            ones = [int(a) for a in rng.permutation(np.flatnonzero(L == 1))]; more = [int(a) for a in rng.permutation(np.flatnonzero(L >= 2))]
            for t in range(RO):
                for i in range((g + r + t) % 4):
                    if len(ones) < t + 1 or len(more) < 1: continue
                    x = more.pop(); ys = [ones.pop() for a in range(max(t, 1))]; by_pass = (i + t + r) % 2 == 0
                    lo = int(first[x]); at = lo + int(L[x]) - 1; b = base[x]
                    c[r, g, :, lo:at + 1] = b
                    if by_pass: c[r, g, :, at] = np.where(rng.permutation(16) < 9, 15, b)
                    else: c[r, g, 1, at] = np.where(rng.permutation(16) < 9, (b + 1) % 15, b)
                    put = [(at, ys[0])] + [(int(first[ys[a]]), ys[a + 1]) for a in range(len(ys) - 1)]
                    for k, s in put:
                        w = int(np.flatnonzero(cs == s)[0]); cs[w] = cs[k]; cs[k] = s
                    for y in ys:
                        if by_pass: v[r, g, :, y] = b
                        else: v[r, g, 0, y] = 15
                    for y in ys[:-1]: c[r, g, :, int(first[y])] = 15
                    if t > 0: c[r, g, :, int(first[ys[-1]])] = (b + 1) % 15
                    elif by_pass: v[r, g, :, ys[0]] = (b + 1) % 15
                    else: v[r, g, 0, ys[0]] = 3
    return pack(calls, lens, c, v)
def check_inputs(d):
    bad = []
    for k, lo, hi in (("jump", 0, 15), ("form", 0, 15), ("calls", 0, SI - 1), ("runs", 1, LM)):
        a = np.asarray(d[k]).astype(np.float64)
        if not (np.min(a) >= lo and np.max(a) <= hi): bad.append("range of " + k)
        if np.any(np.floor(a) != a): bad.append("whole numbers in " + k)
    if np.any(np.sort(np.asarray(d["calls"]), axis=-1) != np.arange(SI)): bad.append("permutation in calls")
    if np.any(np.sum(np.asarray(d["runs"]).astype(np.int64), axis=-1) != SI): bad.append("sum of runs")
    return bad
def reference(jump, form, calls, runs):
    J = jump.astype(np.float32).astype(np.int16).reshape(N, 8, 16, 2 * SI)
    V = np.full((N, 8, 16, PM), 15, np.int16); V[..., :P] = form.astype(np.float32).astype(np.int16).reshape(N, 8, 16, P)
    cnt = np.full((N, 8), P, np.int64); state = {}
    for r in range(N):
        for g in range(8):
            s = calls[r, g].astype(np.int64); state[r, g] = (s, s % P, np.repeat(np.arange(P), runs[r, g]))
    for rnd in range(RO):
        V2 = np.full_like(V, 15); clone = np.full((N, 8, PM), -1, np.int64); mid = {}
        for r in range(N):
            for g in range(8):
                s, c, e = state[r, g]; q = home(r, s)
                F = V[q, g, :, c]
                a = J[q, g, :, s + SI * (F[:, 0] < 15)]; A = np.where(a < 15, a, F)
                first = np.append(True, e[1:] != e[:-1]); at = np.flatnonzero(first); rid = np.add.accumulate(first.astype(np.int64)) - 1
                dis = np.add.reduce((A != A[at[rid]]).astype(np.int64), axis=1) >= 9
                has = np.maximum.reduceat(dis.astype(np.int64), at); before = np.add.accumulate(has) - has
                split = (has == 1) & (before < CAP); num = cnt[r, g] + before
                clone[r, g, e[at[split]]] = num[split]
                mv = dis & split[rid]; e = np.where(mv, num[rid], e)
                o = np.argsort(2 * rid + mv, kind="stable"); s, c, e, A = s[o], c[o], e[o], A[o]
                at = np.flatnonzero(np.append(True, e[1:] != e[:-1]))
                lo = np.minimum.reduceat(A, at, axis=0); hi = np.maximum.reduceat(A, at, axis=0)
                V2[r, g][:, e[at]] = np.where(lo == hi, lo, 15).T
                cnt[r, g] += np.count_nonzero(split); mid[r, g] = (s, c, e)
        for r in range(N):
            for g in range(8):
                s, c, e = mid[r, g]; to = clone[home(r, s), g, c]
                o = np.repeat(np.arange(len(s)), 1 + (to >= 0)); dup = np.append(False, o[1:] == o[:-1])
                state[r, g] = (s[o], np.where(dup, to[o], c[o]), e[o])
        V = V2
    y = np.full((3, N, 8, CM), -1, np.float32)
    for r in range(N):
        for g in range(8):
            for i in range(3): y[i, r, g, :len(state[r, g][i])] = state[r, g][i]
    return {"ysite": y[0], "ycaller": y[1], "ycallee": y[2], "yform": V.reshape(N, 128, PM).astype(np.float32).astype(BF)}

@@ -1,0 +1,772 @@
+from concourse.bass import DstId, RemoteDMATransfer
+from concourse.mybir import AluOpType as OP, ActivationFunctionType as AF
+
+F32, B16, I32, U16 = "float32", "bfloat16", "int32", "uint16"
+NR = 8
+NL = (3840, 5120, 6400)
+NP = (768, 1024)
+MAG = 12582912.0
+SHARE = (3840, 2560)
+
+
+def _s(cols, dtp):
+    return ("sbuf", [128] + (cols if isinstance(cols, list) else [cols]), dtp)
+
+
+def _p(cols):
+    return ("psum", [128, cols], F32)
+
+
+SCRATCH = {
+    "J": _s(7680, B16), "T0": _s(3840, B16), "T1": _s(5120, B16),
+    "A": _s(5136, B16), "NQ": _s(5120, B16), "E": _s(5136, F32), "R": _s(5136, F32),
+    "CL0": _s(3840, B16), "CL1": _s(5120, B16), "W1": _s(6400, F32), "W2": _s(6400, F32),
+    "K32": _s(400, F32), "KM": _s(400, F32),
+    "FV": _s(1296, B16), "VAL": _s(1280, B16), "T15": _s(1280, B16), "PS": _s(2312, F32),
+    "BC": _s(2048, B16), "ZS": _s(144, B16), "ZT": _s(144, B16), "ZC": _s(144, B16), "ZD": _s(144, B16), "ZF": _s(144, F32),
+    "XR": _s(144, F32), "GM": _s(128, B16), "BLK": _s(128, B16), "BLKF": _s(128, F32), "IDN": _s(128, B16), "N16": _s(128, B16),
+    "N8": _s(128, B16), "C85": _s(320, B16),
+    "TRI": _s(128, B16), "TRIF": _s(128, F32), "SHD": _s(128, B16), "SHDF": _s(128, F32), "SHU": _s(128, B16), "SHUF": _s(128, F32),
+    "COL": _s(16, F32), "PI": _s(4, I32), "TMP": _s(8, F32), "CX": _s(320, F32),
+    "ZB": _s(320, B16), "WO": _s(48, U16),
+    "CB": _s(240, I32), "RB": _s(48, I32),
+    "PD": _s([20, 32], F32), "PT": _s(640, F32), "FD": _s([2, 32], F32), "LD": _s([4, 32], F32), "PT2": _s(128, F32),
+    "UW": _s(320, U16), "LW": _s(320, U16), "NW": _s(320, U16), "PW": _s(320, U16), "AO": _s(64, U16), "SO": _s(64, U16),
+    "LP0": _s(64, U16), "LP1": _s(80, U16), "YO": _s(80, U16), "BODY": _s(64, F32), "E257": _s(80, F32),
+    "S1": _s(80, F32), "S2": _s(80, F32), "S3": _s(80, F32),
+    "NF": _s(328, B16), "DIS": _s(328, B16), "OM": _s(328, B16), "BE": _s(328, B16), "MV": _s(320, B16), "FDB": _s(320, B16),
+    "H1": _s(320, B16), "H2": _s(320, B16), "H3": _s(320, B16), "H4": _s(320, B16), "VLD": _s(320, B16), "D0": _s(320, B16),
+    "G1": _s(400, F32), "G2": _s(400, F32), "G3": _s(400, F32), "G4": _s(400, F32), "G5": _s(404, F32), "G6": _s(320, F32),
+    "GI": _s(320, I32), "GJ": _s(320, I32), "CEF": _s(320, F32), "BS": _s(240, F32), "UB": _s(320, F32), "KP": _s(400, B16),
+    "Z": _s([4, 404], F32),
+    "PA": _p(1024), "PC": _p(512), "PE1": _p(512), "PE2": _p(512), "PM": _p(512), "PK": _p(512), "PX": _p(512),
+}
+ALIAS = {"AB0": ("NQ", 0), "AB1": ("NQ", 1024), "TS": ("NQ", 2048), "F240": ("NQ", 4096), "TI": ("T15", 0),
+         "AB2": ("A", 0), "J0": ("J", 0), "J1": ("J", 1536), "J2": ("J", 3072), "J3": ("J", 4608), "J4": ("J", 6144),
+         "PF": ("PS", 0), "SW": ("PS", 1024), "ZI": ("GI", 0), "ZJ": ("GJ", 0), "P0": ("PA", 0), "P1": ("PA", 512)}
+SEMAPHORES = ["qv", "qs", "qp", "qg"] + ["d%d" % i for i in range(100)] + ["r%d" % i for i in range(8)] + ["l%d" % i for i in range(8)]
+
+
+def rank_program(g, core, T, topo):
+    rank = T.rank_of(core)
+    if rank is None:
+        return
+    Q = {"v": g.vector, "s": g.scalar, "p": g.tensor, "g": g, "y": g.sync}
+    count = {"qv": 0, "qs": 0, "qp": 0, "qg": 0}
+    final = {}
+    waited = {q: {} for q in Q}
+    seen = {}
+    nd = [0]
+
+    def X(name, lo, hi, step=1, rows=None):
+        name, o = ALIAS.get(name, (name, 0))
+        lo, hi = lo + o, hi + o
+        pm, ps = (0xFFFF, slice(None)) if rows is None else (1 << rows, slice(rows, 128, 16))
+        return (T[name][ps, slice(lo, hi, step) if step != 1 else slice(lo, hi)], [(name, pm, lo, hi)])
+
+    def RV(name, lo, hi):
+        name, o = ALIAS.get(name, (name, 0))
+        lo, hi = lo + o, hi + o
+        return (T[name][:, slice(hi - 1, lo - 1 if lo > 0 else None, -1)], [(name, 0xFFFF, lo, hi)])
+
+    def X3(name, a, b, lo, hi):
+        w = SCRATCH[name][1][2]
+        return (T[name][:, a:b, lo:hi], [(name, 0xFFFF, k * w + lo, k * w + hi) for k in range(a, b)])
+
+    def X2(name, a, lo, hi):
+        w = SCRATCH[name][1][2]
+        return (T[name][:, a, lo:hi], [(name, 0xFFFF, a * w + lo, a * w + hi)])
+
+    def IN(win, off):
+        return (win[0].indirect(off[0]), win[1], off[1])
+
+    def HB(ap_):
+        return (ap_, [])
+
+    def sync(q, reads, writes, dma_):
+        need = {}
+        for regs, isw in ((reads, False), (writes, True)):
+            for (nm, pm, lo, hi) in regs:
+                ps = SCRATCH[nm][0] == "psum"
+                for (tok, oq, ow, opm, olo, ohi) in seen.get(nm, []):
+                    same = oq == q and not dma_
+                    if ps and not same:
+                        hit = lo // 512 <= (ohi - 1) // 512 and olo // 512 <= (hi - 1) // 512
+                    else:
+                        hit = (pm & opm) and lo < ohi and olo < hi and (ow or isw) and not (same and q == "p")
+                    if hit:
+                        need[tok[0]] = max(need.get(tok[0], 0), tok[1])
+        for s_, v_ in need.items():
+            if waited[q].get(s_, 0) < v_:
+                Q[q].wait_ge(T.sem[s_], v_)
+                waited[q][s_] = v_
+
+    def note(tok, q, reads, writes):
+        final[tok[0]] = max(final.get(tok[0], 0), tok[1])
+        for regs, isw in ((reads, False), (writes, True)):
+            for (nm, pm, lo, hi) in regs:
+                seen.setdefault(nm, []).append((tok, q, isw, pm, lo, hi))
+
+    def op(q, fn, out, ins, more=None):
+        reads, writes = [], list(out[1])
+        if len(out) == 3:
+            reads += out[2]
+        for i in ins:
+            if isinstance(i, tuple):
+                reads += i[1] + (i[2] if len(i) == 3 else [])
+        if more:
+            writes += more[1]
+        sync(q, reads, writes, False)
+        count["q" + q] += 1
+        fn().then_inc(T.sem["q" + q], 1)
+        note(("q" + q, count["q" + q]), q, reads, writes)
+
+    def ap(x):
+        return x[0] if isinstance(x, tuple) else x
+
+    def dma(out, in_, q="y"):
+        sync(q, in_[1], out[1], True)
+        sem = "d%d" % nd[0]
+        nd[0] += 1
+        Q[q].dma_start(out[0], in_[0]).then_inc(T.sem[sem], 16)
+        note((sem, 16), "dma", in_[1], out[1])
+
+    def cp(o, i): op("v", lambda: g.vector.tensor_copy(o[0], i[0]), o, [i])
+    def ms(o, c): op("v", lambda: g.vector.memset(o[0], c), o, [])
+    def tt(o, a, b, f): op("v", lambda: g.vector.tensor_tensor(o[0], a[0], b[0], f), o, [a, b])
+
+    def ts(o, a, s1, f1, s2=None, f2=None):
+        if f2 is None:
+            op("v", lambda: g.vector.tensor_scalar(o[0], a[0], ap(s1), None, f1), o, [a, s1])
+        else:
+            op("v", lambda: g.vector.tensor_scalar(o[0], a[0], ap(s1), ap(s2), f1, f2), o, [a, s1, s2])
+
+    def scan(o, a, b, ini, f0, f1): op("v", lambda: g.vector.tensor_tensor_scan(o[0], a[0], b[0], ap(ini), f0, f1), o, [a, b, ini])
+    def tr(o, i): op("v", lambda: g.vector.transpose(o[0], i[0]), o, [i])
+
+    def act(o, i, bias=0.0, scale=1.0, fn=AF.Identity, acc=None):
+        if fn == AF.Silu:
+            op("s", lambda: g.scalar.activation(o[0], i[0], fn), o, [i])
+        elif acc is None:
+            op("s", lambda: g.scalar.activation(o[0], i[0], fn, bias=ap(bias), scale=ap(scale)), o, [i, bias, scale])
+        else:
+            op("s", lambda: g.scalar.activation(o[0], i[0], fn, accum_out=acc[0]), o, [i], acc)
+
+    def mm(o, l, r, start=True, stop=True): op("p", lambda: g.tensor.matmul(o[0], l[0], r[0], start, stop), o, [l, r])
+
+    def iota(o, pat, base, cm, fl=True):
+        if fl:
+            op("g", lambda: g.iota(o[0], pat, base, cm, allow_small_or_imprecise_dtypes=True), o, [])
+        else:
+            op("g", lambda: g.iota(o[0], pat, base, cm), o, [])
+
+    def aff(o, i, pat, f, base, cm): op("g", lambda: g.affine_select(o[0], i[0], pat, f, 0.0, base, cm), o, [i])
+
+    def gat(q, o, win, off):
+        if q == "s":
+            act(o, IN(win, off))
+        else:
+            cp(o, IN(win, off))
+
+    def addc(q, o, i, c):
+        if q == "s":
+            act(o, i, bias=c)
+        else:
+            ts(o, i, c, OP.add)
+
+    def common(src, dsts):
+        e = [k for k in topo.engines(src, dsts[0]) if all(k in topo.engines(src, d) for d in dsts)]
+        n = 1
+        while 2 * n <= min(len(e), 8):
+            n *= 2
+        return e[-n:]
+
+    def peer(r, d):
+        return T.cores[(r + d) % NR]
+
+    def send(k, src, dsts):
+        e = common(core, [peer(rank, d) for d, _, _ in dsts])
+        sync("g", src[1], [], True)
+        per = len(e) // len(dsts)
+        trs = []
+        for x, (d, reg, rs) in enumerate(dsts):
+            rid, pid, _ = topo.addr(peer(rank, d))
+            trs.append((rid, pid, sum(1 << b for b in e[x * per:(x + 1) * per]), reg, rs))
+        if len(trs) == 1:
+            rid, pid, mk, reg, rs = trs[0]
+            g.remote_dma(reg[0], src[0], T.sem["r%d" % rs], T.sem["l%d" % k], pid, rid, mk)
+        else:
+            g.remote_dma_fused([RemoteDMATransfer(dst_ids=[DstId(rid=rid, pnc=pid)], dma_engine_mask=mk, remote_sem=T.sem["r%d" % rs],
+                                                  src=src[0], dst=reg[0]) for rid, pid, mk, reg, rs in trs], local_sem=T.sem["l%d" % k])
+        note(("l%d" % k, per * len(dsts)), "dma", src[1], [])
+
+    DIST = {3: 1, 4: 3}
+    for r in range(2):
+        for j in (3, 4):
+            sr = (rank - DIST[j]) % NR
+            n1 = len(common(T.cores[sr], [core]))
+            note(("r%d" % (4 * r + j - 3), n1), "dma", [], X("T%d" % r, j * NP[r], (j + 1) * NP[r])[1])
+            n2 = len(common(T.cores[sr], [peer(sr, 1), peer(sr, 3)])) // 2
+            note(("r%d" % (4 * r + j - 1), n2), "dma", [], X("CL%d" % r, j * NP[r], (j + 1) * NP[r])[1])
+
+    def col(k): return X("COL", k, k + 1)
+    def mat(name): return X(name, 0, 128)
+    WSEG = {15: 0, 20: 16, 3: 36, 4: 40, 1: 44}
+    pe = [0]
+
+    def small():
+        pe[0] += 1
+        return "PE%d" % (1 + pe[0] % 2)
+
+    def carry(m_, cols):
+        b = small()
+        for x, c_ in enumerate(cols):
+            mm(X(b, 0, 1), mat(m_), c_, x == 0, x == len(cols) - 1)
+        return X(b, 0, 1)
+
+    def half(m): return X3("PD", 0, m // 16, 0, 16)
+
+    def twin(m): act(X3("PD", 0, m // 16, 16, 32), half(m))
+
+    def turn(out, m):
+        M = m // 16
+        tr(X("PT", 0, 2 * m), X3("PD", 0, M, 0, 32))
+        cp(out, IN(X("PT", 0, 2 * m), X("WO", WSEG[M], WSEG[M] + M)))
+
+    def wrap(out, src, m, add=0.0):
+        ts(half(m), src, add, OP.add)
+        act(X3("PD", 0, m // 16, 16, 32), src, bias=add)
+        turn(out, m)
+
+    def fwd(o, a, b, f0, f1, m, extra=None):
+        scan(X(o, 0, m), a, b, 0.0, f0, f1)
+        c_ = carry("SHD", [X(o, m - 1, m)] + ([extra] if extra else []))
+        scan(X(o, 0, m), a, b, c_, f0, f1)
+
+    def bwd1(o, b, f1, m, fl):
+        scan(RV(o, 0, m), RV("NF", 1, m + 1), RV(b, 0, m), 0.0, OP.mult, f1)
+        return carry("SHUF" if fl else "SHU", [X(o, 0, 1)])
+
+    def bwd2(o, b, f1, m, c_):
+        scan(RV(o, 0, m), RV("NF", 1, m + 1), RV(b, 0, m), c_, OP.mult, f1)
+
+    dma(X("FV", 0, 768), HB(T.form[:, :]))
+    dma(X("RB", 0, 48), HB(T.runs[:, :]), "s")
+    dma(X("CB", 0, 240), HB(T.calls[:, :]), "s")
+    for x, j in enumerate((3, 4, 0, 1, 2)):
+        for h in range(2):
+            dma(X("J%d" % j, 768 * h, 768 * h + 768), HB(T.jump[:, 3840 * h + 768 * j:3840 * h + 768 * j + 768]), "y" if h == 0 or x > 1 else "s")
+    iota(X("PI", 0, 1), [[0, 1]], 0, 1, False)
+    iota(X("XR", 0, 144), [[1, 144]], 0, 0)
+    iota(X("E257", 0, 80), [[16, 80]], 0, 0)
+    iota(X("GM", 0, 128), [[16, 8], [0, 16]], 0, 0)
+    ms(X("G5", 0, 240), 0.0)
+    ms(X("K32", 0, 400), 32.0)
+    dma(X("E", 0, 3840, rows=0), X("G5", 0, 240))
+    ts(X("PI", 1, 2), X("PI", 0, 1), 15, OP.bitwise_and)
+    ts(X("PI", 2, 3), X("PI", 0, 1), 16, OP.bitwise_and)
+    ms(X("ZB", 0, 320), 0.0)
+    cp(X("COL", 0, 3), X("PI", 0, 3))
+    ts(col(4), col(1), 0.0, OP.is_equal, 768.0, OP.mult)
+    tt(col(5), col(0), col(1), OP.subtract)
+    ts(X("BODY", 0, 64), X("E257", 0, 64), col(1), OP.add, 0.25, OP.add)
+    ts(col(3), col(5), 15.0, OP.add)
+    ts(mat("BLKF"), mat("GM"), col(5), OP.is_equal)
+    ts(X("ZT", 0, 144), X("XR", 0, 144), col(3), OP.is_equal, col(4), OP.mult)
+    ts(mat("BLK"), mat("GM"), col(5), OP.is_equal)
+    ts(X("ZF", 0, 144), X("XR", 0, 144), col(3), OP.is_equal, col(4), OP.mult)
+    ts(mat("N16"), X("XR", 0, 128), col(0), OP.is_equal, -16.0, OP.mult)
+    ts(mat("IDN"), X("XR", 0, 128), col(0), OP.is_equal)
+    for M, o in WSEG.items():
+        iota(X("W1", 16 * o, 16 * (o + M)), [[1, 16], [32, M]], 0, 0)
+        if M == 20:
+            aff(mat("TRIF"), mat("BLKF"), [[1, 128]], OP.is_gt, 0, -1)
+    for lo, hi in ((15, 16), (39, 40), (45, 48)):
+        iota(X("W1", 16 * lo, 16 * hi), [[0, 16 * (hi - lo)]], 0, 0)
+    aff(mat("SHDF"), mat("BLKF"), [[1, 128]], OP.is_equal, -1, -1)
+    aff(mat("SHU"), mat("BLK"), [[1, 128]], OP.is_equal, 1, -1)
+    aff(mat("TRI"), mat("BLK"), [[1, 128]], OP.is_gt, 0, -1)
+    aff(mat("SHD"), mat("BLK"), [[1, 128]], OP.is_equal, -1, -1)
+    aff(mat("SHUF"), mat("BLKF"), [[1, 128]], OP.is_equal, 1, -1)
+    iota(X("CX", 0, 320), [[1, 320]], 0, 0)
+
+    def offsets_T(r, f240):
+        n = NP[r]
+        k = n // 16
+        ts(X("TI", 0, n), X("FV", 0, n), 14.5, OP.is_lt)
+        b = small()
+        for i in range(16):
+            mm(X(b, 0, k), X("ZT", 15 - i, 143 - i), X("TI", i, n, 16), i == 0, i == 15)
+        addc(f240, X("F240", 0, n), X("FV", 0, n), 240.0)
+        tt(X("S1", 0, k), X(b, 0, k), X("BODY", 0, k), OP.add)
+        cp(X("AO", 0, k), X("S1", 0, k))
+
+    def args_gather(r, j, q, b):
+        gat(q, X("AB%d" % b, 0, NP[r]), X("J%d" % j, 0, 1536), X("AO", 0, NP[r] // 16))
+        return "AB%d" % b
+
+    def args_min(r, j, ab):
+        n = NP[r]
+        h = n // 2
+        for c_ in range(2):
+            ps = X("P%d" % c_, 0, h)
+            mm(ps, mat("IDN"), X("F240", c_ * h, c_ * h + h), True, False)
+            mm(ps, mat("N16"), X(ab, c_ * h, c_ * h + h), False, True)
+            base = ("TS", (j - 3) * 1024) if j >= 3 else ("T%d" % r, j * n)
+            tt(X(base[0], base[1] + c_ * h, base[1] + c_ * h + h), X(ab, c_ * h, c_ * h + h), ps, OP.min)
+        if j >= 3:
+            k = 4 * r + j - 3
+            send(k, X("TS", (j - 3) * 1024, (j - 3) * 1024 + n), [(DIST[j], X("T%d" % r, j * n, (j + 1) * n), k)])
+
+    cp(X("S2", 0, 48), X("RB", 0, 48))
+    scan(X("S3", 0, 48), X("S2", 0, 48), X("ZB", 0, 48), 0.0, OP.add, OP.add)
+    c_ = carry("TRIF", [X("S3", 47, 48)])
+    tt(X("S2", 0, 48), X("S3", 0, 48), X("S2", 0, 48), OP.subtract)
+    ts(X("SO", 0, 48), X("S2", 0, 48), c_, OP.add)
+    for h in range(2):
+        act(IN(X("E", 0, 3840), X("SO", 24 * h, 24 * h + 24)), X("K32", 0, 384), fn=AF.Silu)
+    dma(X("G5", 0, 240), X("E", 0, 3840, rows=0))
+    ts(X3("LD", 0, 3, 0, 16), X("S2", 0, 48), c_, OP.add)
+    ts(X3("LD", 0, 3, 16, 32), X("S2", 0, 48), c_, OP.add)
+    for i in range(16):
+        mm(X("PX", 0, 48), X("ZF", 15 - i, 143 - i), X("W1", i, 768, 16), i == 0, i == 15)
+    cp(X("G1", 0, 240), X("CB", 0, 240))
+    cp(half(240), X("CB", 0, 240))
+    cp(X3("PD", 0, 15, 16, 32), X("CB", 0, 240))
+    cp(X("PK", 0, 240), X("CB", 0, 240))
+    tr(X("PT2", 0, 96), X3("LD", 0, 3, 0, 32))
+    ms(X("C85", 0, 320), -8.5 / 16)
+    ts(col(6), col(1), 240.0, OP.mult)
+    ts(col(15), col(1), 320.0, OP.mult)
+    ts(col(7), col(1), 1.0, OP.is_equal)
+    ts(col(8), col(1), 2.0, OP.is_equal)
+    ts(col(9), col(1), 3.0, OP.is_equal)
+    ts(mat("N8"), X("XR", 0, 128), col(0), OP.is_equal, 8.0, OP.mult)
+    tt(col(8), col(8), col(7), OP.add)
+    ts(X("ZC", 0, 144), X("XR", 0, 144), col(3), OP.is_equal, col(7), OP.mult)
+    ts(X("ZD", 0, 144), X("XR", 0, 144), col(3), OP.is_equal, col(8), OP.mult)
+    ts(X("E257", 0, 80), X("E257", 0, 80), col(1), OP.add, 257.0, OP.add)
+    ts(X("ZS", 0, 144), X("XR", 0, 144), col(3), OP.is_equal, 1.0 / 16, OP.mult)
+    ts(col(13), col(9), 3840.0, OP.mult, 32.0, OP.add)
+    ts(col(14), col(9), 5120.0, OP.mult, 32.0, OP.add)
+    offsets_T(0, "v")
+    a3 = args_gather(0, 3, "s", 0)
+    a4 = args_gather(0, 4, "s", 1)
+    a0 = args_gather(0, 0, "s", 2)
+    ts(X("S3", 0, 48), X("PX", 0, 48), 1.0 / 768, OP.mult, col(2), OP.add)
+    ts(X("WO", 0, 48), X("S3", 0, 48), 0.25, OP.add)
+    turn(X("UW", 0, 240), 240)
+    args_min(0, 3, a3)
+    ts(X("NF", 0, 240), X("G5", 0, 240), 1.0, OP.is_lt)
+    ts(X("H3", 0, 240), X("G5", 0, 240), 1.0, OP.is_gt)
+    args_min(0, 4, a4)
+    a1 = args_gather(0, 1, "s", 0)
+    a2 = args_gather(0, 2, "s", 1)
+    iota(X("R", 0, 5136), [[0, 5136]], 0, 0)
+
+    def list_static(r):
+        m = NL[r] // 16
+        tt(X("G4", 0, m), X("PK", 0, m), X("H3", 0, m), OP.mult)
+        c2 = carry("SHU", [X("NF", 0, 1)])
+        scan(X("G3", 0, m), X("NF", 0, m), X("G4", 0, m), 0.0, OP.mult, OP.add)
+        c1 = carry("SHDF", [X("G3", m - 1, m)])
+        cp(X("NF", m, m + 1), c2)
+        scan(X("PX", 0, m), X("NF", 0, m), X("G4", 0, m), c1, OP.mult, OP.add)
+        cp(half(m), X("PX", 0, m))
+        cp(X3("PD", 0, m // 16, 16, 32), X("PX", 0, m))
+        turn(X("LW", 0, m), m)
+
+    args_min(0, 0, a0)
+    list_static(0)
+    args_min(0, 1, a1)
+    args_min(0, 2, a2)
+    scan(X("H4", 0, 240), X("H3", 0, 240), X("ZB", 0, 240), 0.0, OP.add, OP.add)
+    cp(X("LP0", 0, 48), IN(X("PT2", 0, 96), X("WO", 36, 39)))
+    ts(col(12), carry("TRI", [X("H4", 239, 240)]), 32.0, OP.add)
+    iota(X("DIS", 0, 8), [[0, 8]], 0, 0)
+    iota(X("BC", 0, 2048), [[0, 2048]], 1, 0)
+    aff(X("BC", 0, 2048), X("BC", 0, 2048), [[-1, 16], [-16, 8], [0, 16]], OP.is_equal, 0, 1)
+    iota(X("KM", 0, 400), [[0, 400]], int(MAG), 0)
+    for nm, lo, v_ in (("A", 3840, 15), ("A", 5120, 15), ("E", 3840, 0), ("E", 5120, 0)):
+        iota(X(nm, lo, lo + 16), [[0, 16]], v_, 0)
+    iota(X("OM", 0, 8), [[0, 8]], 0, 0)
+
+    def first_fields():
+        z = [X2("Z", f, 4, 244) for f in range(4)]
+        u = X("G1", 0, 240)
+        act(X("CEF", 0, 240), X("H4", 0, 240), bias=col(12))
+        act(z[2], u, scale=1.0 / 768, bias=-383.5 / 768)
+        act(z[0], X("CEF", 0, 240), bias=-33.0)
+        act(z[2], z[2], bias=MAG)
+        dma(X("R", 0, 3840, rows=5), z[0])
+        act(z[1], u, bias=33.0)
+        act(z[2], z[2], bias=-MAG)
+        dma(X("R", 0, 3840, rows=0), z[1])
+        act(X("BS", 0, 240), z[2], scale=1024.0, bias=768.0)
+        act(z[3], z[2], scale=256.0, bias=33.0)
+
+    def first_fields2():
+        tt(X2("Z", 2, 4, 244), X2("Z", 3, 4, 244), X("CB", 0, 240), OP.add)
+        dma(X("R", 0, 3840, rows=4), X2("Z", 2, 4, 244))
+
+    def second_fields():
+        m = 320
+        fill("G4", 0, m)
+        ts(X("GI", 0, m), X("UB", 0, m), -33.0, OP.add)
+        act(X("G4", 0, m), X("G4", 0, m), bias=-MAG)
+        ts(X("GJ", 0, m), X("GI", 0, m), 1023, OP.bitwise_and)
+        dma(X("R", 0, 5120, rows=0), X("G4", 0, m))
+        b = small()
+        ts(X(b, 0, m), X("GJ", 0, m), 33.0, OP.add)
+        ts(X("VLD", 0, m), X("CEF", 0, m), 32.5, OP.is_ge)
+        tt(X("G6", 0, m), X(b, 0, m), X("UB", 0, m), OP.min)
+        dma(X("R", 0, 5120, rows=4), X("G6", 0, m))
+
+    def prefill(r):
+        n2 = NL[r + 1]
+        for f in (0, 4, 8, 12):
+            dma(X("W1", 0, n2, rows=f), X("K32", 0, n2 // 16))
+            if SHARE[r] < NL[r]:
+                dma(X("W2", 0, n2, rows=f), X("KM", 0, n2 // 16))
+
+    def dissent(r):
+        n, m = NL[r], NL[r] // 16
+        w = 2 * m
+        mm(X("PC", 0, m), mat("IDN"), X("C85", 0, m), True, False)
+        for c_ in range(8):
+            lo, hi = c_ * w, c_ * w + w
+            gat("s", X("A", lo, hi), X("T%d" % r, 0, n), X("UW", lo // 16, hi // 16))
+            tt(X("NQ", lo, hi), IN(X("T%d" % r, 0, n), X("LW", lo // 16, hi // 16)), X("A", lo, hi), OP.not_equal)
+            for i in (2 * c_, 2 * c_ + 1):
+                mm(X("PC", 0, m), X("ZS", 15 - i, 143 - i), X("NQ", i * m, i * m + m), False, i == 15)
+        act(X("P0", 0, m), X("CX", 0, m), bias=col(6 if r == 0 else 15))
+        act(X("SW", 0, 264), X("ZB", 0, 264), bias=col(13 + r))
+
+    def splits(r):
+        n, m, np_ = NL[r], NL[r] // 16, NP[r]
+        pc, mvp = X("PC", 0, m), X("PM", 0, m)
+        lp, cl = "LP%d" % r, "CL%d" % r
+        ts(X("DIS", 1, m + 1), pc, 0.0, OP.is_gt)
+        fwd("H1", X("DIS", 0, m), X("NF", 0, m), OP.max, OP.mult, m, extra=X("DIS", m, m + 1))
+        tt(X("FDB", 0, m), pc, X("H1", 0, m), OP.is_gt)
+        scan(X("H2", 0, m), X("FDB", 0, m), X("ZB", 0, m), 0.0, OP.add, OP.add)
+        c1 = carry("TRI", [X("H2", m - 1, m)])
+        tt(X("D0", 0, m), pc, X("H1", 0, m), OP.is_le)
+        ts(X("H3", 0, m), X("H2", 0, m), c1, OP.add, 256.5, OP.is_gt)
+        ts(X("G2", 0, m), X("H2", 0, m), c1, OP.add)
+        tt(mvp, pc, X("H3", 0, m), OP.is_gt)
+        tt(X("H4", 0, m), mvp, X("G2", 0, m), OP.mult)
+        c2 = bwd1("H1", "H4", OP.max, m, False)
+        tt(X("MV", 0, m), pc, X("H3", 0, m), OP.is_gt)
+        bwd2("G4", "H4", OP.max, m, c2)
+        dma(X("R", 0, n, rows=1), X("G4", 0, m))
+        if r == 1:
+            ts(X("G5", 0, m), X("G4", 0, m), 0.5, OP.is_gt, col(10), OP.mult)
+            dma(X("R", 0, n, rows=2), X("G5", 0, m), "s")
+        act(X("P1", 0, m), X("MV", 0, m), scale=-127.0 / 128)
+        tt(X("G6", 0, m), X("PK", 0, m), X("FDB", 0, m), OP.mult)
+        tt(X("G1", 0, m), X("P0", 0, m), X("FDB", 0, m), OP.mult)
+        act(X("PK", 0, m), X("MV", 0, m), scale=127.0, bias=1.0)
+        gat("s", X(cl, 0, np_), X("R", 0, n + 16), X(lp, 0, np_ // 16))
+        send(4 * r + 2, X(cl, 0, np_), [(1, X(cl, 3 * np_, 4 * np_), 4 * r + 2), (3, X(cl, 4 * np_, 5 * np_), 4 * r + 3)])
+        scan(X("G3", 0, m), X("D0", 0, m), X("G6", 0, m), 0.0, OP.mult, OP.add)
+        c3 = carry("SHDF", [X("G3", m - 1, m)])
+        c4 = bwd1("PT", "G1", OP.max, m, True)
+        scan(X("G3", 0, m), X("D0", 0, m), X("G6", 0, m), c3, OP.mult, OP.add)
+        bwd2("G6", "G1", OP.max, m, c4)
+        dma(X("R", 0, n, rows=3), X("G6", 0, m))
+        dma(X(cl, np_, 2 * np_), X(cl, 0, np_))
+        dma(X(cl, 2 * np_, 3 * np_), X(cl, 0, np_))
+        tt(X("G3", 0, m), X("G3", 0, m), X("PX", 0, m), OP.subtract)
+        tt(X("BE", 0, m), X("P1", 0, m), X("NF", 0, m), OP.add)
+        tt(X("G3", 0, m), mvp, X("G3", 0, m), OP.mult)
+        c6 = carry("SHU", [X("BE", 0, 1)])
+        tt(half(m), X("PX", 0, m), X("G3", 0, m), OP.add)
+        tt(X3("PD", 0, m // 16, 16, 32), X("PX", 0, m), X("G3", 0, m), OP.add)
+        cp(X("BE", m, m + 1), c6)
+        turn(X("NW", 0, m), m)
+        tt(X("D0", 0, m), X("PK", 0, m), X("BE", 1, m + 1), OP.mult)
+        if r == 0:
+            c5 = carry("BLK", [X("H2", m - 1, m)])
+            ts(col(10), c5, 256.0, OP.min)
+            ts(col(11), c5, 256.0, OP.min, 800.0, OP.add)
+
+    def clone_list(r):
+        n, m, np_ = NL[r], NL[r] // 16, NP[r]
+        k = np_ // 16
+        b = small()
+        for i in range(16):
+            mm(X(b, 0, k), X("ZC", 15 - i, 143 - i), X("CL%d" % r, i, np_, 16), i == 0, i == 15)
+        act(X("PF", 0, np_), IN(X("R", 0, n + 16), X("LP%d" % r, 0, k)), bias=32.0)
+        ts(X("S1", 0, k), X(b, 0, k), 0.5, OP.is_lt)
+        tt(X("S1", 0, k), X("S1", 0, k), X("E257", 0, k), OP.mult)
+        tt(X("S1", 0, k), X("S1", 0, k), X(b, 0, k), OP.add)
+        cp(X("SO", 0, k), X("S1", 0, k))
+        act(IN(X("SW", 0, 1288), X("SO", 0, k)), X("PF", 0, np_), fn=AF.Silu)
+        for u in range(2):
+            dma(X2("FD", 0, 16 * u, 16 * u + 16), X("SW", 1, 257, rows=3))
+            if r == 0:
+                dma(X2("FD", 1, 16 * u, 16 * u + 16), X("SW", 1, 257, rows=5))
+        act(X("PX", 0, m), X("MV", 0, m), scale=1024.0, bias=-512.0)
+
+    def clone_list2(r):
+        k = NP[r] // 16
+        nf_ = 2 - r
+        tr(X("PT2", 0, 32 * nf_), X3("FD", 0, nf_, 0, 32))
+        ts(X("LP%d" % r, k, k + 16), IN(X("PT2", 0, 32), X("WO", 44, 45)), -31.75, OP.add)
+        if r == 0:
+            ts(X("BODY", 48, 64), IN(X("PT2", 32, 64), X("WO", 44, 45)), -31.75, OP.add)
+
+    def callee(r):
+        n, m = NL[r], NL[r] // 16
+        ts(X("G2", 0, m), X("G2", 0, m), 800.0 if r == 0 else col(11), OP.add)
+        tt(X("PK", 0, m), X("PM", 0, m), X("G2", 0, m), OP.mult)
+        tt(X("G2", 0, m), X("PK", 0, m), X("CEF", 0, m), OP.max)
+        dma(X("R", 0, n, rows=8), X("G2", 0, m))
+        act(X("PK", 0, m), X("MV", 0, m), scale=-1.0, bias=1.0)
+
+    def differ(r, c_, parts):
+        w = NL[r] // parts
+        lo, hi = c_ * w, c_ * w + w
+        tt(X("NQ", lo, hi), IN(X("T%d" % r, 0, NL[r]), X("NW", lo // 16, hi // 16)), X("A", lo, hi), OP.not_equal)
+
+    def tally(r, t):
+        n, m = NL[r], NL[r] // 16
+        hi = n - 512 * t
+        lo = max(0, hi - 512)
+        pb = "P%d" % (t % 2)
+        x = lo
+        while x < hi:
+            y = min(hi, (x // m + 1) * m)
+            i = x // m
+            mm(X(pb, x - lo, y - lo), X("BC", 128 * i, 128 * i + 128), X("D0", x - i * m, y - i * m))
+            x = y
+        scan(RV("E", lo, hi), RV(pb, 0, hi - lo), RV("NQ", lo, hi), 0.0 if hi == n else X("E", hi, hi + 1), OP.mult, OP.add)
+
+    def lead_values(r):
+        gat("s", X("VAL", 0, NP[r] + 256), X("A", 0, NL[r] + 16), X("LP%d" % r, 0, NP[r] // 16 + 16))
+
+    def formals_gather(r, q):
+        act(X("T15", 0, NP[r]), IN(X("E", 0, NL[r] + 16), X("LP%d" % r, 0, NP[r] // 16)), bias=-0.88, fn=AF.Sign)
+
+    def formals(r, q):
+        n, np_ = NL[r], NP[r]
+        k = np_ // 16
+        lp = "LP%d" % r
+        if q == "v":
+            ts(X("T15", 0, np_), IN(X("E", 0, n + 16), X(lp, 0, k)), 1.0, OP.is_ge, 2.0, OP.mult)
+        cp(X("ZI", 0, 256), IN(X("E", 0, n + 16), X(lp, k, k + 16)))
+        ts(X("ZJ", 0, 256), X("ZI", 0, 256), 127, OP.bitwise_and)
+        ts(X("T15", np_, np_ + 256), X("ZJ", 0, 256), 0.5, OP.is_gt, 2.0, OP.mult)
+        for t, (lo, hi) in enumerate(((0, np_ // 2), (np_ // 2, np_), (np_, np_ + 256))):
+            ps = X("P%d" % (t % 2), 0, hi - lo)
+            mm(ps, mat("IDN"), X("VAL", lo, hi), True, False)
+            mm(ps, mat("N8"), X("T15", lo, hi), False, True)
+            ts(X("FV", lo, hi), ps, 8.0 if q == "s" and t < 2 else 0.0, OP.add, 15.0, OP.min)
+
+    def copies(r, qs):
+        n, m = NL[r], NL[r] // 16
+        w = 4 * m
+        for c_ in range(4):
+            lo, hi = c_ * w, c_ * w + w
+            gat(qs[c_], found(r, lo, hi), X("CL%d" % r, 0, n), X("UW", lo // 16, hi // 16))
+
+    def found(r, lo, hi):
+        if r == 1:
+            return X("J", lo, hi)
+        return X("T1", lo, hi) if hi <= 2880 else X("CL1", lo - 2880, hi - 2880)
+
+    def copies2(r, c_):
+        m = NL[r] // 16
+        for i in range(4 * c_, 4 * c_ + 4):
+            mm(X("PC", 0, m), X("ZD", 15 - i, 143 - i), found(r, i * m, i * m + m), i == 0, i == 15)
+
+    def places(r):
+        n, m = NL[r], NL[r] // 16
+        om = X("OM", 1, m + 1)
+        if r == 0:
+            ts(om, X("PC", 0, m), 0.5, OP.is_gt, 1.0, OP.add)
+            ts(X("G5", 0, m), X("PC", 0, m), 32.0, OP.add)
+        else:
+            tt(X("G5", 0, m), X("PC", 0, m), X("VLD", 0, m), OP.mult)
+            ts(om, X("G5", 0, m), 0.5, OP.is_gt, 1.0, OP.add)
+        act(X("H2", 0, m), om, acc=col(12))
+        if r == 0:
+            act(X("P0", 0, m), om, bias=-1.0)
+        else:
+            act(X("P0", 0, m), om, scale=768.0, bias=32.0 - 768.0)
+        tt(X("H1", 0, m), X("PM", 0, m), om, OP.mult)
+        tt(X("H4", 0, m), X("PK", 0, m), om, OP.mult)
+        c1 = carry("TRIF", [col(12)])
+        scan(X("H3", 0, m), X("NF", 0, m), X("H1", 0, m), 0.0, OP.mult, OP.subtract)
+        scan(X("G3", 0, m), X("OM", 0, m), X("ZB", 0, m), c1, OP.add, OP.add)
+        c2 = carry("SHD", [X("H3", m - 1, m)])
+        c3 = bwd1("H2", "H4", OP.add, m, False)
+        if r == 0:
+            tt(X("P1", 0, m), X("P0", 0, m), X("BS", 0, m), OP.mult)
+        tt(X("G1", 0, m), X("P%d" % (1 - r), 0, m), X("G5", 0, m), OP.add)
+        dma(X("R", 0, n, rows=12), X("G1", 0, m))
+        scan(X("PC", 0, m), X("NF", 0, m), X("H1", 0, m), c2, OP.mult, OP.subtract)
+        bwd2("H2", "H4", OP.add, m, c3)
+        tt(X("H2", 0, m), X("PX", 0, m), X("H2", 0, m), OP.min)
+        tt(X("PM", 0, m), X("PC", 0, m), X("H2", 0, m), OP.max)
+        tt(half(m), X("PM", 0, m), X("G3", 0, m), OP.add)
+        tt(X3("PD", 0, m // 16, 16, 32), X("PM", 0, m), X("G3", 0, m), OP.add)
+        turn(X("PW", 0, m), m)
+        if r == 0:
+            tt(X("G6", 0, m), X("PM", 0, m), X("G3", 0, m), OP.add)
+
+    def scatter_s(r):
+        n2, h = NL[r + 1], SHARE[r]
+        act(IN(X("W1", 0, n2), X("PW", 0, h // 16)), X("R", 0, h), fn=AF.Silu)
+
+    def scatter_v(r):
+        n, n2, h = NL[r], NL[r + 1], SHARE[r]
+        if h < n:
+            ts(IN(X("W2", 0, n2), X("PW", h // 16, n // 16)), X("R", h, n), 1.0, OP.mult, MAG - 32.0, OP.add)
+
+    def z2(r, f):
+        m = NL[r + 1] // 16
+        o = 1024 if r == 0 else 0
+        return X("PS", o + f * m, o + f * m + m)
+
+    def fetch(r, w):
+        n2 = NL[r + 1]
+        if w == 2 and SHARE[r] == NL[r]:
+            return
+        for x, f in enumerate((3, 1, 2, 0)):
+            dma(X2("Z", f, 4, 4 + n2 // 16) if w == 1 else z2(r, f), X("W%d" % w, 0, n2, rows=4 * f), "y" if x % 2 == 0 or w == 2 else "s")
+
+    def merge(r):
+        m = NL[r + 1] // 16
+        both = SHARE[r] < NL[r]
+        last = X3("Z", 0, 4, m + 3, m + 4)
+        if both:
+            o = 1024 if r == 0 else 0
+            tt(X("TMP", 4, 8), last, X("PS", o + m - 1, o + 4 * m, m), OP.add)
+        else:
+            ts(X("TMP", 4, 8), last, MAG, OP.add)
+        ts(X("TMP", 0, 4), X("TMP", 4, 8), -MAG, OP.add)
+        b = small()
+        mm(X(b, 0, 4), mat("SHDF"), X("TMP", 0, 4))
+        for f in (3, 1, 2, 0):
+            if both:
+                tt(X2("Z", f, 4, m + 4), X2("Z", f, 4, m + 4), z2(r, f), OP.add)
+            else:
+                addc("v" if f % 2 else "s", X2("Z", f, 4, m + 4), X2("Z", f, 4, m + 4), MAG)
+            if f == 3:
+                ts(X3("Z", 0, 4, 3, 4), X(b, 0, 4), MAG, OP.add)
+        tt(X("G1", 0, m), X2("Z", 1, 4, m + 4), X2("Z", 3, 3, m + 3), OP.max)
+        ts(X("KP", 0, m), X2("Z", 3, 3, m + 3), MAG + 33.0, OP.is_ge)
+
+    def fill(o, f, m):
+        scan(X(o, 0, m), X("KP", 0, m), X2("Z", f, 4, m + 4), X2("Z", f, 3, 4), OP.mult, OP.max)
+
+    dissent(0)
+    first_fields()
+    prefill(0)
+    splits(0)
+    differ(0, 3, 4)
+    clone_list(0)
+    differ(0, 2, 4)
+    for t in range(3):
+        tally(0, t)
+    differ(0, 1, 4)
+    clone_list2(0)
+    lead_values(0)
+    copies(0, "ssss")
+    callee(0)
+    differ(0, 0, 4)
+    first_fields2()
+    for t in range(3, 8):
+        tally(0, t)
+        if t in (5, 6, 7):
+            copies2(0, t - 5)
+    copies2(0, 3)
+    formals_gather(0, "s")
+    places(0)
+    scatter_s(0)
+    scatter_v(0)
+    fetch(0, 2)
+    formals(0, "s")
+    offsets_T(1, "v")
+    ms(X("E", 3840, 3848), 5120.0)
+    dma(X("E", 0, 3840, rows=0), X("G6", 0, 240))
+    a3 = args_gather(1, 3, "v", 0)
+    a4 = args_gather(1, 4, "v", 1)
+    args_min(1, 3, a3)
+    a0 = args_gather(1, 0, "v", 2)
+    args_min(1, 4, a4)
+    a1 = args_gather(1, 1, "v", 0)
+    fetch(0, 1)
+    a2 = args_gather(1, 2, "s", 1)
+    args_min(1, 0, a0)
+    args_min(1, 1, a1)
+    args_min(1, 2, a2)
+    merge(0)
+    m = 320
+    fill("G3", 2, m)
+    ts(half(m), X("G1", 0, m), -(MAG + 33.0), OP.add)
+    act(X3("PD", 0, 20, 16, 32), X("G1", 0, m), bias=-(MAG + 33.0))
+    act(X("CEF", 0, m), X("G3", 0, m), bias=-MAG)
+    act(X("G5", 1, m + 1), X("CEF", 0, m), bias=-32.5, fn=AF.Abs)
+    act(X("PM", 0, m), X("CEF", 0, m), bias=-32.5)
+    act(X("PK", 0, m), X("G1", 0, m), bias=-(MAG + 33.0))
+    turn(X("UW", 0, m), m)
+    cp(X("G5", 0, 1), carry("SHDF", [X("G5", m, m + 1)]))
+    tt(X("H3", 0, m), X("PM", 0, m), X("G5", 0, m), OP.not_equal)
+    tt(X("NF", 0, m), X("PM", 0, m), X("G5", 0, m), OP.is_equal)
+    act(X("UB", 0, m), X("G1", 0, m), bias=-MAG)
+    list_static(1)
+    prefill(1)
+    gat("s", X("PF", 0, 1024), X("E", 0, 3856), X("LP0", 0, 64))
+    for u in range(2):
+        dma(X3("LD", 0, 4, 16 * u, 16 * u + 16), X("PF", 0, 1024, rows=0))
+    dissent(1)
+    tr(X("PT2", 0, 128), X3("LD", 0, 4, 0, 32))
+    cp(X("LP1", 0, 64), IN(X("PT2", 0, 128), X("WO", 40, 44)))
+    splits(1)
+    differ(1, 3, 4)
+    clone_list(1)
+    differ(1, 2, 4)
+    for t in range(5):
+        tally(1, t)
+    differ(1, 1, 4)
+    copies(1, "ssss")
+    clone_list2(1)
+    callee(1)
+    differ(1, 0, 4)
+    second_fields()
+    for t in range(5, 10):
+        tally(1, t)
+        if t > 5:
+            copies2(1, t - 6)
+    lead_values(1)
+    ts(col(13), col(10), -1.0, OP.mult, 256.0, OP.add)
+    ts(col(14), col(10), 1024.5, OP.add)
+    ts(X("S2", 0, 80), X("E257", 0, 80), col(14), OP.is_ge, col(13), OP.mult)
+    ms(X("FV", 1280, 1296), 15.0)
+    tt(X("S2", 0, 80), X("S2", 0, 80), X("E257", 0, 80), OP.add)
+    ts(X("YO", 0, 80), X("S2", 0, 80), -257.0, OP.add, 1280.0, OP.min)
+    formals_gather(1, "s")
+    places(1)
+    scatter_s(1)
+    scatter_v(1)
+    fetch(1, 2)
+    fetch(1, 1)
+    formals(1, "s")
+    gat("s", X("T15", 0, 1280), X("FV", 0, 1296), X("YO", 0, 80))
+    dma(HB(T.yform[:, :]), X("T15", 0, 1280))
+    m = 400
+    merge(1)
+    act(X("G1", 0, m), X("G1", 0, m), bias=-(MAG + 33.0))
+    dma(HB(T.ycaller[:, :]), X("G1", 0, m))
+    fill("G3", 2, m)
+    act(X("G3", 0, m), X("G3", 0, m), bias=-(MAG + 33.0))
+    dma(HB(T.ycallee[:, :]), X("G3", 0, m))
+    fill("G4", 0, m)
+    ts(X("G4", 0, m), X("G4", 0, m), -(MAG + 33.0), OP.add)
+    dma(HB(T.ysite[:, :]), X("G4", 0, m), "s")
+    for s_, v_ in final.items():
+        if all(waited[q].get(s_, 0) < v_ for q in Q):
+            g.sync.wait_ge(T.sem[s_], v_)

@@ -18,16 +18,16 @@ def _p(cols):
 
 
 SCRATCH = {
-    "J": _s(7680, B16), "T0": _s(3840, B16), "T1": _s(5120, B16),
+    "J": _s(7680, B16), "T0": _s(5136, B16), "T1": _s(5136, B16),
     "A": _s(5136, B16), "NQ": _s(5120, B16), "E": _s(5136, F32), "R": _s(5136, F32),
-    "CL0": _s(3840, B16), "CL1": _s(5120, B16), "W1": _s(6400, F32), "W2": _s(6400, F32),
+    "CL0": _s(5136, B16), "CL1": _s(5136, B16), "W1": _s(6400, F32), "W2": _s(6400, F32),
     "K32": _s(400, F32), "KM": _s(400, F32),
     "FV": _s(1296, B16), "VAL": _s(1280, B16), "T15": _s(1280, B16), "PS": _s(2312, F32),
-    "BC": _s(2048, B16), "ZS": _s(144, B16), "ZT": _s(144, B16), "ZC": _s(144, B16), "ZD": _s(144, B16), "ZF": _s(144, F32),
-    "XR": _s(144, F32), "GM": _s(128, B16), "BLK": _s(128, B16), "BLKF": _s(128, F32), "IDN": _s(128, B16), "N16": _s(128, B16),
+    "BC": _s(2048, B16), "ZS": _s(144, B16), "ZT": _s(144, B16), "ZC": _s(144, B16), "ZD": _s(144, B16),
+    "IDF": _s(128, F32), "NKF": _s(128, F32), "GM": _s(128, B16), "BLK": _s(128, B16), "BLKF": _s(128, F32), "IDN": _s(128, B16), "N16": _s(128, B16),
     "N8": _s(128, B16), "C85": _s(320, B16),
     "TRI": _s(128, B16), "TRIF": _s(128, F32), "SHD": _s(128, B16), "SHDF": _s(128, F32), "SHU": _s(128, B16), "SHUF": _s(128, F32),
-    "COL": _s(16, F32), "PI": _s(4, I32), "TMP": _s(8, F32), "CX": _s(320, F32),
+    "COL": _s(16, F32), "PI": _s(4, I32), "TMP": _s(16, F32), "CX": _s(320, F32),
     "ZB": _s(320, B16), "WO": _s(48, U16),
     "CB": _s(240, I32), "RB": _s(48, I32),
     "PD": _s([20, 32], F32), "PT": _s(640, F32), "FD": _s([2, 32], F32), "LD": _s([4, 32], F32), "PT2": _s(128, F32),
@@ -35,14 +35,15 @@ SCRATCH = {
     "LP0": _s(64, U16), "LP1": _s(80, U16), "YO": _s(80, U16), "BODY": _s(64, F32), "E257": _s(80, F32),
     "S1": _s(80, F32), "S2": _s(80, F32), "S3": _s(80, F32),
     "NF": _s(328, B16), "DIS": _s(328, B16), "OM": _s(328, B16), "BE": _s(328, B16), "MV": _s(320, B16), "FDB": _s(320, B16),
-    "H1": _s(320, B16), "H2": _s(320, B16), "H3": _s(320, B16), "H4": _s(320, B16), "VLD": _s(320, B16), "D0": _s(320, B16),
+    "H1": _s(320, B16), "H2": _s(320, B16), "H3": _s(320, B16), "H4": _s(320, B16), "D0": _s(320, B16),
     "G1": _s(400, F32), "G2": _s(400, F32), "G3": _s(400, F32), "G4": _s(400, F32), "G5": _s(404, F32), "G6": _s(320, F32),
-    "GI": _s(320, I32), "GJ": _s(320, I32), "CEF": _s(320, F32), "BS": _s(240, F32), "UB": _s(320, F32), "KP": _s(400, B16),
-    "Z": _s([4, 404], F32),
+    "GI": _s(256, I32), "GJ": _s(256, I32), "CEF": _s(320, F32), "UB": _s(320, F32), "KP": _s(400, B16),
+    "Z": _s([5, 404], F32),
     "PA": _p(1024), "PC": _p(512), "PE1": _p(512), "PE2": _p(512), "PM": _p(512), "PK": _p(512), "PX": _p(512),
 }
 ALIAS = {"AB0": ("NQ", 0), "AB1": ("NQ", 1024), "TS": ("NQ", 2048), "F240": ("NQ", 4096), "TI": ("T15", 0),
          "AB2": ("A", 0), "J0": ("J", 0), "J1": ("J", 1536), "J2": ("J", 3072), "J3": ("J", 4608), "J4": ("J", 6144),
+         "BS": ("W2", 0), "ZF": ("W2", 256), "XR": ("W2", 400),
          "PF": ("PS", 0), "SW": ("PS", 1024), "ZI": ("GI", 0), "ZJ": ("GJ", 0), "P0": ("PA", 0), "P1": ("PA", 512)}
 SEMAPHORES = ["qv", "qs", "qp", "qg"] + ["d%d" % i for i in range(100)] + ["r%d" % i for i in range(8)] + ["l%d" % i for i in range(8)]
 
@@ -200,14 +201,18 @@ def rank_program(g, core, T, topo):
                                                   src=src[0], dst=reg[0]) for rid, pid, mk, reg, rs in trs], local_sem=T.sem["l%d" % k])
         note(("l%d" % k, per * len(dsts)), "dma", src[1], [])
 
+    def sec(name, r, j, lo=0, hi=None):
+        return X(name + str(r), 16 + 1024 * j + lo, 16 + 1024 * j + (NP[r] if hi is None else hi))
+
     DIST = {3: 1, 4: 3}
+    ROWS = (0, 4, 8, 12, 6)
     for r in range(2):
         for j in (3, 4):
             sr = (rank - DIST[j]) % NR
             n1 = len(common(T.cores[sr], [core]))
-            note(("r%d" % (4 * r + j - 3), n1), "dma", [], X("T%d" % r, j * NP[r], (j + 1) * NP[r])[1])
+            note(("r%d" % (4 * r + j - 3), n1), "dma", [], sec("T", r, j)[1])
             n2 = len(common(T.cores[sr], [peer(sr, 1), peer(sr, 3)])) // 2
-            note(("r%d" % (4 * r + j - 1), n2), "dma", [], X("CL%d" % r, j * NP[r], (j + 1) * NP[r])[1])
+            note(("r%d" % (4 * r + j - 1), n2), "dma", [], sec("CL", r, j)[1])
 
     def col(k): return X("COL", k, k + 1)
     def mat(name): return X(name, 0, 128)
@@ -298,6 +303,10 @@ def rank_program(g, core, T, topo):
         for i in range(16):
             mm(X(b, 0, k), X("ZT", 15 - i, 143 - i), X("TI", i, n, 16), i == 0, i == 15)
         addc(f240, X("F240", 0, n), X("FV", 0, n), 240.0)
+        return b
+
+    def offsets_T2(r, b):
+        k = NP[r] // 16
         tt(X("S1", 0, k), X(b, 0, k), X("BODY", 0, k), OP.add)
         cp(X("AO", 0, k), X("S1", 0, k))
 
@@ -312,11 +321,11 @@ def rank_program(g, core, T, topo):
             ps = X("P%d" % c_, 0, h)
             mm(ps, mat("IDN"), X("F240", c_ * h, c_ * h + h), True, False)
             mm(ps, mat("N16"), X(ab, c_ * h, c_ * h + h), False, True)
-            base = ("TS", (j - 3) * 1024) if j >= 3 else ("T%d" % r, j * n)
+            base = ("TS", (j - 3) * 1024) if j >= 3 else ("T%d" % r, 16 + j * 1024)
             tt(X(base[0], base[1] + c_ * h, base[1] + c_ * h + h), X(ab, c_ * h, c_ * h + h), ps, OP.min)
         if j >= 3:
             k = 4 * r + j - 3
-            send(k, X("TS", (j - 3) * 1024, (j - 3) * 1024 + n), [(DIST[j], X("T%d" % r, j * n, (j + 1) * n), k)])
+            send(k, X("TS", (j - 3) * 1024, (j - 3) * 1024 + n), [(DIST[j], sec("T", r, j), k)])
 
     cp(X("S2", 0, 48), X("RB", 0, 48))
     scan(X("S3", 0, 48), X("S2", 0, 48), X("ZB", 0, 48), 0.0, OP.add, OP.add)
@@ -330,10 +339,20 @@ def rank_program(g, core, T, topo):
     ts(X3("LD", 0, 3, 16, 32), X("S2", 0, 48), c_, OP.add)
     for i in range(16):
         mm(X("PX", 0, 48), X("ZF", 15 - i, 143 - i), X("W1", i, 768, 16), i == 0, i == 15)
+    for nm in ("T0", "CL0"):
+        dma(X(nm, 0, 16), X("ZB", 0, 16))
+        for j in range(5):
+            dma(sec(nm[:-1], 0, j, 768, 1024), X("ZB", 0, 256))
+    dma(X("CL1", 0, 16), X("ZB", 0, 16))
+    ts(X("GI", 0, 240), X("CB", 0, 240), -383.5, OP.add, 1.0 / 768, OP.mult)
     cp(X("G1", 0, 240), X("CB", 0, 240))
-    cp(half(240), X("CB", 0, 240))
-    cp(X3("PD", 0, 15, 16, 32), X("CB", 0, 240))
-    cp(X("PK", 0, 240), X("CB", 0, 240))
+    ts(X("PM", 0, 240), X("GI", 0, 240), 256.0, OP.mult, 16.0, OP.add)
+    ts(X("BS", 0, 240), X("GI", 0, 240), 1024.0, OP.mult, 768.0, OP.add)
+    b0 = offsets_T(0, "v")
+    tt(X("G2", 0, 240), X("PM", 0, 240), X("G1", 0, 240), OP.add)
+    tt(half(240), X("PM", 0, 240), X("G1", 0, 240), OP.add)
+    tt(X3("PD", 0, 15, 16, 32), X("PM", 0, 240), X("G1", 0, 240), OP.add)
+    tt(X("PK", 0, 240), X("PM", 0, 240), X("G1", 0, 240), OP.add)
     tr(X("PT2", 0, 96), X3("LD", 0, 3, 0, 32))
     ms(X("C85", 0, 320), -8.5 / 16)
     ts(col(6), col(1), 240.0, OP.mult)
@@ -349,7 +368,7 @@ def rank_program(g, core, T, topo):
     ts(X("ZS", 0, 144), X("XR", 0, 144), col(3), OP.is_equal, 1.0 / 16, OP.mult)
     ts(col(13), col(9), 3840.0, OP.mult, 32.0, OP.add)
     ts(col(14), col(9), 5120.0, OP.mult, 32.0, OP.add)
-    offsets_T(0, "v")
+    offsets_T2(0, b0)
     a3 = args_gather(0, 3, "s", 0)
     a4 = args_gather(0, 4, "s", 1)
     a0 = args_gather(0, 0, "s", 2)
@@ -387,6 +406,9 @@ def rank_program(g, core, T, topo):
     iota(X("BC", 0, 2048), [[0, 2048]], 1, 0)
     aff(X("BC", 0, 2048), X("BC", 0, 2048), [[-1, 16], [-16, 8], [0, 16]], OP.is_equal, 0, 1)
     iota(X("KM", 0, 400), [[0, 400]], int(MAG), 0)
+    aff(mat("IDF"), mat("BLKF"), [[1, 128]], OP.is_equal, 0, -1)
+    iota(mat("NKF"), [[0, 128]], -1024, 0)
+    aff(mat("NKF"), mat("NKF"), [[1, 128]], OP.is_equal, 0, -1)
     for nm, lo, v_ in (("A", 3840, 15), ("A", 5120, 15), ("E", 3840, 0), ("E", 5120, 0)):
         iota(X(nm, lo, lo + 16), [[0, 16]], v_, 0)
     iota(X("OM", 0, 8), [[0, 8]], 0, 0)
@@ -395,48 +417,48 @@ def rank_program(g, core, T, topo):
         z = [X2("Z", f, 4, 244) for f in range(4)]
         u = X("G1", 0, 240)
         act(X("CEF", 0, 240), X("H4", 0, 240), bias=col(12))
-        act(z[2], u, scale=1.0 / 768, bias=-383.5 / 768)
-        act(z[0], X("CEF", 0, 240), bias=-33.0)
-        act(z[2], z[2], bias=MAG)
-        dma(X("R", 0, 3840, rows=5), z[0])
         act(z[1], u, bias=33.0)
-        act(z[2], z[2], bias=-MAG)
+        act(z[2], X("G2", 0, 240), bias=17.0)
+        act(z[0], X("CEF", 0, 240), bias=-33.0)
         dma(X("R", 0, 3840, rows=0), z[1])
-        act(X("BS", 0, 240), z[2], scale=1024.0, bias=768.0)
-        act(z[3], z[2], scale=256.0, bias=33.0)
-
-    def first_fields2():
-        tt(X2("Z", 2, 4, 244), X2("Z", 3, 4, 244), X("CB", 0, 240), OP.add)
-        dma(X("R", 0, 3840, rows=4), X2("Z", 2, 4, 244))
+        dma(X("R", 0, 3840, rows=4), z[2])
+        dma(X("R", 0, 3840, rows=5), z[0])
 
     def second_fields():
         m = 320
-        fill("G4", 0, m)
-        ts(X("GI", 0, m), X("UB", 0, m), -33.0, OP.add)
-        act(X("G4", 0, m), X("G4", 0, m), bias=-MAG)
-        ts(X("GJ", 0, m), X("GI", 0, m), 1023, OP.bitwise_and)
-        dma(X("R", 0, 5120, rows=0), X("G4", 0, m))
-        b = small()
-        ts(X(b, 0, m), X("GJ", 0, m), 33.0, OP.add)
-        ts(X("VLD", 0, m), X("CEF", 0, m), 32.5, OP.is_ge)
-        tt(X("G6", 0, m), X(b, 0, m), X("UB", 0, m), OP.min)
-        dma(X("R", 0, 5120, rows=4), X("G6", 0, m))
+        z0, z1 = X2("Z", 0, 4, m + 4), X2("Z", 1, 4, m + 4)
+        act(z1, X("UB", 0, m), scale=1.0 / 1024, bias=-33.0 / 1024 - 0.4995)
+        act(z0, X2("Z", 4, 4, m + 4), bias=-MAG)
+        act(z1, z1, bias=MAG)
+        act(z1, z1, bias=-MAG, fn=AF.Relu)
+        dma(X("R", 0, 5120, rows=0), z0)
+
+    def second_fields2(step):
+        m = 320
+        if step == 0:
+            mm(X("PC", 0, m), mat("IDF"), X("UB", 0, m), True, False)
+            mm(X("PC", 0, m), mat("NKF"), X2("Z", 1, 4, m + 4), False, True)
+        else:
+            act(X2("Z", 2, 4, m + 4), X("PC", 0, m))
+            dma(X("R", 0, 5120, rows=4), X2("Z", 2, 4, m + 4))
 
     def prefill(r):
         n2 = NL[r + 1]
-        for f in (0, 4, 8, 12):
+        for f in ROWS[:5 - r]:
             dma(X("W1", 0, n2, rows=f), X("K32", 0, n2 // 16))
             if SHARE[r] < NL[r]:
                 dma(X("W2", 0, n2, rows=f), X("KM", 0, n2 // 16))
 
-    def dissent(r):
+    def dissent(r, hooks):
         n, m = NL[r], NL[r] // 16
         w = 2 * m
         mm(X("PC", 0, m), mat("IDN"), X("C85", 0, m), True, False)
         for c_ in range(8):
             lo, hi = c_ * w, c_ * w + w
-            gat("s", X("A", lo, hi), X("T%d" % r, 0, n), X("UW", lo // 16, hi // 16))
-            tt(X("NQ", lo, hi), IN(X("T%d" % r, 0, n), X("LW", lo // 16, hi // 16)), X("A", lo, hi), OP.not_equal)
+            gat("s", X("A", lo, hi), X("T%d" % r, 0, 5136), X("UW", lo // 16, hi // 16))
+            if c_ in hooks:
+                hooks[c_]()
+            tt(X("NQ", lo, hi), IN(X("T%d" % r, 0, 5136), X("LW", lo // 16, hi // 16)), X("A", lo, hi), OP.not_equal)
             for i in (2 * c_, 2 * c_ + 1):
                 mm(X("PC", 0, m), X("ZS", 15 - i, 143 - i), X("NQ", i * m, i * m + m), False, i == 15)
         act(X("P0", 0, m), X("CX", 0, m), bias=col(6 if r == 0 else 15))
@@ -451,32 +473,36 @@ def rank_program(g, core, T, topo):
         tt(X("FDB", 0, m), pc, X("H1", 0, m), OP.is_gt)
         scan(X("H2", 0, m), X("FDB", 0, m), X("ZB", 0, m), 0.0, OP.add, OP.add)
         c1 = carry("TRI", [X("H2", m - 1, m)])
-        tt(X("D0", 0, m), pc, X("H1", 0, m), OP.is_le)
+        act(X("D0", 0, m), X("FDB", 0, m), scale=-1.0, bias=1.0)
         ts(X("H3", 0, m), X("H2", 0, m), c1, OP.add, 256.5, OP.is_gt)
         ts(X("G2", 0, m), X("H2", 0, m), c1, OP.add)
         tt(mvp, pc, X("H3", 0, m), OP.is_gt)
         tt(X("H4", 0, m), mvp, X("G2", 0, m), OP.mult)
         c2 = bwd1("H1", "H4", OP.max, m, False)
-        tt(X("MV", 0, m), pc, X("H3", 0, m), OP.is_gt)
+        act(X("MV", 0, m), mvp)
+        if r == 1:
+            second_fields2(0)
         bwd2("G4", "H4", OP.max, m, c2)
         dma(X("R", 0, n, rows=1), X("G4", 0, m))
         if r == 1:
             ts(X("G5", 0, m), X("G4", 0, m), 0.5, OP.is_gt, col(10), OP.mult)
             dma(X("R", 0, n, rows=2), X("G5", 0, m), "s")
+            tr(X("PT2", 0, 128), X3("LD", 0, 4, 0, 32))
+            cp(X("LP1", 0, 64), IN(X("PT2", 0, 128), X("WO", 40, 44)))
         act(X("P1", 0, m), X("MV", 0, m), scale=-127.0 / 128)
         tt(X("G6", 0, m), X("PK", 0, m), X("FDB", 0, m), OP.mult)
         tt(X("G1", 0, m), X("P0", 0, m), X("FDB", 0, m), OP.mult)
         act(X("PK", 0, m), X("MV", 0, m), scale=127.0, bias=1.0)
-        gat("s", X(cl, 0, np_), X("R", 0, n + 16), X(lp, 0, np_ // 16))
-        send(4 * r + 2, X(cl, 0, np_), [(1, X(cl, 3 * np_, 4 * np_), 4 * r + 2), (3, X(cl, 4 * np_, 5 * np_), 4 * r + 3)])
+        gat("s", sec("CL", r, 0), X("R", 0, n + 16), X(lp, 0, np_ // 16))
+        send(4 * r + 2, sec("CL", r, 0), [(1, sec("CL", r, 3), 4 * r + 2), (3, sec("CL", r, 4), 4 * r + 3)])
         scan(X("G3", 0, m), X("D0", 0, m), X("G6", 0, m), 0.0, OP.mult, OP.add)
         c3 = carry("SHDF", [X("G3", m - 1, m)])
         c4 = bwd1("PT", "G1", OP.max, m, True)
         scan(X("G3", 0, m), X("D0", 0, m), X("G6", 0, m), c3, OP.mult, OP.add)
         bwd2("G6", "G1", OP.max, m, c4)
-        dma(X("R", 0, n, rows=3), X("G6", 0, m))
-        dma(X(cl, np_, 2 * np_), X(cl, 0, np_))
-        dma(X(cl, 2 * np_, 3 * np_), X(cl, 0, np_))
+        dma(X("RE"[r], 0, n, rows=3), X("G6", 0, m))
+        dma(sec("CL", r, 1), sec("CL", r, 0))
+        dma(sec("CL", r, 2), sec("CL", r, 0))
         tt(X("G3", 0, m), X("G3", 0, m), X("PX", 0, m), OP.subtract)
         tt(X("BE", 0, m), X("P1", 0, m), X("NF", 0, m), OP.add)
         tt(X("G3", 0, m), mvp, X("G3", 0, m), OP.mult)
@@ -496,8 +522,10 @@ def rank_program(g, core, T, topo):
         k = np_ // 16
         b = small()
         for i in range(16):
-            mm(X(b, 0, k), X("ZC", 15 - i, 143 - i), X("CL%d" % r, i, np_, 16), i == 0, i == 15)
-        act(X("PF", 0, np_), IN(X("R", 0, n + 16), X("LP%d" % r, 0, k)), bias=32.0)
+            mm(X(b, 0, k), X("ZC", 15 - i, 143 - i), X("CL%d" % r, 16 + i, 16 + np_, 16), i == 0, i == 15)
+        if r == 1:
+            second_fields2(1)
+        act(X("PF", 0, np_), IN(X("RE"[r], 0, n + 16), X("LP%d" % r, 0, k)), bias=32.0)
         ts(X("S1", 0, k), X(b, 0, k), 0.5, OP.is_lt)
         tt(X("S1", 0, k), X("S1", 0, k), X("E257", 0, k), OP.mult)
         tt(X("S1", 0, k), X("S1", 0, k), X(b, 0, k), OP.add)
@@ -508,6 +536,10 @@ def rank_program(g, core, T, topo):
             if r == 0:
                 dma(X2("FD", 1, 16 * u, 16 * u + 16), X("SW", 1, 257, rows=5))
         act(X("PX", 0, m), X("MV", 0, m), scale=1024.0, bias=-512.0)
+        act(X("G2", 0, m), X("G2", 0, m), bias=800.0 if r == 0 else col(11))
+        if r == 0:
+            act(X("UB", 0, m), half(m), bias=17.0)
+            dma(X("R", 0, n, rows=6), X("UB", 0, m))
 
     def clone_list2(r):
         k = NP[r] // 16
@@ -519,16 +551,14 @@ def rank_program(g, core, T, topo):
 
     def callee(r):
         n, m = NL[r], NL[r] // 16
-        ts(X("G2", 0, m), X("G2", 0, m), 800.0 if r == 0 else col(11), OP.add)
         tt(X("PK", 0, m), X("PM", 0, m), X("G2", 0, m), OP.mult)
         tt(X("G2", 0, m), X("PK", 0, m), X("CEF", 0, m), OP.max)
         dma(X("R", 0, n, rows=8), X("G2", 0, m))
-        act(X("PK", 0, m), X("MV", 0, m), scale=-1.0, bias=1.0)
 
-    def differ(r, c_, parts):
-        w = NL[r] // parts
-        lo, hi = c_ * w, c_ * w + w
-        tt(X("NQ", lo, hi), IN(X("T%d" % r, 0, NL[r]), X("NW", lo // 16, hi // 16)), X("A", lo, hi), OP.not_equal)
+    def differ(r, t):
+        hi = NL[r] - 512 * t
+        lo = max(0, hi - 512)
+        tt(X("NQ", lo, hi), IN(X("T%d" % r, 0, 5136), X("NW", lo // 16, hi // 16)), X("A", lo, hi), OP.not_equal)
 
     def tally(r, t):
         n, m = NL[r], NL[r] // 16
@@ -554,47 +584,66 @@ def rank_program(g, core, T, topo):
         k = np_ // 16
         lp = "LP%d" % r
         if q == "v":
-            ts(X("T15", 0, np_), IN(X("E", 0, n + 16), X(lp, 0, k)), 1.0, OP.is_ge, 2.0, OP.mult)
-        cp(X("ZI", 0, 256), IN(X("E", 0, n + 16), X(lp, k, k + 16)))
-        ts(X("ZJ", 0, 256), X("ZI", 0, 256), 127, OP.bitwise_and)
-        ts(X("T15", np_, np_ + 256), X("ZJ", 0, 256), 0.5, OP.is_gt, 2.0, OP.mult)
+            cp(X("ZI", 0, 256), IN(X("E", 0, n + 16), X(lp, k, k + 16)))
+            ts(X("ZJ", 0, 256), X("ZI", 0, 256), 127, OP.bitwise_and)
+            ts(X("T15", np_, np_ + 256), X("ZJ", 0, 256), 0.5, OP.is_gt, 2.0, OP.mult)
+            return
         for t, (lo, hi) in enumerate(((0, np_ // 2), (np_ // 2, np_), (np_, np_ + 256))):
             ps = X("P%d" % (t % 2), 0, hi - lo)
             mm(ps, mat("IDN"), X("VAL", lo, hi), True, False)
             mm(ps, mat("N8"), X("T15", lo, hi), False, True)
             ts(X("FV", lo, hi), ps, 8.0 if q == "s" and t < 2 else 0.0, OP.add, 15.0, OP.min)
 
-    def copies(r, qs):
-        n, m = NL[r], NL[r] // 16
-        w = 4 * m
-        for c_ in range(4):
+    def copies(r, q, parts):
+        w = NL[r] // 4
+        for c_ in parts:
             lo, hi = c_ * w, c_ * w + w
-            gat(qs[c_], found(r, lo, hi), X("CL%d" % r, 0, n), X("UW", lo // 16, hi // 16))
+            gat(q, found(r, lo, hi), X("CL%d" % r, 0, 5136), X("UW", lo // 16, hi // 16))
 
     def found(r, lo, hi):
         if r == 1:
             return X("J", lo, hi)
-        return X("T1", lo, hi) if hi <= 2880 else X("CL1", lo - 2880, hi - 2880)
+        return X("T1", lo, hi) if hi <= 2880 else X("CL1", lo - 2864, hi - 2864)
 
     def copies2(r, c_):
         m = NL[r] // 16
         for i in range(4 * c_, 4 * c_ + 4):
             mm(X("PC", 0, m), X("ZD", 15 - i, 143 - i), found(r, i * m, i * m + m), i == 0, i == 15)
 
+    def middle(r):
+        nt = (NL[r] + 511) // 512
+        m = NL[r] // 16
+        differ(r, 0)
+        differ(r, 1)
+        clone_list(r)
+        for t in range(nt):
+            if t + 2 < nt:
+                differ(r, t + 2)
+            tally(r, t)
+            if t == 0:
+                copies(r, "s", (0, 1, 2, 3))
+            if t == 3:
+                callee(r)
+                act(X("PK", 0, m), X("MV", 0, m), scale=-1.0, bias=1.0)
+            if t == nt - 3:
+                clone_list2(r)
+            if t >= nt - 3:
+                copies2(r, t - nt + 3)
+        copies2(r, 3)
+        formals(r, "v")
+
     def places(r):
         n, m = NL[r], NL[r] // 16
         om = X("OM", 1, m + 1)
-        if r == 0:
-            ts(om, X("PC", 0, m), 0.5, OP.is_gt, 1.0, OP.add)
-            ts(X("G5", 0, m), X("PC", 0, m), 32.0, OP.add)
-        else:
-            tt(X("G5", 0, m), X("PC", 0, m), X("VLD", 0, m), OP.mult)
-            ts(om, X("G5", 0, m), 0.5, OP.is_gt, 1.0, OP.add)
+        ts(om, X("PC", 0, m), 0.5, OP.is_gt, 1.0, OP.add)
         act(X("H2", 0, m), om, acc=col(12))
+        act(X("G5", 0, m), X("PC", 0, m), bias=32.0)
         if r == 0:
             act(X("P0", 0, m), om, bias=-1.0)
         else:
-            act(X("P0", 0, m), om, scale=768.0, bias=32.0 - 768.0)
+            act(X("P0", 0, m), om, scale=768.0, bias=-768.0)
+        lead_values(r)
+        formals_gather(r, "s")
         tt(X("H1", 0, m), X("PM", 0, m), om, OP.mult)
         tt(X("H4", 0, m), X("PK", 0, m), om, OP.mult)
         c1 = carry("TRIF", [col(12)])
@@ -613,8 +662,6 @@ def rank_program(g, core, T, topo):
         tt(half(m), X("PM", 0, m), X("G3", 0, m), OP.add)
         tt(X3("PD", 0, m // 16, 16, 32), X("PM", 0, m), X("G3", 0, m), OP.add)
         turn(X("PW", 0, m), m)
-        if r == 0:
-            tt(X("G6", 0, m), X("PM", 0, m), X("G3", 0, m), OP.add)
 
     def scatter_s(r):
         n2, h = NL[r + 1], SHARE[r]
@@ -634,64 +681,47 @@ def rank_program(g, core, T, topo):
         n2 = NL[r + 1]
         if w == 2 and SHARE[r] == NL[r]:
             return
-        for x, f in enumerate((3, 1, 2, 0)):
-            dma(X2("Z", f, 4, 4 + n2 // 16) if w == 1 else z2(r, f), X("W%d" % w, 0, n2, rows=4 * f), "y" if x % 2 == 0 or w == 2 else "s")
+        for x, f in enumerate((3, 1, 2, 0, 4)[:5 - r]):
+            dma(X2("Z", f, 4, 4 + n2 // 16) if w == 1 else z2(r, f), X("W%d" % w, 0, n2, rows=ROWS[f]), "y" if x % 2 == 0 or w == 2 else "s")
 
     def merge(r):
         m = NL[r + 1] // 16
         both = SHARE[r] < NL[r]
-        last = X3("Z", 0, 4, m + 3, m + 4)
+        k = 5 - r
+        last = X3("Z", 0, k, m + 3, m + 4)
         if both:
-            o = 1024 if r == 0 else 0
-            tt(X("TMP", 4, 8), last, X("PS", o + m - 1, o + 4 * m, m), OP.add)
+            tt(X("TMP", 8, 8 + k), last, X("PS", m - 1, 4 * m, m), OP.add)
         else:
-            ts(X("TMP", 4, 8), last, MAG, OP.add)
-        ts(X("TMP", 0, 4), X("TMP", 4, 8), -MAG, OP.add)
+            ts(X("TMP", 8, 8 + k), last, MAG, OP.add)
+        ts(X("TMP", 0, k), X("TMP", 8, 8 + k), -MAG, OP.add)
         b = small()
-        mm(X(b, 0, 4), mat("SHDF"), X("TMP", 0, 4))
-        for f in (3, 1, 2, 0):
+        mm(X(b, 0, k), mat("SHDF"), X("TMP", 0, k))
+        for f in ((3, 1, 2, 0) if both else (3, 4, 1, 2, 0)):
             if both:
                 tt(X2("Z", f, 4, m + 4), X2("Z", f, 4, m + 4), z2(r, f), OP.add)
             else:
                 addc("v" if f % 2 else "s", X2("Z", f, 4, m + 4), X2("Z", f, 4, m + 4), MAG)
             if f == 3:
-                ts(X3("Z", 0, 4, 3, 4), X(b, 0, 4), MAG, OP.add)
+                ts(X3("Z", 0, k, 3, 4), X(b, 0, k), MAG, OP.add)
         tt(X("G1", 0, m), X2("Z", 1, 4, m + 4), X2("Z", 3, 3, m + 3), OP.max)
         ts(X("KP", 0, m), X2("Z", 3, 3, m + 3), MAG + 33.0, OP.is_ge)
 
     def fill(o, f, m):
         scan(X(o, 0, m), X("KP", 0, m), X2("Z", f, 4, m + 4), X2("Z", f, 3, 4), OP.mult, OP.max)
 
-    dissent(0)
+    dissent(0, {})
     first_fields()
     prefill(0)
     splits(0)
-    differ(0, 3, 4)
-    clone_list(0)
-    differ(0, 2, 4)
-    for t in range(3):
-        tally(0, t)
-    differ(0, 1, 4)
-    clone_list2(0)
-    lead_values(0)
-    copies(0, "ssss")
-    callee(0)
-    differ(0, 0, 4)
-    first_fields2()
-    for t in range(3, 8):
-        tally(0, t)
-        if t in (5, 6, 7):
-            copies2(0, t - 5)
-    copies2(0, 3)
-    formals_gather(0, "s")
+    iota(X("E", 3856, 5120), [[0, 1264]], 0, 0)
+    middle(0)
     places(0)
     scatter_s(0)
     scatter_v(0)
     fetch(0, 2)
     formals(0, "s")
-    offsets_T(1, "v")
+    offsets_T2(1, offsets_T(1, "v"))
     ms(X("E", 3840, 3848), 5120.0)
-    dma(X("E", 0, 3840, rows=0), X("G6", 0, 240))
     a3 = args_gather(1, 3, "v", 0)
     a4 = args_gather(1, 4, "v", 1)
     args_min(1, 3, a3)
@@ -699,61 +729,61 @@ def rank_program(g, core, T, topo):
     args_min(1, 4, a4)
     a1 = args_gather(1, 1, "v", 0)
     fetch(0, 1)
+    act(X("G6", 0, 240), half(240))
+    dma(X("E", 0, 3840, rows=0), X("G6", 0, 240))
     a2 = args_gather(1, 2, "s", 1)
     args_min(1, 0, a0)
     args_min(1, 1, a1)
     args_min(1, 2, a2)
     merge(0)
     m = 320
-    fill("G3", 2, m)
-    ts(half(m), X("G1", 0, m), -(MAG + 33.0), OP.add)
-    act(X3("PD", 0, 20, 16, 32), X("G1", 0, m), bias=-(MAG + 33.0))
-    act(X("CEF", 0, m), X("G3", 0, m), bias=-MAG)
-    act(X("G5", 1, m + 1), X("CEF", 0, m), bias=-32.5, fn=AF.Abs)
-    act(X("PM", 0, m), X("CEF", 0, m), bias=-32.5)
-    act(X("PK", 0, m), X("G1", 0, m), bias=-(MAG + 33.0))
+    ts(half(m), X("G1", 0, m), -(MAG + 17.0), OP.add)
+    act(X3("PD", 0, 20, 16, 32), X("G1", 0, m), bias=-(MAG + 17.0))
+    fill("G4", 4, m)
     turn(X("UW", 0, m), m)
-    cp(X("G5", 0, 1), carry("SHDF", [X("G5", m, m + 1)]))
-    tt(X("H3", 0, m), X("PM", 0, m), X("G5", 0, m), OP.not_equal)
-    tt(X("NF", 0, m), X("PM", 0, m), X("G5", 0, m), OP.is_equal)
-    act(X("UB", 0, m), X("G1", 0, m), bias=-MAG)
-    list_static(1)
+    ts(half(m), X("G4", 0, m), -(MAG + 17.0), OP.add)
+    ts(X3("PD", 0, 20, 16, 32), X("G4", 0, m), -(MAG + 17.0), OP.add)
+    turn(X("LW", 0, m), m)
+    fill("G3", 2, m)
     prefill(1)
-    gat("s", X("PF", 0, 1024), X("E", 0, 3856), X("LP0", 0, 64))
-    for u in range(2):
-        dma(X3("LD", 0, 4, 16 * u, 16 * u + 16), X("PF", 0, 1024, rows=0))
-    dissent(1)
-    tr(X("PT2", 0, 128), X3("LD", 0, 4, 0, 32))
-    cp(X("LP1", 0, 64), IN(X("PT2", 0, 128), X("WO", 40, 44)))
-    splits(1)
-    differ(1, 3, 4)
-    clone_list(1)
-    differ(1, 2, 4)
-    for t in range(5):
-        tally(1, t)
-    differ(1, 1, 4)
-    copies(1, "ssss")
-    clone_list2(1)
-    callee(1)
-    differ(1, 0, 4)
+
+    def runs1():
+        act(X("CEF", 0, m), X("G3", 0, m), bias=-MAG)
+        act(X("G5", 1, m + 1), X("CEF", 0, m), bias=-32.5, fn=AF.Abs)
+        act(X("PM", 0, m), X("CEF", 0, m), bias=-32.5)
+
+    held = []
+
+    def runs2():
+        cp(X("G5", 0, 1), held[0])
+        tt(X("NF", 0, m), X("PM", 0, m), X("G5", 0, m), OP.is_equal)
+
+    def runs3():
+        cp(X("NF", m, m + 1), held[1])
+        gat("s", X("PF", 0, 1024), X("E", 0, 3856), X("LP0", 0, 64))
+        for u in range(2):
+            dma(X3("LD", 0, 4, 16 * u, 16 * u + 16), X("PF", 0, 1024, rows=0))
+        act(X("PK", 0, m), X("G1", 0, m), bias=-(MAG + 17.0))
+        act(X("PX", 0, m), X("G4", 0, m), bias=-(MAG + 17.0))
+        act(X("UB", 0, m), X("G1", 0, m), bias=-MAG)
+
+    dissent(1, {2: runs1, 3: lambda: held.append(carry("SHDF", [X("G5", m, m + 1)])), 4: runs2,
+                5: lambda: held.append(carry("SHU", [X("NF", 0, 1)])), 7: runs3})
+    scan(X2("Z", 4, 4, m + 4), X("KP", 0, m), X2("Z", 0, 4, m + 4), X2("Z", 0, 3, 4), OP.mult, OP.max)
     second_fields()
-    for t in range(5, 10):
-        tally(1, t)
-        if t > 5:
-            copies2(1, t - 6)
-    lead_values(1)
+    splits(1)
+    middle(1)
+    places(1)
+    scatter_s(1)
+    scatter_v(1)
+    fetch(1, 2)
+    fetch(1, 1)
     ts(col(13), col(10), -1.0, OP.mult, 256.0, OP.add)
     ts(col(14), col(10), 1024.5, OP.add)
     ts(X("S2", 0, 80), X("E257", 0, 80), col(14), OP.is_ge, col(13), OP.mult)
     ms(X("FV", 1280, 1296), 15.0)
     tt(X("S2", 0, 80), X("S2", 0, 80), X("E257", 0, 80), OP.add)
     ts(X("YO", 0, 80), X("S2", 0, 80), -257.0, OP.add, 1280.0, OP.min)
-    formals_gather(1, "s")
-    places(1)
-    scatter_s(1)
-    scatter_v(1)
-    fetch(1, 2)
-    fetch(1, 1)
     formals(1, "s")
     gat("s", X("T15", 0, 1280), X("FV", 0, 1296), X("YO", 0, 80))
     dma(HB(T.yform[:, :]), X("T15", 0, 1280))

@@ -5,47 +5,53 @@ F32, B16, I32, U16 = "float32", "bfloat16", "int32", "uint16"
 NR = 8
 NL = (3840, 5120, 6400)
 NP = (768, 1024)
+REACH = (48, 98)
 MAG = 12582912.0
-SHARE = (3840, 2560)
+BIG = 8192.0
+ARGQ = ("ssvss", "vvvvs")
+LOOKQ = ("s" * 8, "s" * 10)
+FLAGQ = "vs"
+VSHARE = 2560
+PARTS = 3
+PASSES = 4
+L_SITE, L_CALL, L_CALLEE, L_COPY, L_LEAD, L_FIRST, L_CLONE, L_COUNT = 0, 4, 8, 12, 6, 3, 1, 2
 
 
 def _s(cols, dtp):
     return ("sbuf", [128] + (cols if isinstance(cols, list) else [cols]), dtp)
 
 
-def _p(cols):
-    return ("psum", [128, cols], F32)
-
-
 SCRATCH = {
-    "J": _s(7680, B16), "T0": _s(5136, B16), "T1": _s(5136, B16),
-    "A": _s(5136, B16), "NQ": _s(5120, B16), "E": _s(5136, F32), "R": _s(5136, F32),
-    "CL0": _s(5136, B16), "CL1": _s(5136, B16), "W1": _s(6400, F32), "W2": _s(6400, F32),
-    "K32": _s(400, F32), "KM": _s(400, F32),
-    "FV": _s(1296, B16), "VAL": _s(1280, B16), "T15": _s(1280, B16), "PS": _s(2312, F32),
-    "BC": _s(2048, B16), "ZS": _s(144, B16), "ZT": _s(144, B16), "ZC": _s(144, B16), "ZD": _s(144, B16),
-    "IDF": _s(128, F32), "NKF": _s(128, F32), "GM": _s(128, B16), "BLK": _s(128, B16), "BLKF": _s(128, F32), "IDN": _s(128, B16), "N16": _s(128, B16),
-    "N8": _s(128, B16), "C85": _s(320, B16),
-    "TRI": _s(128, B16), "TRIF": _s(128, F32), "SHD": _s(128, B16), "SHDF": _s(128, F32), "SHU": _s(128, B16), "SHUF": _s(128, F32),
-    "COL": _s(16, F32), "PI": _s(4, I32), "TMP": _s(16, F32), "CX": _s(320, F32),
-    "ZB": _s(320, B16), "WO": _s(48, U16),
-    "CB": _s(240, I32), "RB": _s(48, I32),
+    "J": _s(7680, B16), "T0": _s(5136, B16), "T1": _s(5136, B16), "CL0": _s(5136, B16), "CL1": _s(5136, B16),
+    "A": _s(5136, B16), "NQ": _s(5136, B16), "N2": _s(5120, B16),
+    "E": _s(5136, F32), "R": _s(5136, F32), "W1": _s(6408, F32), "W2": _s(6408, F32), "PS": _s(2312, F32),
+    "FV": _s(1296, B16), "TP": _s(1280, B16), "BC": _s(2048, B16), "K32": _s(400, F32), "KM": _s(400, F32),
+    "ZS": _s(144, B16), "ZT": _s(144, B16), "ZC": _s(144, B16), "ZN": _s(144, B16), "ZQ": _s(144, B16), "CN": _s(320, B16),
+    "IDF": _s(128, F32), "NKF": _s(128, F32), "NTF": _s(128, F32), "SHDF": _s(128, F32), "SHUF": _s(128, F32),
+    "GM": _s(128, B16), "BLK": _s(128, B16), "IDN": _s(128, B16), "N16": _s(128, B16), "NB": _s(128, B16), "NI": _s(128, B16),
+    "TRI": _s(128, B16), "SHD": _s(128, B16), "SHU": _s(128, B16), "M127": _s(128, B16), "S127": _s(128, B16),
+    "K1024": _s(128, B16), "K33": _s(128, B16), "CNT": _s(128, B16),
+    "COL": _s(16, F32), "K16": _s(8, B16), "PI": _s(4, I32), "TMP": _s(8, F32), "CX": _s(320, F32),
+    "ZB": _s(320, B16), "ONE": _s(320, B16), "C85": _s(320, B16), "WO": _s(48, U16), "CB": _s(240, I32), "RB": _s(48, I32),
     "PD": _s([20, 32], F32), "PT": _s(640, F32), "FD": _s([2, 32], F32), "LD": _s([4, 32], F32), "PT2": _s(128, F32),
     "UW": _s(320, U16), "LW": _s(320, U16), "NW": _s(320, U16), "PW": _s(320, U16), "AO": _s(64, U16), "SO": _s(64, U16),
-    "LP0": _s(64, U16), "LP1": _s(80, U16), "YO": _s(80, U16), "BODY": _s(64, F32), "E257": _s(80, F32),
-    "S1": _s(80, F32), "S2": _s(80, F32), "S3": _s(80, F32),
-    "NF": _s(328, B16), "DIS": _s(328, B16), "OM": _s(328, B16), "BE": _s(328, B16), "MV": _s(320, B16), "FDB": _s(320, B16),
-    "H1": _s(320, B16), "H2": _s(320, B16), "H3": _s(320, B16), "H4": _s(320, B16), "D0": _s(320, B16),
-    "G1": _s(400, F32), "G2": _s(400, F32), "G3": _s(400, F32), "G4": _s(400, F32), "G5": _s(404, F32), "G6": _s(320, F32),
-    "GI": _s(256, I32), "GJ": _s(256, I32), "CEF": _s(320, F32), "UB": _s(320, F32), "KP": _s(400, B16),
-    "Z": _s([5, 404], F32),
-    "PA": _p(1024), "PC": _p(512), "PE1": _p(512), "PE2": _p(512), "PM": _p(512), "PK": _p(512), "PX": _p(512),
+    "LS0": _s(64, U16), "LS1": _s(80, U16), "LC0": _s(64, U16), "LC1": _s(80, U16), "YO": _s(32, U16),
+    "BODY": _s(64, F32), "PX": _s(80, F32), "S1": _s(64, F32), "S2": _s(64, F32), "S3": _s(64, F32), "S4": _s(64, F32), "SI": _s(64, I32),
+    "NF": _s(328, B16), "DIS": _s(328, B16), "H": _s(328, B16), "NFD": _s(320, B16), "MV": _s(320, B16), "JB": _s(240, B16),
+    "H1": _s(320, B16), "H2": _s(320, B16), "H3": _s(320, B16), "H4": _s(320, B16), "D0": _s(320, B16), "KP": _s(400, B16),
+    "U": _s(320, F32), "LF": _s(320, F32), "CE": _s(320, F32),
+    "G1": _s(320, F32), "G2": _s(320, F32), "G3": _s(320, F32), "G4": _s(320, F32), "G5": _s(320, F32),
+    "GI": _s(256, I32),
 }
-ALIAS = {"AB0": ("NQ", 0), "AB1": ("NQ", 1024), "TS": ("NQ", 2048), "F240": ("NQ", 4096), "TI": ("T15", 0),
-         "AB2": ("A", 0), "J0": ("J", 0), "J1": ("J", 1536), "J2": ("J", 3072), "J3": ("J", 4608), "J4": ("J", 6144),
-         "BS": ("W2", 0), "ZF": ("W2", 256), "XR": ("W2", 400),
-         "PF": ("PS", 0), "SW": ("PS", 1024), "ZI": ("GI", 0), "ZJ": ("GJ", 0), "P0": ("PA", 0), "P1": ("PA", 512)}
-SEMAPHORES = ["qv", "qs", "qp", "qg"] + ["d%d" % i for i in range(100)] + ["r%d" % i for i in range(8)] + ["l%d" % i for i in range(8)]
+SCRATCH.update({"P%d" % b: ("psum", [128, 512], F32) for b in range(8)})
+ALIAS = {"AB0": ("N2", 0), "AB1": ("N2", 1024), "AB2": ("N2", 2048), "TS": ("N2", 3072), "D20": ("N2", 0), "D21": ("T0", 0),
+         "J0": ("J", 0), "J1": ("J", 1536), "J2": ("J", 3072), "J3": ("J", 4608), "J4": ("J", 6144),
+         "ZF": ("W2", 0), "XR": ("W2", 144), "BLKF": ("W2", 288), "WR": ("W2", 416), "Z0": ("W2", 1280), "PF2": ("W2", 3072),
+         "Z1": ("R", 0), "Y": ("R", 3200), "PF": ("PS", 0), "SW": ("PS", 1024), "YF": ("CL0", 0), "KN": ("PT", 0)}
+SEMAPHORES = ["qv", "qs", "qp", "qg"] + ["d%d" % i for i in range(110)] + ["r%d" % i for i in range(8)] + ["l%d" % i for i in range(8)]
+
+CYC, GATHER, SCATTER, PECYC, WAKE, DMA0, DMARATE, FAR0, FARRATE = 0.9e-3, 1.4, 3.0, 0.5e-3, 0.06, 1.6, 300e3, 2.8, 25e3
+SIZE = {F32: 4, B16: 2, I32: 4, U16: 2}
 
 
 def rank_program(g, core, T, topo):
@@ -53,88 +59,73 @@ def rank_program(g, core, T, topo):
     if rank is None:
         return
     Q = {"v": g.vector, "s": g.scalar, "p": g.tensor, "g": g, "y": g.sync}
-    count = {"qv": 0, "qs": 0, "qp": 0, "qg": 0}
-    final = {}
-    waited = {q: {} for q in Q}
-    seen = {}
-    nd = [0]
+    nodes, seen, nd = [], {}, [0]
 
     def X(name, lo, hi, step=1, rows=None):
         name, o = ALIAS.get(name, (name, 0))
         lo, hi = lo + o, hi + o
         pm, ps = (0xFFFF, slice(None)) if rows is None else (1 << rows, slice(rows, 128, 16))
-        return (T[name][ps, slice(lo, hi, step) if step != 1 else slice(lo, hi)], [(name, pm, lo, hi)])
+        return (T[name][ps, slice(lo, hi, step) if step != 1 else slice(lo, hi)], [(name, pm, lo, hi)], None, len(range(lo, hi, step)), name)
 
-    def RV(name, lo, hi):
+    def RV(name, lo, hi, step=1):
         name, o = ALIAS.get(name, (name, 0))
-        lo, hi = lo + o, hi + o
-        return (T[name][:, slice(hi - 1, lo - 1 if lo > 0 else None, -1)], [(name, 0xFFFF, lo, hi)])
+        cols = range(lo + o, hi + o, step)
+        end = cols[0] - step
+        return (T[name][:, slice(cols[-1], end if end >= 0 else None, -step)], [(name, 0xFFFF, lo + o, hi + o)], None, len(cols), name)
 
     def X3(name, a, b, lo, hi):
         w = SCRATCH[name][1][2]
-        return (T[name][:, a:b, lo:hi], [(name, 0xFFFF, k * w + lo, k * w + hi) for k in range(a, b)])
-
-    def X2(name, a, lo, hi):
-        w = SCRATCH[name][1][2]
-        return (T[name][:, a, lo:hi], [(name, 0xFFFF, a * w + lo, a * w + hi)])
+        return (T[name][:, a:b, lo:hi], [(name, 0xFFFF, k * w + lo, k * w + hi) for k in range(a, b)], None, (b - a) * (hi - lo), name)
 
     def IN(win, off):
-        return (win[0].indirect(off[0]), win[1], off[1])
+        return (win[0].indirect(off[0]), win[1], off[1], 16 * off[3], win[4])
 
     def HB(ap_):
-        return (ap_, [])
+        return (ap_, [], None, 0, None)
 
-    def sync(q, reads, writes, dma_):
-        need = {}
+    def record(q, fn, reads, writes, busy, late, sem=None, inc=1, after=()):
+        deps = set(after)
         for regs, isw in ((reads, False), (writes, True)):
             for (nm, pm, lo, hi) in regs:
                 ps = SCRATCH[nm][0] == "psum"
-                for (tok, oq, ow, opm, olo, ohi) in seen.get(nm, []):
-                    same = oq == q and not dma_
-                    if ps and not same:
-                        hit = lo // 512 <= (ohi - 1) // 512 and olo // 512 <= (hi - 1) // 512
-                    else:
-                        hit = (pm & opm) and lo < ohi and olo < hi and (ow or isw) and not (same and q == "p")
-                    if hit:
-                        need[tok[0]] = max(need.get(tok[0], 0), tok[1])
-        for s_, v_ in need.items():
-            if waited[q].get(s_, 0) < v_:
-                Q[q].wait_ge(T.sem[s_], v_)
-                waited[q][s_] = v_
-
-    def note(tok, q, reads, writes):
-        final[tok[0]] = max(final.get(tok[0], 0), tok[1])
+                for (k, ow, opm, olo, ohi) in seen.get(nm, []):
+                    same = nodes[k]["q"] == q and sem is None and nodes[k]["sem"] is None
+                    if (ps and (q == "p" or not same)) or ((pm & opm) and lo < ohi and olo < hi and (ow or isw)):
+                        deps.add(k)
+        nodes.append({"q": q, "fn": fn, "deps": deps, "busy": busy, "late": late, "sem": sem, "inc": inc})
         for regs, isw in ((reads, False), (writes, True)):
             for (nm, pm, lo, hi) in regs:
-                seen.setdefault(nm, []).append((tok, q, isw, pm, lo, hi))
+                seen.setdefault(nm, []).append((len(nodes) - 1, isw, pm, lo, hi))
+        return len(nodes) - 1
 
-    def op(q, fn, out, ins, more=None):
-        reads, writes = [], list(out[1])
-        if len(out) == 3:
-            reads += out[2]
-        for i in ins:
-            if isinstance(i, tuple):
-                reads += i[1] + (i[2] if len(i) == 3 else [])
-        if more:
-            writes += more[1]
-        sync(q, reads, writes, False)
-        count["q" + q] += 1
-        fn().then_inc(T.sem["q" + q], 1)
-        note(("q" + q, count["q" + q]), q, reads, writes)
+    def op(q, fn, out, ins, rate=None, more=None, busy=None):
+        aps = [i for i in ins if isinstance(i, tuple)]
+        reads = [x for i in aps for x in i[1] + (i[2] or [])] + (out[2] or [])
+        if busy is None:
+            if out[2]:
+                busy = 0.06 + out[3] * SCATTER * CYC
+            elif aps and aps[0][2]:
+                busy = 0.06 + out[3] * GATHER * CYC
+            else:
+                rate = rate or (0.5 if all(SIZE[SCRATCH[i[4]][2]] == 2 for i in aps + [out] if i[3] > 1) else 1)
+                busy = max(64, out[3] * rate) * CYC
+        record(q, fn, reads, out[1] + (more[1] if more else []), busy, busy)
 
     def ap(x):
         return x[0] if isinstance(x, tuple) else x
 
     def dma(out, in_, q="y"):
-        sync(q, in_[1], out[1], True)
         sem = "d%d" % nd[0]
         nd[0] += 1
-        Q[q].dma_start(out[0], in_[0]).then_inc(T.sem[sem], 16)
-        note((sem, 16), "dma", in_[1], out[1])
+        side = out if out[4] else in_
+        move = (128 if side[1][0][1] == 0xFFFF else 8) * side[3] * SIZE[SCRATCH[side[4]][2]] / DMARATE
+        record(q, lambda: Q[q].dma_start(out[0], in_[0]), in_[1], out[1], max(0.1, move) if q == "y" else 0.1, DMA0 + move, sem, 16)
 
     def cp(o, i): op("v", lambda: g.vector.tensor_copy(o[0], i[0]), o, [i])
     def ms(o, c): op("v", lambda: g.vector.memset(o[0], c), o, [])
-    def tt(o, a, b, f): op("v", lambda: g.vector.tensor_tensor(o[0], a[0], b[0], f), o, [a, b])
+
+    def tt(o, a, b, f):
+        op("v", lambda: g.vector.tensor_tensor(o[0], a[0], b[0], f), o, [a, b], 2 if SCRATCH[a[4]][0] == SCRATCH[b[4]][0] else 1)
 
     def ts(o, a, s1, f1, s2=None, f2=None):
         if f2 is None:
@@ -149,31 +140,42 @@ def rank_program(g, core, T, topo):
         if fn == AF.Silu:
             op("s", lambda: g.scalar.activation(o[0], i[0], fn), o, [i])
         elif acc is None:
-            op("s", lambda: g.scalar.activation(o[0], i[0], fn, bias=ap(bias), scale=ap(scale)), o, [i, bias, scale])
+            op("s", lambda: g.scalar.activation(o[0], i[0], fn, bias=ap(bias), scale=ap(scale)), o, [i, bias, scale], 1)
         else:
-            op("s", lambda: g.scalar.activation(o[0], i[0], fn, accum_out=acc[0]), o, [i], acc)
+            op("s", lambda: g.scalar.activation(o[0], i[0], fn, accum_out=acc[0]), o, [i], 1, acc)
 
-    def mm(o, l, r, start=True, stop=True): op("p", lambda: g.tensor.matmul(o[0], l[0], r[0], start, stop), o, [l, r])
+    def mm(o, l, r, start=True, stop=True):
+        op("p", lambda: g.tensor.matmul(o[0], l[0], r[0], start, stop), o, [l, r],
+           busy=max(64, r[3]) * PECYC * (4 if SCRATCH[r[4]][2] == F32 else 1))
+
+    def mms(o, terms):
+        for x, (m_, r_) in enumerate(terms):
+            mm(o, mat(m_), r_, x == 0, x == len(terms) - 1)
 
     def iota(o, pat, base, cm, fl=True):
         if fl:
-            op("g", lambda: g.iota(o[0], pat, base, cm, allow_small_or_imprecise_dtypes=True), o, [])
+            op("g", lambda: g.iota(o[0], pat, base, cm, allow_small_or_imprecise_dtypes=True), o, [], busy=0.13 + 2 * o[3] * CYC)
         else:
-            op("g", lambda: g.iota(o[0], pat, base, cm), o, [])
+            op("g", lambda: g.iota(o[0], pat, base, cm), o, [], busy=0.13 + 2 * o[3] * CYC)
 
-    def aff(o, i, pat, f, base, cm): op("g", lambda: g.affine_select(o[0], i[0], pat, f, 0.0, base, cm), o, [i])
+    def aff(o, i, pat, f, base, cm):
+        op("g", lambda: g.affine_select(o[0], i[0], pat, f, 0.0, base, cm), o, [i], busy=0.17 + 2 * o[3] * CYC)
+
+    def const(name, lo, hi, v):
+        for a in range(lo, hi, 300):
+            iota(X(name, a, min(hi, a + 300)), [[0, min(hi, a + 300) - a]], v, 0)
+
+    def lin(q, o, i, scale, bias):
+        if q == "s":
+            act(o, i, bias=bias, scale=scale)
+        else:
+            ts(o, i, scale, OP.mult, bias, OP.add)
 
     def gat(q, o, win, off):
         if q == "s":
             act(o, IN(win, off))
         else:
             cp(o, IN(win, off))
-
-    def addc(q, o, i, c):
-        if q == "s":
-            act(o, i, bias=c)
-        else:
-            ts(o, i, c, OP.add)
 
     def common(src, dsts):
         e = [k for k in topo.engines(src, dsts[0]) if all(k in topo.engines(src, d) for d in dsts)]
@@ -186,33 +188,31 @@ def rank_program(g, core, T, topo):
         return T.cores[(r + d) % NR]
 
     def send(k, src, dsts):
-        e = common(core, [peer(rank, d) for d, _, _ in dsts])
-        sync("g", src[1], [], True)
+        ds = [d for d, _, _ in dsts]
+        e = common(core, [peer(rank, d) for d in ds])
         per = len(e) // len(dsts)
         trs = []
         for x, (d, reg, rs) in enumerate(dsts):
             rid, pid, _ = topo.addr(peer(rank, d))
             trs.append((rid, pid, sum(1 << b for b in e[x * per:(x + 1) * per]), reg, rs))
-        if len(trs) == 1:
-            rid, pid, mk, reg, rs = trs[0]
-            g.remote_dma(reg[0], src[0], T.sem["r%d" % rs], T.sem["l%d" % k], pid, rid, mk)
-        else:
-            g.remote_dma_fused([RemoteDMATransfer(dst_ids=[DstId(rid=rid, pnc=pid)], dma_engine_mask=mk, remote_sem=T.sem["r%d" % rs],
-                                                  src=src[0], dst=reg[0]) for rid, pid, mk, reg, rs in trs], local_sem=T.sem["l%d" % k])
-        note(("l%d" % k, per * len(dsts)), "dma", src[1], [])
 
-    def sec(name, r, j, lo=0, hi=None):
-        return X(name + str(r), 16 + 1024 * j + lo, 16 + 1024 * j + (NP[r] if hi is None else hi))
+        def issue():
+            if len(trs) == 1:
+                rid, pid, mk, reg, rs = trs[0]
+                g.remote_dma(reg[0], src[0], T.sem["r%d" % rs], T.sem["l%d" % k], pid, rid, mk)
+            else:
+                g.remote_dma_fused([RemoteDMATransfer(dst_ids=[DstId(rid=rid, pnc=pid)], dma_engine_mask=mk, remote_sem=T.sem["r%d" % rs],
+                                                      src=src[0], dst=reg[0]) for rid, pid, mk, reg, rs in trs], local_sem=T.sem["l%d" % k])
+        first = 2.0 if k == 0 else 0.0
+        me = record("g", issue, src[1], [], 0.3 + first, first + FAR0 + 256 * src[3] / per / FARRATE, "l%d" % k, per * len(dsts))
+        for d, reg, rs in dsts:
+            sr = (rank - d) % NR
+            record(None, None, [], reg[1], 0.0, 0.0, "r%d" % rs, len(common(T.cores[sr], [peer(sr, x) for x in ds])) // len(ds), [me])
+
+    def sec(name, r, j, lo=0, hi=None, rows=None):
+        return X(name + str(r), 16 + 1024 * j + lo, 16 + 1024 * j + (NP[r] if hi is None else hi), rows=rows)
 
     DIST = {3: 1, 4: 3}
-    ROWS = (0, 4, 8, 12, 6)
-    for r in range(2):
-        for j in (3, 4):
-            sr = (rank - DIST[j]) % NR
-            n1 = len(common(T.cores[sr], [core]))
-            note(("r%d" % (4 * r + j - 3), n1), "dma", [], sec("T", r, j)[1])
-            n2 = len(common(T.cores[sr], [peer(sr, 1), peer(sr, 3)])) // 2
-            note(("r%d" % (4 * r + j - 1), n2), "dma", [], sec("CL", r, j)[1])
 
     def col(k): return X("COL", k, k + 1)
     def mat(name): return X(name, 0, 128)
@@ -221,582 +221,459 @@ def rank_program(g, core, T, topo):
 
     def small():
         pe[0] += 1
-        return "PE%d" % (1 + pe[0] % 2)
+        return "P%d" % (2 + pe[0] % 2)
 
-    def carry(m_, cols):
-        b = small()
-        for x, c_ in enumerate(cols):
-            mm(X(b, 0, 1), mat(m_), c_, x == 0, x == len(cols) - 1)
-        return X(b, 0, 1)
+    def carry(*terms):
+        c_ = X(small(), 0, terms[0][1][3])
+        mms(c_, terms)
+        return c_
 
-    def half(m): return X3("PD", 0, m // 16, 0, 16)
+    def pick(sel, src, k, bank=None):
+        b = X(bank or small(), 0, k)
+        for i in range(16):
+            mm(b, X(sel, 15 - i, 143 - i), src(i), i == 0, i == 15)
+        return b
 
-    def twin(m): act(X3("PD", 0, m // 16, 16, 32), half(m))
+    def half(m, u=0): return X3("PD", 0, m // 16, 16 * u, 16 * u + 16)
 
-    def turn(out, m):
-        M = m // 16
-        tr(X("PT", 0, 2 * m), X3("PD", 0, M, 0, 32))
-        cp(out, IN(X("PT", 0, 2 * m), X("WO", WSEG[M], WSEG[M] + M)))
+    def fwd(o, a, b, f1, r, shift):
+        m, h = NL[r] // 16, REACH[r]
+        scan(o(0, m), a(0, m), b(0, m), 0.0, OP.mult, f1)
+        scan(o(0, h), a(0, h), b(0, h), carry((shift, o(m - 1, m))), OP.mult, f1)
 
-    def wrap(out, src, m, add=0.0):
-        ts(half(m), src, add, OP.add)
-        act(X3("PD", 0, m // 16, 16, 32), src, bias=add)
-        turn(out, m)
+    def bwd(o, b, f1, r, shift):
+        m, h = NL[r] // 16, REACH[r]
+        scan(RV(o, 0, m), RV("NF", 2, m + 2), RV(b, 0, m), 0.0, OP.mult, f1)
+        scan(RV(o, m - h, m), RV("NF", m - h + 2, m + 2), RV(b, m - h, m), carry((shift, X(o, 0, 1))), OP.mult, f1)
 
-    def fwd(o, a, b, f0, f1, m, extra=None):
-        scan(X(o, 0, m), a, b, 0.0, f0, f1)
-        c_ = carry("SHD", [X(o, m - 1, m)] + ([extra] if extra else []))
-        scan(X(o, 0, m), a, b, c_, f0, f1)
+    def at(name, o=0): return lambda lo, hi: X(name, lo + o, hi + o)
 
-    def bwd1(o, b, f1, m, fl):
-        scan(RV(o, 0, m), RV("NF", 1, m + 1), RV(b, 0, m), 0.0, OP.mult, f1)
-        return carry("SHUF" if fl else "SHU", [X(o, 0, 1)])
+    def columns(r, lo, hi):
+        m, ls, w = NL[r] // 16, X("LS%d" % r, lo, hi), hi - lo
+        ts(X("SI", 0, w), ls, -(m - 1) / 2, OP.add, 1.0 / m, OP.mult)
+        ts(X("S3", 0, w), ls, 16.0, OP.mult, 0.25, OP.add)
+        ts(X("S2", 0, w), X("SI", 0, w), 15.0, OP.min, -(16.0 * m - 1), OP.mult)
+        tt(X("S2", 0, w), X("S2", 0, w), X("S3", 0, w), OP.add)
+        cp(X("LC%d" % r, lo, hi), X("S2", 0, w))
 
-    def bwd2(o, b, f1, m, c_):
-        scan(RV(o, 0, m), RV("NF", 1, m + 1), RV(b, 0, m), c_, OP.mult, f1)
-
-    dma(X("FV", 0, 768), HB(T.form[:, :]))
+    ms(X("G5", 0, 240), 0.0)
+    dma(X("TP", 0, 768), HB(T.form[:, :]))
     dma(X("RB", 0, 48), HB(T.runs[:, :]), "s")
+    dma(X("E", 0, 3840, rows=0), X("G5", 0, 240), "s")
     dma(X("CB", 0, 240), HB(T.calls[:, :]), "s")
     for x, j in enumerate((3, 4, 0, 1, 2)):
         for h in range(2):
-            dma(X("J%d" % j, 768 * h, 768 * h + 768), HB(T.jump[:, 3840 * h + 768 * j:3840 * h + 768 * j + 768]), "y" if h == 0 or x > 1 else "s")
+            dma(X("J%d" % j, 768 * h, 768 * h + 768), HB(T.jump[:, 3840 * h + 768 * j:3840 * h + 768 * j + 768]))
     iota(X("PI", 0, 1), [[0, 1]], 0, 1, False)
     iota(X("XR", 0, 144), [[1, 144]], 0, 0)
-    iota(X("E257", 0, 80), [[16, 80]], 0, 0)
+    iota(X("PX", 0, 80), [[16, 80]], 0, 0)
     iota(X("GM", 0, 128), [[16, 8], [0, 16]], 0, 0)
-    ms(X("G5", 0, 240), 0.0)
-    ms(X("K32", 0, 400), 32.0)
-    dma(X("E", 0, 3840, rows=0), X("G5", 0, 240))
+    iota(X("PF", 0, 768), [[1, 48], [48, 16]], 33, 0)
     ts(X("PI", 1, 2), X("PI", 0, 1), 15, OP.bitwise_and)
     ts(X("PI", 2, 3), X("PI", 0, 1), 16, OP.bitwise_and)
     ms(X("ZB", 0, 320), 0.0)
     cp(X("COL", 0, 3), X("PI", 0, 3))
-    ts(col(4), col(1), 0.0, OP.is_equal, 768.0, OP.mult)
     tt(col(5), col(0), col(1), OP.subtract)
-    ts(X("BODY", 0, 64), X("E257", 0, 64), col(1), OP.add, 0.25, OP.add)
     ts(col(3), col(5), 15.0, OP.add)
-    ts(mat("BLKF"), mat("GM"), col(5), OP.is_equal)
-    ts(X("ZT", 0, 144), X("XR", 0, 144), col(3), OP.is_equal, col(4), OP.mult)
+    ts(col(4), col(1), 0.0, OP.is_equal)
+    ts(col(7), col(1), float(L_CLONE), OP.is_equal)
+    ts(col(8), col(7), -1.0, OP.mult)
+    ts(col(6), col(1), float(L_COUNT), OP.is_equal, col(8), OP.add)
+    ts(X("PX", 0, 80), X("PX", 0, 80), col(1), OP.add)
+    ts(X("BODY", 0, 64), X("PX", 0, 64), 0.25, OP.add)
+    for nm, c_ in (("ZT", col(4)), ("ZF", col(4)), ("ZS", 1.0 / 16), ("ZC", col(7)), ("ZN", col(8)), ("ZQ", col(6))):
+        ts(X(nm, 0, 144), X("XR", 0, 144), col(3), OP.is_equal, c_, OP.mult)
+    for nm, c_ in (("IDN", 1.0), ("N16", -16.0), ("IDF", 1.0), ("NB", -BIG), ("NI", -1.0), ("M127", -127.0 / 128), ("K1024", 1024.0),
+                   ("K33", 33.0), ("NKF", -1024.0)):
+        ts(mat(nm), X("XR", 0, 128), col(0), OP.is_equal, c_, OP.mult)
+    ts(mat("BLKF"), mat("GM"), col(5), OP.is_equal, -1.0, OP.mult)
     ts(mat("BLK"), mat("GM"), col(5), OP.is_equal)
-    ts(X("ZF", 0, 144), X("XR", 0, 144), col(3), OP.is_equal, col(4), OP.mult)
-    ts(mat("N16"), X("XR", 0, 128), col(0), OP.is_equal, -16.0, OP.mult)
-    ts(mat("IDN"), X("XR", 0, 128), col(0), OP.is_equal)
-    for M, o in WSEG.items():
-        iota(X("W1", 16 * o, 16 * (o + M)), [[1, 16], [32, M]], 0, 0)
-        if M == 20:
-            aff(mat("TRIF"), mat("BLKF"), [[1, 128]], OP.is_gt, 0, -1)
-    for lo, hi in ((15, 16), (39, 40), (45, 48)):
-        iota(X("W1", 16 * lo, 16 * hi), [[0, 16 * (hi - lo)]], 0, 0)
-    aff(mat("SHDF"), mat("BLKF"), [[1, 128]], OP.is_equal, -1, -1)
+    aff(mat("NTF"), mat("BLKF"), [[1, 128]], OP.is_gt, 0, -1)
+    aff(mat("SHD"), mat("BLK"), [[1, 128]], OP.is_equal, -1, -1)
     aff(mat("SHU"), mat("BLK"), [[1, 128]], OP.is_equal, 1, -1)
     aff(mat("TRI"), mat("BLK"), [[1, 128]], OP.is_gt, 0, -1)
-    aff(mat("SHD"), mat("BLK"), [[1, 128]], OP.is_equal, -1, -1)
-    aff(mat("SHUF"), mat("BLKF"), [[1, 128]], OP.is_equal, 1, -1)
+    cp(mat("SHDF"), mat("SHD"))
+    cp(mat("SHUF"), mat("SHU"))
+    ts(mat("S127"), mat("SHU"), -127.0 / 128, OP.mult)
+    ts(X("K16", 0, 1), col(4), 16.0, OP.add)
+    for M, o in WSEG.items():
+        iota(X("WR", 16 * o, 16 * (o + M)), [[1, 16], [32, M]], 0, 0)
+    for lo, hi in ((15, 16), (39, 40), (45, 48)):
+        iota(X("WR", 16 * lo, 16 * hi), [[0, 16 * (hi - lo)]], 0, 0)
+    ts(X("WO", 0, 48), pick("ZF", lambda i: X("WR", i, 768, 16), 48, "P1"), col(2), OP.add, 0.25, OP.add)
     iota(X("CX", 0, 320), [[1, 320]], 0, 0)
-
-    def offsets_T(r, f240):
-        n = NP[r]
-        k = n // 16
-        ts(X("TI", 0, n), X("FV", 0, n), 14.5, OP.is_lt)
-        b = small()
-        for i in range(16):
-            mm(X(b, 0, k), X("ZT", 15 - i, 143 - i), X("TI", i, n, 16), i == 0, i == 15)
-        addc(f240, X("F240", 0, n), X("FV", 0, n), 240.0)
-        return b
-
-    def offsets_T2(r, b):
-        k = NP[r] // 16
-        tt(X("S1", 0, k), X(b, 0, k), X("BODY", 0, k), OP.add)
-        cp(X("AO", 0, k), X("S1", 0, k))
-
-    def args_gather(r, j, q, b):
-        gat(q, X("AB%d" % b, 0, NP[r]), X("J%d" % j, 0, 1536), X("AO", 0, NP[r] // 16))
-        return "AB%d" % b
-
-    def args_min(r, j, ab):
-        n = NP[r]
-        h = n // 2
-        for c_ in range(2):
-            ps = X("P%d" % c_, 0, h)
-            mm(ps, mat("IDN"), X("F240", c_ * h, c_ * h + h), True, False)
-            mm(ps, mat("N16"), X(ab, c_ * h, c_ * h + h), False, True)
-            base = ("TS", (j - 3) * 1024) if j >= 3 else ("T%d" % r, 16 + j * 1024)
-            tt(X(base[0], base[1] + c_ * h, base[1] + c_ * h + h), X(ab, c_ * h, c_ * h + h), ps, OP.min)
-        if j >= 3:
-            k = 4 * r + j - 3
-            send(k, X("TS", (j - 3) * 1024, (j - 3) * 1024 + n), [(DIST[j], sec("T", r, j), k)])
-
-    cp(X("S2", 0, 48), X("RB", 0, 48))
-    scan(X("S3", 0, 48), X("S2", 0, 48), X("ZB", 0, 48), 0.0, OP.add, OP.add)
-    c_ = carry("TRIF", [X("S3", 47, 48)])
-    tt(X("S2", 0, 48), X("S3", 0, 48), X("S2", 0, 48), OP.subtract)
-    ts(X("SO", 0, 48), X("S2", 0, 48), c_, OP.add)
-    for h in range(2):
-        act(IN(X("E", 0, 3840), X("SO", 24 * h, 24 * h + 24)), X("K32", 0, 384), fn=AF.Silu)
-    dma(X("G5", 0, 240), X("E", 0, 3840, rows=0))
-    ts(X3("LD", 0, 3, 0, 16), X("S2", 0, 48), c_, OP.add)
-    ts(X3("LD", 0, 3, 16, 32), X("S2", 0, 48), c_, OP.add)
-    for i in range(16):
-        mm(X("PX", 0, 48), X("ZF", 15 - i, 143 - i), X("W1", i, 768, 16), i == 0, i == 15)
-    for nm in ("T0", "CL0"):
-        dma(X(nm, 0, 16), X("ZB", 0, 16))
-        for j in range(5):
-            dma(sec(nm[:-1], 0, j, 768, 1024), X("ZB", 0, 256))
-    dma(X("CL1", 0, 16), X("ZB", 0, 16))
-    ts(X("GI", 0, 240), X("CB", 0, 240), -383.5, OP.add, 1.0 / 768, OP.mult)
-    cp(X("G1", 0, 240), X("CB", 0, 240))
-    ts(X("PM", 0, 240), X("GI", 0, 240), 256.0, OP.mult, 16.0, OP.add)
-    ts(X("BS", 0, 240), X("GI", 0, 240), 1024.0, OP.mult, 768.0, OP.add)
-    b0 = offsets_T(0, "v")
-    tt(X("G2", 0, 240), X("PM", 0, 240), X("G1", 0, 240), OP.add)
-    tt(half(240), X("PM", 0, 240), X("G1", 0, 240), OP.add)
-    tt(X3("PD", 0, 15, 16, 32), X("PM", 0, 240), X("G1", 0, 240), OP.add)
-    tt(X("PK", 0, 240), X("PM", 0, 240), X("G1", 0, 240), OP.add)
-    tr(X("PT2", 0, 96), X3("LD", 0, 3, 0, 32))
+    for nm, w, v_ in (("K32", 400, 32), ("ONE", 320, 1), ("DIS", 8, 0), ("NF", 8, 1), ("KM", 400, -int(MAG) - 33)):
+        iota(X(nm, 0, w), [[0, w]], v_, 0)
     ms(X("C85", 0, 320), -8.5 / 16)
-    ts(col(6), col(1), 240.0, OP.mult)
-    ts(col(15), col(1), 320.0, OP.mult)
-    ts(col(7), col(1), 1.0, OP.is_equal)
-    ts(col(8), col(1), 2.0, OP.is_equal)
-    ts(col(9), col(1), 3.0, OP.is_equal)
-    ts(mat("N8"), X("XR", 0, 128), col(0), OP.is_equal, 8.0, OP.mult)
-    tt(col(8), col(8), col(7), OP.add)
-    ts(X("ZC", 0, 144), X("XR", 0, 144), col(3), OP.is_equal, col(7), OP.mult)
-    ts(X("ZD", 0, 144), X("XR", 0, 144), col(3), OP.is_equal, col(8), OP.mult)
-    ts(X("E257", 0, 80), X("E257", 0, 80), col(1), OP.add, 257.0, OP.add)
-    ts(X("ZS", 0, 144), X("XR", 0, 144), col(3), OP.is_equal, 1.0 / 16, OP.mult)
-    ts(col(13), col(9), 3840.0, OP.mult, 32.0, OP.add)
-    ts(col(14), col(9), 5120.0, OP.mult, 32.0, OP.add)
-    offsets_T2(0, b0)
-    a3 = args_gather(0, 3, "s", 0)
-    a4 = args_gather(0, 4, "s", 1)
-    a0 = args_gather(0, 0, "s", 2)
-    ts(X("S3", 0, 48), X("PX", 0, 48), 1.0 / 768, OP.mult, col(2), OP.add)
-    ts(X("WO", 0, 48), X("S3", 0, 48), 0.25, OP.add)
-    turn(X("UW", 0, 240), 240)
-    args_min(0, 3, a3)
-    ts(X("NF", 0, 240), X("G5", 0, 240), 1.0, OP.is_lt)
-    ts(X("H3", 0, 240), X("G5", 0, 240), 1.0, OP.is_gt)
-    args_min(0, 4, a4)
-    a1 = args_gather(0, 1, "s", 0)
-    a2 = args_gather(0, 2, "s", 1)
-    iota(X("R", 0, 5136), [[0, 5136]], 0, 0)
+    for r in range(2):
+        ts(col(9 + r), col(1), NL[r] / 16, OP.mult)
+        ts(col(11 + r), col(1), -NL[r] / 16, OP.mult, float(NL[r]), OP.add)
+    for j in range(5):
+        ms(sec("T", 0, j, 768, 1024), 0.0)
+    for nm, lo, hi, v_ in (("T0", 0, 16, 0), ("T1", 0, 16, 0), ("A", 3840, 3856, 0), ("A", 5120, 5136, 0), ("NQ", 5120, 5136, 0),
+                           ("E", 3840, 3856, 5120), ("E", 5120, 5136, 0), ("FV", 1280, 1296, 0), ("CL0", 0, 16, 0), ("CL1", 0, 16, 0),
+                           ("R", 1536, 5136, 0)):
+        const(nm, lo, hi, v_)
+    for a in range(0, 1536, 512):
+        ms(X("R", a, a + 512), 0.0)
+    ts(X("S2", 0, 16), X("XR", 0, 16), col(1), OP.is_equal)
+    for i in range(16):
+        ts(X("BC", 128 * i, 128 * i + 128), mat("BLK"), X("S2", i, i + 1), OP.mult)
 
-    def list_static(r):
-        m = NL[r] // 16
-        tt(X("G4", 0, m), X("PK", 0, m), X("H3", 0, m), OP.mult)
-        c2 = carry("SHU", [X("NF", 0, 1)])
-        scan(X("G3", 0, m), X("NF", 0, m), X("G4", 0, m), 0.0, OP.mult, OP.add)
-        c1 = carry("SHDF", [X("G3", m - 1, m)])
-        cp(X("NF", m, m + 1), c2)
-        scan(X("PX", 0, m), X("NF", 0, m), X("G4", 0, m), c1, OP.mult, OP.add)
-        cp(half(m), X("PX", 0, m))
-        cp(X3("PD", 0, m // 16, 16, 32), X("PX", 0, m))
-        turn(X("LW", 0, m), m)
+    def arguments(r):
+        n, k = NP[r], NP[r] // 16
+        b = pick("ZT", lambda i: X("FV", i, n, 16), k)
+        ts(X("S1", 0, k), b, 0.5, OP.is_gt, 768.0, OP.mult)
+        tt(X("S1", 0, k), X("S1", 0, k), X("BODY", 0, k), OP.add)
+        cp(X("AO", 0, k), X("S1", 0, k))
+        h = n // 2
+        for x, j in enumerate((3, 4, 0, 1, 2)):
+            ab = "AB%d" % (x % 3)
+            base = ("TS", (j - 3) * 1024) if j >= 3 else ("T%d" % r, 16 + j * 1024)
+            for lo in (0, h):
+                lin(ARGQ[r][x], X(ab, lo, lo + h), IN(X("J%d" % j, 0, 1536), X("AO", lo // 16, (lo + h) // 16)), -1.0, 15.0)
+                ps = X("P%d" % (6 + lo // h), 0, h)
+                mms(ps, [("IDN", X("FV", lo, lo + h)), ("N16", X(ab, lo, lo + h))])
+                tt(X(base[0], base[1] + lo, base[1] + lo + h), X(ab, lo, lo + h), ps, OP.max)
+            if j >= 3:
+                send(4 * r + j - 3, X("TS", base[1], base[1] + n), [(DIST[j], sec("T", r, j), 4 * r + j - 3)])
 
-    args_min(0, 0, a0)
-    list_static(0)
-    args_min(0, 1, a1)
-    args_min(0, 2, a2)
-    scan(X("H4", 0, 240), X("H3", 0, 240), X("ZB", 0, 240), 0.0, OP.add, OP.add)
-    cp(X("LP0", 0, 48), IN(X("PT2", 0, 96), X("WO", 36, 39)))
-    ts(col(12), carry("TRI", [X("H4", 239, 240)]), 32.0, OP.add)
-    iota(X("DIS", 0, 8), [[0, 8]], 0, 0)
-    iota(X("BC", 0, 2048), [[0, 2048]], 1, 0)
-    aff(X("BC", 0, 2048), X("BC", 0, 2048), [[-1, 16], [-16, 8], [0, 16]], OP.is_equal, 0, 1)
-    iota(X("KM", 0, 400), [[0, 400]], int(MAG), 0)
-    aff(mat("IDF"), mat("BLKF"), [[1, 128]], OP.is_equal, 0, -1)
-    iota(mat("NKF"), [[0, 128]], -1024, 0)
-    aff(mat("NKF"), mat("NKF"), [[1, 128]], OP.is_equal, 0, -1)
-    for nm, lo, v_ in (("A", 3840, 15), ("A", 5120, 15), ("E", 3840, 0), ("E", 5120, 0)):
-        iota(X(nm, lo, lo + 16), [[0, 16]], v_, 0)
-    iota(X("OM", 0, 8), [[0, 8]], 0, 0)
+    def pieces(r):
+        w = (30, 32)[r]
+        return [(a, a + w) for a in range(0, NL[r] // 16, w)]
 
-    def first_fields():
-        z = [X2("Z", f, 4, 244) for f in range(4)]
-        u = X("G1", 0, 240)
-        act(X("CEF", 0, 240), X("H4", 0, 240), bias=col(12))
-        act(z[1], u, bias=33.0)
-        act(z[2], X("G2", 0, 240), bias=17.0)
-        act(z[0], X("CEF", 0, 240), bias=-33.0)
-        dma(X("R", 0, 3840, rows=0), z[1])
-        dma(X("R", 0, 3840, rows=4), z[2])
-        dma(X("R", 0, 3840, rows=5), z[0])
+    def blocks(r, x, a, b, sel, bank="P0", last=True):
+        if x % 2 == 1:
+            a = 2 * a - b
+            for i in range(16):
+                mm(X(bank, a, b), X(sel, 15 - i, 143 - i), X("NQ", 16 * a + i, 16 * b, 16), False, last and i == 15 and b == NL[r] // 16)
 
-    def second_fields():
-        m = 320
-        z0, z1 = X2("Z", 0, 4, m + 4), X2("Z", 1, 4, m + 4)
-        act(z1, X("UB", 0, m), scale=1.0 / 1024, bias=-33.0 / 1024 - 0.4995)
-        act(z0, X2("Z", 4, 4, m + 4), bias=-MAG)
-        act(z1, z1, bias=MAG)
-        act(z1, z1, bias=-MAG, fn=AF.Relu)
-        dma(X("R", 0, 5120, rows=0), z0)
+    def dissent(r):
+        m, t_ = NL[r] // 16, X("T%d" % r, 0, 5136)
+        mm(X("P0", 0, m), mat("IDN"), X("C85", 0, m), True, False)
+        for x, (a, b) in enumerate(pieces(r)):
+            gat("s", X("A", 16 * a, 16 * b), t_, X("UW", a, b))
+            tt(X("NQ", 16 * a, 16 * b), IN(t_, X("LW", a, b)), X("A", 16 * a, 16 * b), OP.not_equal)
+            blocks(r, x, a, b, "ZS")
 
-    def second_fields2(step):
-        m = 320
-        if step == 0:
-            mm(X("PC", 0, m), mat("IDF"), X("UB", 0, m), True, False)
-            mm(X("PC", 0, m), mat("NKF"), X2("Z", 1, 4, m + 4), False, True)
-        else:
-            act(X2("Z", 2, 4, m + 4), X("PC", 0, m))
-            dma(X("R", 0, 5120, rows=4), X2("Z", 2, 4, m + 4))
-
-    def prefill(r):
-        n2 = NL[r + 1]
-        for f in ROWS[:5 - r]:
-            dma(X("W1", 0, n2, rows=f), X("K32", 0, n2 // 16))
-            if SHARE[r] < NL[r]:
-                dma(X("W2", 0, n2, rows=f), X("KM", 0, n2 // 16))
-
-    def dissent(r, hooks):
-        n, m = NL[r], NL[r] // 16
-        w = 2 * m
-        mm(X("PC", 0, m), mat("IDN"), X("C85", 0, m), True, False)
-        for c_ in range(8):
-            lo, hi = c_ * w, c_ * w + w
-            gat("s", X("A", lo, hi), X("T%d" % r, 0, 5136), X("UW", lo // 16, hi // 16))
-            if c_ in hooks:
-                hooks[c_]()
-            tt(X("NQ", lo, hi), IN(X("T%d" % r, 0, 5136), X("LW", lo // 16, hi // 16)), X("A", lo, hi), OP.not_equal)
-            for i in (2 * c_, 2 * c_ + 1):
-                mm(X("PC", 0, m), X("ZS", 15 - i, 143 - i), X("NQ", i * m, i * m + m), False, i == 15)
-        act(X("P0", 0, m), X("CX", 0, m), bias=col(6 if r == 0 else 15))
-        act(X("SW", 0, 264), X("ZB", 0, 264), bias=col(13 + r))
+    def ends(m):
+        cp(X("NF", m + 1, m + 2), carry(("SHU", X("NF", 1, 2))))
 
     def splits(r):
-        n, m, np_ = NL[r], NL[r] // 16, NP[r]
-        pc, mvp = X("PC", 0, m), X("PM", 0, m)
-        lp, cl = "LP%d" % r, "CL%d" % r
-        ts(X("DIS", 1, m + 1), pc, 0.0, OP.is_gt)
-        fwd("H1", X("DIS", 0, m), X("NF", 0, m), OP.max, OP.mult, m, extra=X("DIS", m, m + 1))
-        tt(X("FDB", 0, m), pc, X("H1", 0, m), OP.is_gt)
-        scan(X("H2", 0, m), X("FDB", 0, m), X("ZB", 0, m), 0.0, OP.add, OP.add)
-        c1 = carry("TRI", [X("H2", m - 1, m)])
-        act(X("D0", 0, m), X("FDB", 0, m), scale=-1.0, bias=1.0)
-        ts(X("H3", 0, m), X("H2", 0, m), c1, OP.add, 256.5, OP.is_gt)
-        ts(X("G2", 0, m), X("H2", 0, m), c1, OP.add)
-        tt(mvp, pc, X("H3", 0, m), OP.is_gt)
-        tt(X("H4", 0, m), mvp, X("G2", 0, m), OP.mult)
-        c2 = bwd1("H1", "H4", OP.max, m, False)
-        act(X("MV", 0, m), mvp)
+        n, m, np_, h = NL[r], NL[r] // 16, NP[r], REACH[r]
+        pc, dis, nfd, mv, x_ = X("P0", 0, m), X("DIS", 1, m + 1), X("NFD", 0, m), X("MV", 0, m), X("P1", 0, m)
+        act(X("KN", 0, m), X("CX", 0, m), bias=col(11 + r), scale=-1.0)
+        mm(X("P4", 0, m), mat("IDF"), X("KN", 0, m), True, False)
+        mm(X("P5", 0, m), mat("IDF"), X("U", 0, m), True, False)
+        ts(dis, pc, 0.0, OP.is_gt)
+        scan(X("H", 1, m + 1), X("NF", 1, m + 1), dis, 0.0, OP.mult, OP.max)
+        scan(X("H", 0, h + 1), X("NF", 0, h + 1), X("DIS", 0, h + 1), carry(("SHD", X("H", m, m + 1))), OP.mult, OP.max)
+        tt(nfd, pc, X("H", 0, m), OP.is_le)
+        scan(X("H1", 0, m), nfd, X("ONE", 0, m), 0.0, OP.add, OP.subtract)
+        ts(x_, X("H1", 0, m), carry(("TRI", X("H1", m - 1, m)), ("BLK", X("K16", 0, 1))), OP.add, 0.0, OP.max)
+        tt(X("H4", 0, m), x_, dis, OP.mult)
+        bwd("H2", "H4", OP.max, r, "SHU")
+        dma(X("NQ", 0, n, rows=L_CLONE), X("H2", 0, m))
         if r == 1:
-            second_fields2(0)
-        bwd2("G4", "H4", OP.max, m, c2)
-        dma(X("R", 0, n, rows=1), X("G4", 0, m))
-        if r == 1:
-            ts(X("G5", 0, m), X("G4", 0, m), 0.5, OP.is_gt, col(10), OP.mult)
-            dma(X("R", 0, n, rows=2), X("G5", 0, m), "s")
-            tr(X("PT2", 0, 128), X3("LD", 0, 4, 0, 32))
-            cp(X("LP1", 0, 64), IN(X("PT2", 0, 128), X("WO", 40, 44)))
-        act(X("P1", 0, m), X("MV", 0, m), scale=-127.0 / 128)
-        tt(X("G6", 0, m), X("PK", 0, m), X("FDB", 0, m), OP.mult)
-        tt(X("G1", 0, m), X("P0", 0, m), X("FDB", 0, m), OP.mult)
-        act(X("PK", 0, m), X("MV", 0, m), scale=127.0, bias=1.0)
-        gat("s", sec("CL", r, 0), X("R", 0, n + 16), X(lp, 0, np_ // 16))
+            dma(X("NQ", 0, n, rows=L_COUNT), X("CN", 0, m))
+        gat("s", sec("CL", r, 0), X("NQ", 0, n + 16 * r), X("LS%d" % r, 0, np_ // 16))
         send(4 * r + 2, sec("CL", r, 0), [(1, sec("CL", r, 3), 4 * r + 2), (3, sec("CL", r, 4), 4 * r + 3)])
-        scan(X("G3", 0, m), X("D0", 0, m), X("G6", 0, m), 0.0, OP.mult, OP.add)
-        c3 = carry("SHDF", [X("G3", m - 1, m)])
-        c4 = bwd1("PT", "G1", OP.max, m, True)
-        scan(X("G3", 0, m), X("D0", 0, m), X("G6", 0, m), c3, OP.mult, OP.add)
-        bwd2("G6", "G1", OP.max, m, c4)
-        dma(X("RE"[r], 0, n, rows=3), X("G6", 0, m))
-        dma(sec("CL", r, 1), sec("CL", r, 0))
-        dma(sec("CL", r, 2), sec("CL", r, 0))
-        tt(X("G3", 0, m), X("G3", 0, m), X("PX", 0, m), OP.subtract)
-        tt(X("BE", 0, m), X("P1", 0, m), X("NF", 0, m), OP.add)
-        tt(X("G3", 0, m), mvp, X("G3", 0, m), OP.mult)
-        c6 = carry("SHU", [X("BE", 0, 1)])
-        tt(half(m), X("PX", 0, m), X("G3", 0, m), OP.add)
-        tt(X3("PD", 0, m // 16, 16, 32), X("PX", 0, m), X("G3", 0, m), OP.add)
-        cp(X("BE", m, m + 1), c6)
-        turn(X("NW", 0, m), m)
-        tt(X("D0", 0, m), X("PK", 0, m), X("BE", 1, m + 1), OP.mult)
+        for j in (1, 2):
+            dma(sec("CL", r, j, rows=L_CLONE), sec("CL", r, 0, rows=L_CLONE))
+        tt(mv, x_, dis, OP.min)
+        mm(X("P5", 0, m), mat("NB"), nfd, False, True)
+        mm(X("P4", 0, m), mat("NB"), nfd, False, True)
+        fwd(at("G1"), at("NF", 1), at("P5"), OP.max, r, "SHDF")
+        bwd("G2", "P4", OP.max, r, "SHUF")
+        dma(X("R", 0, n, rows=L_FIRST), X("G2", 0, m))
+        act(X("P7", 0, m), mv, scale=BIG)
+        mms(X("P4", 0, m), [("IDF", X("LF", 0, m)), ("NB", mv)])
+        tt(X("G1", 0, m), X("P7", 0, m), X("G1", 0, m), OP.min)
+        tt(X("G3", 0, m), X("P4", 0, m), X("G1", 0, m), OP.max)
+        ts(X("NW", 0, m), X("G3", 0, m), -17.0, OP.add)
+        mm(X("P6", 0, m), mat("IDN"), X("NF", 2, m + 2), True, False)
+        mm(X("P6", 0, m - 1), mat("M127"), X("MV", 1, m), False, False)
+        mm(X("P6", m - 1, m), mat("S127"), X("MV", 0, 1), False, True)
+        act(X("H3", 0, m), mv, scale=127.0, bias=1.0)
+        tt(X("D0", 0, m), X("P6", 0, m), X("H3", 0, m), OP.mult)
+        mms(X("P5", 0, m), [("K1024", mv), ("K33", mv), ("NI", X("H4", 0, m))] + [("CNT", mv)] * r)
+        tt(X("G4", 0, m), X("P5", 0, m), X("CE", 0, m), OP.max)
+        dma(X("R", 0, n, rows=L_CALLEE), X("G4", 0, m))
         if r == 0:
-            c5 = carry("BLK", [X("H2", m - 1, m)])
-            ts(col(10), c5, 256.0, OP.min)
-            ts(col(11), c5, 256.0, OP.min, 800.0, OP.add)
+            dma(X("R", 0, n, rows=L_LEAD), X("G3", 0, m))
+            ts(col(13), carry(("BLK", X("H1", m - 1, m))), -1.0, OP.mult, 256.0, OP.min)
+            ts(mat("CNT"), mat("IDN"), col(13), OP.mult)
+            ts(X("CN", 0, 320), X("ONE", 0, 320), col(13), OP.mult)
+            for j in (1, 2):
+                dma(sec("CL", 1, j, rows=L_COUNT), X("CN", 0, 64))
 
     def clone_list(r):
-        n, m, np_ = NL[r], NL[r] // 16, NP[r]
-        k = np_ // 16
-        b = small()
-        for i in range(16):
-            mm(X(b, 0, k), X("ZC", 15 - i, 143 - i), X("CL%d" % r, 16 + i, 16 + np_, 16), i == 0, i == 15)
-        if r == 1:
-            second_fields2(1)
-        act(X("PF", 0, np_), IN(X("RE"[r], 0, n + 16), X("LP%d" % r, 0, k)), bias=32.0)
-        ts(X("S1", 0, k), X(b, 0, k), 0.5, OP.is_lt)
-        tt(X("S1", 0, k), X("S1", 0, k), X("E257", 0, k), OP.mult)
-        tt(X("S1", 0, k), X("S1", 0, k), X(b, 0, k), OP.add)
-        cp(X("SO", 0, k), X("S1", 0, k))
-        act(IN(X("SW", 0, 1288), X("SO", 0, k)), X("PF", 0, np_), fn=AF.Silu)
-        for u in range(2):
-            dma(X2("FD", 0, 16 * u, 16 * u + 16), X("SW", 1, 257, rows=3))
-            if r == 0:
-                dma(X2("FD", 1, 16 * u, 16 * u + 16), X("SW", 1, 257, rows=5))
-        act(X("PX", 0, m), X("MV", 0, m), scale=1024.0, bias=-512.0)
-        act(X("G2", 0, m), X("G2", 0, m), bias=800.0 if r == 0 else col(11))
+        n, np_, k = NL[r], NP[r], NP[r] // 16
+        b = pick("ZC", lambda i: X("CL%d" % r, 16 + i, 16 + np_, 16), k)
+        ts(X("S1", 0, k), b, 0.5, OP.is_lt)
+        tt(X("S1", 0, k), X("S1", 0, k), X("PX", 0, k), OP.mult)
+        tt(X("S1", 0, k), X("S1", 0, k), b, OP.subtract)
+        ts(X("SO", 0, k), X("S1", 0, k), 256.25, OP.add)
+        const("SW", 0, 256, 32)
+        act(X("PF", 0, np_), IN(X("R", 0, n + 16), X("LS%d" % r, 0, k)), bias=32.0)
+        for lo in range(0, k, 16):
+            act(IN(X("SW", 0, 1288), X("SO", lo, lo + 16)), X("PF", 16 * lo, 16 * lo + 256), fn=AF.Silu)
+        for f, lane in enumerate((L_FIRST, L_CALLEE)[:2 - r]):
+            for u in range(2):
+                dma(X3("FD", f, f + 1, 16 * u, 16 * u + 16), X("SW", 0, 256, rows=lane))
+        tr(X("PT2", 0, 64 - 32 * r), X3("FD", 0, 2 - r, 0, 32))
+        ts(X("S4", 0, 16), IN(X("PT2", 0, 32), X("WO", 44, 45)), -1.0, OP.mult, n + 32.25, OP.add)
+        cp(X("LS%d" % r, k, k + 16), X("S4", 0, 16))
+        columns(r, k, k + 16)
         if r == 0:
-            act(X("UB", 0, m), half(m), bias=17.0)
-            dma(X("R", 0, n, rows=6), X("UB", 0, m))
+            ts(X("BODY", 48, 64), IN(X("PT2", 32, 64), X("WO", 44, 45)), -64.75, OP.add)
 
-    def clone_list2(r):
-        k = NP[r] // 16
-        nf_ = 2 - r
-        tr(X("PT2", 0, 32 * nf_), X3("FD", 0, nf_, 0, 32))
-        ts(X("LP%d" % r, k, k + 16), IN(X("PT2", 0, 32), X("WO", 44, 45)), -31.75, OP.add)
-        if r == 0:
-            ts(X("BODY", 48, 64), IN(X("PT2", 32, 64), X("WO", 44, 45)), -31.75, OP.add)
+    def tally(r):
+        n, m, d2 = NL[r], NL[r] // 16, "D2%d" % r
+        for a, b in pieces(r):
+            tt(X(d2, 16 * a, 16 * b), IN(X("T%d" % r, 0, 5136), X("NW", a, b)), X("A", 16 * a, 16 * b), OP.not_equal)
+        for x, i in enumerate([y for z in range(8) for y in (15 - z, 7 - z)] + [7]):
+            lo = m - REACH[r] if x == 16 else 0
+            pb = "P%d" % (6 + x % 2)
+            mm(X(pb, lo, m), X("BC", 128 * i, 128 * i + 128), X("D0", lo, m))
+            scan(RV("E", i * m + lo, i * m + m), RV(pb, lo, m), RV(d2, 16 * lo + i, n, 16),
+                 0.0 if x < 2 else X("E", i * m + m, i * m + m + 1), OP.mult, OP.add)
 
-    def callee(r):
-        n, m = NL[r], NL[r] // 16
-        tt(X("PK", 0, m), X("PM", 0, m), X("G2", 0, m), OP.mult)
-        tt(X("G2", 0, m), X("PK", 0, m), X("CEF", 0, m), OP.max)
-        dma(X("R", 0, n, rows=8), X("G2", 0, m))
-
-    def differ(r, t):
-        hi = NL[r] - 512 * t
-        lo = max(0, hi - 512)
-        tt(X("NQ", lo, hi), IN(X("T%d" % r, 0, 5136), X("NW", lo // 16, hi // 16)), X("A", lo, hi), OP.not_equal)
-
-    def tally(r, t):
-        n, m = NL[r], NL[r] // 16
-        hi = n - 512 * t
-        lo = max(0, hi - 512)
-        pb = "P%d" % (t % 2)
-        x = lo
-        while x < hi:
-            y = min(hi, (x // m + 1) * m)
-            i = x // m
-            mm(X(pb, x - lo, y - lo), X("BC", 128 * i, 128 * i + 128), X("D0", x - i * m, y - i * m))
-            x = y
-        scan(RV("E", lo, hi), RV(pb, 0, hi - lo), RV("NQ", lo, hi), 0.0 if hi == n else X("E", hi, hi + 1), OP.mult, OP.add)
-
-    def lead_values(r):
-        gat("s", X("VAL", 0, NP[r] + 256), X("A", 0, NL[r] + 16), X("LP%d" % r, 0, NP[r] // 16 + 16))
-
-    def formals_gather(r, q):
-        act(X("T15", 0, NP[r]), IN(X("E", 0, NL[r] + 16), X("LP%d" % r, 0, NP[r] // 16)), bias=-0.88, fn=AF.Sign)
-
-    def formals(r, q):
-        n, np_ = NL[r], NP[r]
-        k = np_ // 16
-        lp = "LP%d" % r
-        if q == "v":
-            cp(X("ZI", 0, 256), IN(X("E", 0, n + 16), X(lp, k, k + 16)))
-            ts(X("ZJ", 0, 256), X("ZI", 0, 256), 127, OP.bitwise_and)
-            ts(X("T15", np_, np_ + 256), X("ZJ", 0, 256), 0.5, OP.is_gt, 2.0, OP.mult)
-            return
-        for t, (lo, hi) in enumerate(((0, np_ // 2), (np_ // 2, np_), (np_, np_ + 256))):
-            ps = X("P%d" % (t % 2), 0, hi - lo)
-            mm(ps, mat("IDN"), X("VAL", lo, hi), True, False)
-            mm(ps, mat("N8"), X("T15", lo, hi), False, True)
-            ts(X("FV", lo, hi), ps, 8.0 if q == "s" and t < 2 else 0.0, OP.add, 15.0, OP.min)
-
-    def copies(r, q, parts):
-        w = NL[r] // 4
-        for c_ in parts:
-            lo, hi = c_ * w, c_ * w + w
-            gat(q, found(r, lo, hi), X("CL%d" % r, 0, 5136), X("UW", lo // 16, hi // 16))
-
-    def found(r, lo, hi):
-        if r == 1:
-            return X("J", lo, hi)
-        return X("T1", lo, hi) if hi <= 2880 else X("CL1", lo - 2864, hi - 2864)
-
-    def copies2(r, c_):
-        m = NL[r] // 16
-        for i in range(4 * c_, 4 * c_ + 4):
-            mm(X("PC", 0, m), X("ZD", 15 - i, 143 - i), found(r, i * m, i * m + m), i == 0, i == 15)
-
-    def middle(r):
-        nt = (NL[r] + 511) // 512
-        m = NL[r] // 16
-        differ(r, 0)
-        differ(r, 1)
-        clone_list(r)
-        for t in range(nt):
-            if t + 2 < nt:
-                differ(r, t + 2)
-            tally(r, t)
-            if t == 0:
-                copies(r, "s", (0, 1, 2, 3))
-            if t == 3:
-                callee(r)
-                act(X("PK", 0, m), X("MV", 0, m), scale=-1.0, bias=1.0)
-            if t == nt - 3:
-                clone_list2(r)
-            if t >= nt - 3:
-                copies2(r, t - nt + 3)
-        copies2(r, 3)
-        formals(r, "v")
+    def formals(r):
+        n, np_, k = NL[r], NP[r], NP[r] // 16
+        if FLAGQ[r] == "s":
+            act(X("TP", 0, np_), IN(X("E", 0, n + 16), X("LS%d" % r, 0, k)), bias=64.0, scale=-64.0, fn=AF.Relu)
+        else:
+            ts(X("TP", 0, np_), IN(X("E", 0, n + 16), X("LS%d" % r, 0, k)), 0.9, OP.is_lt, 16.0, OP.mult)
+        cp(X("GI", 0, 256), IN(X("E", 0, n + 16), X("LS%d" % r, k, k + 16)))
+        ts(X("GI", 0, 256), X("GI", 0, 256), 127, OP.bitwise_and)
+        ts(X("TP", np_, np_ + 256), X("GI", 0, 256), 0.5, OP.is_lt, 16.0, OP.mult)
+        for lo in range(0, k + 16, 32):
+            hi = min(k + 16, lo + 32)
+            tt(X("FV", 16 * lo, 16 * hi), IN(X("A", 0, n + 16), X("LC%d" % r, lo, hi)), X("TP", 16 * lo, 16 * hi), OP.min)
 
     def places(r):
         n, m = NL[r], NL[r] // 16
-        om = X("OM", 1, m + 1)
-        ts(om, X("PC", 0, m), 0.5, OP.is_gt, 1.0, OP.add)
-        act(X("H2", 0, m), om, acc=col(12))
-        act(X("G5", 0, m), X("PC", 0, m), bias=32.0)
-        if r == 0:
-            act(X("P0", 0, m), om, bias=-1.0)
-        else:
-            act(X("P0", 0, m), om, scale=768.0, bias=-768.0)
-        lead_values(r)
-        formals_gather(r, "s")
-        tt(X("H1", 0, m), X("PM", 0, m), om, OP.mult)
-        tt(X("H4", 0, m), X("PK", 0, m), om, OP.mult)
-        c1 = carry("TRIF", [col(12)])
-        scan(X("H3", 0, m), X("NF", 0, m), X("H1", 0, m), 0.0, OP.mult, OP.subtract)
-        scan(X("G3", 0, m), X("OM", 0, m), X("ZB", 0, m), c1, OP.add, OP.add)
-        c2 = carry("SHD", [X("H3", m - 1, m)])
-        c3 = bwd1("H2", "H4", OP.add, m, False)
-        if r == 0:
-            tt(X("P1", 0, m), X("P0", 0, m), X("BS", 0, m), OP.mult)
-        tt(X("G1", 0, m), X("P%d" % (1 - r), 0, m), X("G5", 0, m), OP.add)
-        dma(X("R", 0, n, rows=12), X("G1", 0, m))
-        scan(X("PC", 0, m), X("NF", 0, m), X("H1", 0, m), c2, OP.mult, OP.subtract)
-        bwd2("H2", "H4", OP.add, m, c3)
-        tt(X("H2", 0, m), X("PX", 0, m), X("H2", 0, m), OP.min)
-        tt(X("PM", 0, m), X("PC", 0, m), X("H2", 0, m), OP.max)
-        tt(half(m), X("PM", 0, m), X("G3", 0, m), OP.add)
-        tt(X3("PD", 0, m // 16, 16, 32), X("PM", 0, m), X("G3", 0, m), OP.add)
-        turn(X("PW", 0, m), m)
-
-    def scatter_s(r):
-        n2, h = NL[r + 1], SHARE[r]
-        act(IN(X("W1", 0, n2), X("PW", 0, h // 16)), X("R", 0, h), fn=AF.Silu)
-
-    def scatter_v(r):
-        n, n2, h = NL[r], NL[r + 1], SHARE[r]
-        if h < n:
-            ts(IN(X("W2", 0, n2), X("PW", h // 16, n // 16)), X("R", h, n), 1.0, OP.mult, MAG - 32.0, OP.add)
-
-    def z2(r, f):
-        m = NL[r + 1] // 16
-        o = 1024 if r == 0 else 0
-        return X("PS", o + f * m, o + f * m + m)
-
-    def fetch(r, w):
-        n2 = NL[r + 1]
-        if w == 2 and SHARE[r] == NL[r]:
-            return
-        for x, f in enumerate((3, 1, 2, 0, 4)[:5 - r]):
-            dma(X2("Z", f, 4, 4 + n2 // 16) if w == 1 else z2(r, f), X("W%d" % w, 0, n2, rows=ROWS[f]), "y" if x % 2 == 0 or w == 2 else "s")
-
-    def merge(r):
-        m = NL[r + 1] // 16
-        both = SHARE[r] < NL[r]
-        k = 5 - r
-        last = X3("Z", 0, k, m + 3, m + 4)
-        if both:
-            tt(X("TMP", 8, 8 + k), last, X("PS", m - 1, 4 * m, m), OP.add)
-        else:
-            ts(X("TMP", 8, 8 + k), last, MAG, OP.add)
-        ts(X("TMP", 0, k), X("TMP", 8, 8 + k), -MAG, OP.add)
-        b = small()
-        mm(X(b, 0, k), mat("SHDF"), X("TMP", 0, k))
-        for f in ((3, 1, 2, 0) if both else (3, 4, 1, 2, 0)):
-            if both:
-                tt(X2("Z", f, 4, m + 4), X2("Z", f, 4, m + 4), z2(r, f), OP.add)
-            else:
-                addc("v" if f % 2 else "s", X2("Z", f, 4, m + 4), X2("Z", f, 4, m + 4), MAG)
-            if f == 3:
-                ts(X3("Z", 0, k, 3, 4), X(b, 0, k), MAG, OP.add)
-        tt(X("G1", 0, m), X2("Z", 1, 4, m + 4), X2("Z", 3, 3, m + 3), OP.max)
-        ts(X("KP", 0, m), X2("Z", 3, 3, m + 3), MAG + 33.0, OP.is_ge)
-
-    def fill(o, f, m):
-        scan(X(o, 0, m), X("KP", 0, m), X2("Z", f, 4, m + 4), X2("Z", f, 3, 4), OP.mult, OP.max)
-
-    dissent(0, {})
-    first_fields()
-    prefill(0)
-    splits(0)
-    iota(X("E", 3856, 5120), [[0, 1264]], 0, 0)
-    middle(0)
-    places(0)
-    scatter_s(0)
-    scatter_v(0)
-    fetch(0, 2)
-    formals(0, "s")
-    offsets_T2(1, offsets_T(1, "v"))
-    ms(X("E", 3840, 3848), 5120.0)
-    a3 = args_gather(1, 3, "v", 0)
-    a4 = args_gather(1, 4, "v", 1)
-    args_min(1, 3, a3)
-    a0 = args_gather(1, 0, "v", 2)
-    args_min(1, 4, a4)
-    a1 = args_gather(1, 1, "v", 0)
-    fetch(0, 1)
-    act(X("G6", 0, 240), half(240))
-    dma(X("E", 0, 3840, rows=0), X("G6", 0, 240))
-    a2 = args_gather(1, 2, "s", 1)
-    args_min(1, 0, a0)
-    args_min(1, 1, a1)
-    args_min(1, 2, a2)
-    merge(0)
-    m = 320
-    ts(half(m), X("G1", 0, m), -(MAG + 17.0), OP.add)
-    act(X3("PD", 0, 20, 16, 32), X("G1", 0, m), bias=-(MAG + 17.0))
-    fill("G4", 4, m)
-    turn(X("UW", 0, m), m)
-    ts(half(m), X("G4", 0, m), -(MAG + 17.0), OP.add)
-    ts(X3("PD", 0, 20, 16, 32), X("G4", 0, m), -(MAG + 17.0), OP.add)
-    turn(X("LW", 0, m), m)
-    fill("G3", 2, m)
-    prefill(1)
-
-    def runs1():
-        act(X("CEF", 0, m), X("G3", 0, m), bias=-MAG)
-        act(X("G5", 1, m + 1), X("CEF", 0, m), bias=-32.5, fn=AF.Abs)
-        act(X("PM", 0, m), X("CEF", 0, m), bias=-32.5)
-
-    held = []
-
-    def runs2():
-        cp(X("G5", 0, 1), held[0])
-        tt(X("NF", 0, m), X("PM", 0, m), X("G5", 0, m), OP.is_equal)
-
-    def runs3():
-        cp(X("NF", m, m + 1), held[1])
-        gat("s", X("PF", 0, 1024), X("E", 0, 3856), X("LP0", 0, 64))
+        mm(X("P0", 0, m), mat("IDN"), X("ZB", 0, m), True, False)
+        mm(X("P4", 0, m), mat("IDN"), X("ZB" if r else "JB", 0, m), True, False)
+        for x, (a, b) in enumerate(pieces(r)):
+            gat(LOOKQ[r][x], X("NQ", 16 * a, 16 * b), X("CL%d" % r, 0, 5136), X("UW", a, b))
+            blocks(r, x, a, b, "ZN")
+            blocks(r, x, a, b, "ZQ" if r else "ZN", "P4", False)
+        pc, om, mv, px = X("P0", 0, m), X("P1", 1, m + 1), X("MV", 0, m), X("P5", 0, m)
+        act(px, mv, scale=1024.0, bias=-512.0)
+        ms(X("P1", 0, 1), 0.0)
+        ts(om, pc, -0.5, OP.is_lt, 1.0, OP.add)
+        act(X("H3", 0, m), pc, fn=AF.Sign, acc=col(15))
+        mm(X("P4", 0, m), mat("NB"), X("H3", 0, m), False, True)
+        act(X("G1", 0, m), X("P4", 0, m), bias=1057.25 - BIG)
+        dma(X("R", 0, n, rows=L_COPY), X("G1", 0, m))
+        tt(X("H1", 0, m), om, mv, OP.mult)
+        tt(X("NFD", 0, m), om, X("H1", 0, m), OP.subtract)
+        fwd(at("H"), at("NF", 1), at("H1"), OP.subtract, r, "SHD")
+        bwd("H2", "NFD", OP.add, r, "SHU")
+        scan(X("G2", 0, m), X("P1", 0, m), X("ZB", 0, m), carry(("NTF", col(15)), ("IDF", col(9 + r))), OP.add, OP.add)
+        tt(px, px, X("H2", 0, m), OP.min)
+        tt(px, px, X("H", 0, m), OP.max)
         for u in range(2):
-            dma(X3("LD", 0, 4, 16 * u, 16 * u + 16), X("PF", 0, 1024, rows=0))
-        act(X("PK", 0, m), X("G1", 0, m), bias=-(MAG + 17.0))
-        act(X("PX", 0, m), X("G4", 0, m), bias=-(MAG + 17.0))
-        act(X("UB", 0, m), X("G1", 0, m), bias=-MAG)
+            tt(half(m, u), px, X("G2", 0, m), OP.add)
+        tr(X("PT", 0, 2 * m), X3("PD", 0, m // 16, 0, 32))
+        cp(X("PW", 0, m), IN(X("PT", 0, 2 * m), X("WO", WSEG[m // 16], WSEG[m // 16] + m // 16)))
 
-    dissent(1, {2: runs1, 3: lambda: held.append(carry("SHDF", [X("G5", m, m + 1)])), 4: runs2,
-                5: lambda: held.append(carry("SHU", [X("NF", 0, 1)])), 7: runs3})
-    scan(X2("Z", 4, 4, m + 4), X("KP", 0, m), X2("Z", 0, 4, m + 4), X2("Z", 0, 3, 4), OP.mult, OP.max)
-    second_fields()
+    def window(w, r, lane):
+        o = 7 if lane == L_COPY else 8
+        return X(w, o, o + NL[r + 1], rows=lane)
+
+    def scatter(q, r, lo, hi, parts):
+        w = (hi - lo) // parts
+        for a in range(lo, hi, w):
+            if q == "s":
+                act(IN(X("W1", 8, 8 + NL[r + 1]), X("PW", a // 16, (a + w) // 16)), X("R", a, a + w), fn=AF.Silu)
+            else:
+                ts(IN(X("W2", 8, 8 + NL[r + 1]), X("PW", a // 16, (a + w) // 16)), X("R", a, a + w), 1.0, OP.mult, -MAG - 65.0, OP.add)
+
+    act(X("FV", 0, 768), X("TP", 0, 768), scale=-1.0, bias=15.0)
+    arguments(0)
+    m = 240
+    cp(X("S4", 0, 48), X("RB", 0, 48))
+    scan(X("S3", 0, 48), X("ZB", 0, 48), X("S4", 0, 48), 0.0, OP.add, OP.subtract)
+    c_ = carry(("NTF", X("S3", 47, 48)))
+    tt(X("S4", 0, 48), X("S3", 0, 48), X("S4", 0, 48), OP.add)
+    ts(X("SO", 0, 48), X("S4", 0, 48), -1.0, OP.mult, c_, OP.add)
+    for u in range(2):
+        ts(X3("LD", 0, 3, 16 * u, 16 * u + 16), X("S4", 0, 48), -1.0, OP.mult, c_, OP.add)
+    for h in range(2):
+        act(IN(X("E", 0, 3840), X("SO", 24 * h, 24 * h + 24)), X("PF", 384 * h, 384 * h + 384), fn=AF.Silu)
+    dma(X("G5", 0, m), X("E", 0, 3840, rows=0))
+    ts(X("GI", 0, m), X("CB", 0, m), -383.5, OP.add, 1.0 / 768, OP.mult)
+    ts(X("G3", 0, m), X("CB", 0, m), 33.0, OP.add)
+    ts(X("P5", 0, m), X("GI", 0, m), 256.0, OP.mult, 0.25, OP.add)
+    tt(X("U", 0, m), X("P5", 0, m), X("G3", 0, m), OP.add)
+    ts(X("UW", 0, m), X("U", 0, m), -17.0, OP.add)
+    ts(X("JB", 0, m), X("GI", 0, m), 1024.0, OP.mult)
+    ts(X("NF", 1, m + 1), X("G5", 0, m), 1.0, OP.is_lt)
+    ends(m)
+    mms(X("P4", 0, m), [("IDF", X("U", 0, m)), ("NB", X("NF", 1, m + 1))])
+    fwd(at("LF"), at("NF", 1), at("P4"), OP.max, 0, "SHDF")
+    ts(X("LW", 0, m), X("LF", 0, m), -17.0, OP.add)
+    fwd(at("CE"), at("NF", 1), at("G5"), OP.max, 0, "SHDF")
+    tr(X("PT2", 0, 96), X3("LD", 0, 3, 0, 32))
+    cp(X("LS0", 0, 48), IN(X("PT2", 0, 96), X("WO", 36, 39)))
+    columns(0, 0, 48)
+    dma(X("R", 0, 3840, rows=L_SITE), X("G3", 0, m))
+    dma(X("R", 0, 3840, rows=L_CALL), X("U", 0, m))
+    FIELDS = (L_CALL, L_COPY, L_LEAD, L_SITE, L_CALLEE)
+    for lane in FIELDS:
+        dma(window("W1", 0, lane), X("K32", 0, 320))
+    for nm, lo, hi in (("CL0", 784, 3088), ("CL0", 3856, 4112), ("CL0", 4880, 5136), ("CL1", 1040, 3088)):
+        dma(X(nm, lo, hi), X("T0", 2816, 2816 + hi - lo))
+
+    dissent(0)
+    splits(0)
+    clone_list(0)
+    tally(0)
+    places(0)
+    formals(0)
+    scatter("s", 0, 0, 3840, PARTS)
+    act(X("G2", 0, m), half(m))
+    dma(X("E", 0, 3840, rows=0), X("G2", 0, m))
+    arguments(1)
+    m = 320
+    z = [X("Z0", f * m, f * m + m) for f in range(5)]
+    for f, lane in enumerate(FIELDS):
+        dma(z[f], window("W1", 0, lane), "ys"[f % 2])
+    cp(X("TMP", 0, 3), carry(("SHDF", X("Z0", 3 * m - 1, 5 * m, m))))
+    tt(X("U", 0, m), z[0], z[1], OP.max)
+    ts(X("UW", 0, m), X("U", 0, m), -17.0, OP.add)
+    ts(X("KP", 0, m), z[1], 100.0, OP.is_gt)
+    scan(X("LF", 0, m), X("KP", 0, m), z[2], X("TMP", 0, 1), OP.mult, OP.max)
+    ts(X("LW", 0, m), X("LF", 0, m), -17.0, OP.add)
+    tt(X("NF", 1, m + 1), X("U", 0, m), X("LF", 0, m), OP.not_equal)
+    ends(m)
+    scan(X("G3", 0, m), X("KP", 0, m), z[3], X("TMP", 1, 2), OP.mult, OP.max)
+    dma(X("R", 0, 5120, rows=L_SITE), X("G3", 0, m))
+    scan(X("CE", 0, m), X("KP", 0, m), z[4], X("TMP", 2, 3), OP.mult, OP.max)
+    act(X("G4", 0, m), X("U", 0, m), scale=1.0 / 1024, bias=-33.25 / 1024 - 0.4995)
+    act(X("G4", 0, m), X("G4", 0, m), bias=MAG)
+    act(X("G4", 0, m), X("G4", 0, m), bias=-MAG, fn=AF.Relu)
+    mms(X("P4", 0, m), [("IDF", X("U", 0, m)), ("NKF", X("G4", 0, m))])
+    act(X("G5", 0, m), X("P4", 0, m))
+    dma(X("R", 0, 5120, rows=L_CALL), X("G5", 0, m))
+    gat("s", X("PF2", 0, 1024), X("E", 0, 3856), X("LS0", 0, 64))
+    for u in range(2):
+        dma(X3("LD", 0, 4, 16 * u, 16 * u + 16), X("PF2", 0, 1024, rows=0))
+    tr(X("PT2", 0, 128), X3("LD", 0, 4, 0, 32))
+    cp(X("LS1", 0, 64), IN(X("PT2", 0, 128), X("WO", 40, 44)))
+    columns(1, 0, 64)
+    LAST = (L_COPY, L_CALL, L_CALLEE, L_SITE)
+    for lane in LAST:
+        dma(window("W1", 1, lane), X("K32", 0, 400))
+        dma(window("W2", 1, lane), X("KM", 0, 400))
+
+    dissent(1)
     splits(1)
-    middle(1)
+    clone_list(1)
+    tally(1)
     places(1)
-    scatter_s(1)
-    scatter_v(1)
-    fetch(1, 2)
-    fetch(1, 1)
-    ts(col(13), col(10), -1.0, OP.mult, 256.0, OP.add)
-    ts(col(14), col(10), 1024.5, OP.add)
-    ts(X("S2", 0, 80), X("E257", 0, 80), col(14), OP.is_ge, col(13), OP.mult)
-    ms(X("FV", 1280, 1296), 15.0)
-    tt(X("S2", 0, 80), X("S2", 0, 80), X("E257", 0, 80), OP.add)
-    ts(X("YO", 0, 80), X("S2", 0, 80), -257.0, OP.add, 1280.0, OP.min)
-    formals(1, "s")
-    gat("s", X("T15", 0, 1280), X("FV", 0, 1296), X("YO", 0, 80))
-    dma(HB(T.yform[:, :]), X("T15", 0, 1280))
+    formals(1)
+    ts(X("TMP", 4, 5), col(13), -1.0, OP.mult, 256.0, OP.add)
+    ts(X("TMP", 5, 6), col(13), 767.5, OP.add)
+    ts(X("S1", 0, 32), X("PX", 48, 80), X("TMP", 5, 6), OP.is_ge, X("TMP", 4, 5), OP.mult)
+    tt(X("S1", 0, 32), X("S1", 0, 32), X("PX", 48, 80), OP.add)
+    ts(X("YO", 0, 32), X("S1", 0, 32), 1280.0, OP.min)
+    ts(X("YF", 0, 768), X("FV", 0, 768), -1.0, OP.mult, 15.0, OP.add)
+    act(X("YF", 768, 1280), IN(X("FV", 0, 1296), X("YO", 0, 32)), scale=-1.0, bias=15.0)
+    dma(HB(T.yform[:, :]), X("YF", 0, 1280))
+    scatter("v", 1, 0, VSHARE, 2)
+    scatter("s", 1, VSHARE, 5120, 2)
     m = 400
-    merge(1)
-    act(X("G1", 0, m), X("G1", 0, m), bias=-(MAG + 33.0))
-    dma(HB(T.ycaller[:, :]), X("G1", 0, m))
-    fill("G3", 2, m)
-    act(X("G3", 0, m), X("G3", 0, m), bias=-(MAG + 33.0))
-    dma(HB(T.ycallee[:, :]), X("G3", 0, m))
-    fill("G4", 0, m)
-    ts(X("G4", 0, m), X("G4", 0, m), -(MAG + 33.0), OP.add)
-    dma(HB(T.ysite[:, :]), X("G4", 0, m), "s")
+    bank = [X(b, 0, m) for b in ("P0", "P1", "P4", "P5")]
+    for f, lane in enumerate(LAST):
+        dma(X("Z1", 2 * f * m, (2 * f + 1) * m), window("W1", 1, lane), "s")
+        dma(X("Z1", (2 * f + 1) * m, (2 * f + 2) * m), window("W2", 1, lane))
+    y = [bank[0]] + [X("Y", f * m, f * m + m) for f in range(4)]
+    for f in range(4):
+        act(bank[f], X("Z1", 2 * f * m, (2 * f + 1) * m), bias=MAG)
+        tt(y[f], bank[f], X("Z1", (2 * f + 1) * m, (2 * f + 2) * m), OP.add)
+    ts(X("KP", 0, m), y[0], 0.0, OP.is_le, -BIG, OP.mult)
+    tt(y[1], y[0], y[1], OP.max)
+    dma(HB(T.ycaller[:, :]), y[1])
+    for f, out, q in ((2, T.ycallee, "s"), (3, T.ysite, "y")):
+        o = y[4] if f == 2 else X("Z1", 0, m)
+        scan(o, X("KP", 0, m), y[f], carry(("SHDF", X("Y", f * m - 1, f * m))), OP.add, OP.max)
+        dma(HB(out[:, :]), o, q)
+
+    def plan(before, gap, rank_):
+        users = [[] for _ in nodes]
+        for k, ds in enumerate(before):
+            for d in ds:
+                users[d].append(k)
+        left = [len(ds) for ds in before]
+        can = [gap(None, k) for k in range(len(nodes))]
+        free = {q: 0.0 for q in list(Q) + [None]}
+        ready = {q: [k for k in range(len(nodes)) if left[k] == 0 and nodes[k]["q"] == q] for q in free}
+        order, start = [], [0.0] * len(nodes)
+        while len(order) < len(nodes):
+            soon, first = min((max(can[k], free[q]) + nodes[k]["busy"], k) for q in ready for k in ready[q])
+            q = nodes[first]["q"]
+            k = max([x for x in ready[q] if x == first or can[x] < soon], key=lambda x: (rank_[x], -x))
+            start[k] = max(can[k], free[q])
+            free[q] = start[k] + nodes[k]["busy"]
+            ready[q].remove(k)
+            order.append(k)
+            for u in users[k]:
+                can[u] = max(can[u], start[k] + gap(k, u))
+                left[u] -= 1
+                if left[u] == 0:
+                    ready[nodes[u]["q"]].append(u)
+        return order, start
+
+    def wake(a, b): return 0.0 if nodes[a]["q"] == nodes[b]["q"] == "p" else WAKE
+    def ahead(d, k): return 0.0 if d is None else nodes[d]["late"] + wake(d, k)
+    def back(u, k): return nodes[k]["late"] - nodes[k]["busy"] + (0.0 if u is None else nodes[u]["busy"] + wake(u, k))
+
+    deps = [sorted(x["deps"]) for x in nodes]
+    after = [[] for _ in nodes]
+    way = [0.0] * len(nodes)
+    for k in range(len(nodes) - 1, -1, -1):
+        way[k] += nodes[k]["late"]
+        for d in deps[k]:
+            way[d] = max(way[d], way[k] + WAKE)
+            after[d].append(k)
+    best = None
+    for _ in range(PASSES):
+        order, start = plan(deps, ahead, way)
+        end = [start[k] + nodes[k]["late"] for k in range(len(nodes))]
+        if best is None or max(end) < best[0]:
+            best = (max(end), order)
+        way = [t + nodes[k]["busy"] for k, t in enumerate(plan(after, back, end)[1])]
+    count = {q: 0 for q in Q}
+    waited = {q: {} for q in Q}
+    token = {}
+    for k in best[1]:
+        x = nodes[k]
+        q = x["q"]
+        if x["sem"] is None:
+            count[q] += 1
+            token[k] = ("q" + q, count[q])
+        else:
+            token[k] = (x["sem"], x["inc"])
+        if q is None:
+            continue
+        need = {}
+        for d in x["deps"]:
+            if not (q == "p" and nodes[d]["q"] == "p"):
+                need[token[d][0]] = max(need.get(token[d][0], 0), token[d][1])
+        for s_, v_ in need.items():
+            if waited[q].get(s_, 0) < v_:
+                Q[q].wait_ge(T.sem[s_], v_)
+                waited[q][s_] = v_
+        call = x["fn"]()
+        if call is not None:
+            call.then_inc(T.sem[token[k][0]], x["inc"])
+    final = {}
+    for s_, v_ in token.values():
+        final[s_] = max(final.get(s_, 0), v_)
     for s_, v_ in final.items():
         if all(waited[q].get(s_, 0) < v_ for q in Q):
             g.sync.wait_ge(T.sem[s_], v_)

from concourse.bass import DstId, RemoteDMATransfer
from concourse.mybir import AluOpType as OP, ActivationFunctionType as AF

F32, B16, I32, U16 = "float32", "bfloat16", "int32", "uint16"
NR = 8
NL = (3840, 5120, 6400)
NP = (768, 1024)
REACH = (48, 98)
MAG = 12582912.0
BIG = 8192.0
ARGQ = ("ssvss", "vvvvs")
LOOKQ = ("s" * 8, "s" * 10)
FLAGQ = "vs"
VSHARE = 2560
PARTS = 3
PASSES = 4
L_SITE, L_CALL, L_CALLEE, L_COPY, L_LEAD, L_FIRST, L_CLONE, L_COUNT = 0, 4, 8, 12, 6, 3, 1, 2


def _s(cols, dtp):
    return ("sbuf", [128] + (cols if isinstance(cols, list) else [cols]), dtp)


SCRATCH = {
    "J": _s(7680, B16), "T0": _s(5136, B16), "T1": _s(5136, B16), "CL0": _s(5136, B16), "CL1": _s(5136, B16),
    "A": _s(5136, B16), "NQ": _s(5136, B16), "N2": _s(5120, B16),
    "E": _s(5136, F32), "R": _s(5136, F32), "W1": _s(6408, F32), "W2": _s(6408, F32), "PS": _s(2312, F32),
    "FV": _s(1296, B16), "TP": _s(1280, B16), "BC": _s(2048, B16), "K32": _s(400, F32), "KM": _s(400, F32),
    "ZS": _s(144, B16), "ZT": _s(144, B16), "ZC": _s(144, B16), "ZN": _s(144, B16), "ZQ": _s(144, B16), "CN": _s(320, B16),
    "IDF": _s(128, F32), "NKF": _s(128, F32), "NTF": _s(128, F32), "SHDF": _s(128, F32), "SHUF": _s(128, F32),
    "GM": _s(128, B16), "BLK": _s(128, B16), "IDN": _s(128, B16), "N16": _s(128, B16), "NB": _s(128, B16), "NI": _s(128, B16),
    "TRI": _s(128, B16), "SHD": _s(128, B16), "SHU": _s(128, B16), "M127": _s(128, B16), "S127": _s(128, B16),
    "K1024": _s(128, B16), "K33": _s(128, B16), "CNT": _s(128, B16),
    "COL": _s(16, F32), "K16": _s(8, B16), "PI": _s(4, I32), "TMP": _s(8, F32), "CX": _s(320, F32),
    "ZB": _s(320, B16), "ONE": _s(320, B16), "C85": _s(320, B16), "WO": _s(48, U16), "CB": _s(240, I32), "RB": _s(48, I32),
    "PD": _s([20, 32], F32), "PT": _s(640, F32), "FD": _s([2, 32], F32), "LD": _s([4, 32], F32), "PT2": _s(128, F32),
    "UW": _s(320, U16), "LW": _s(320, U16), "NW": _s(320, U16), "PW": _s(320, U16), "AO": _s(64, U16), "SO": _s(64, U16),
    "LS0": _s(64, U16), "LS1": _s(80, U16), "LC0": _s(64, U16), "LC1": _s(80, U16), "YO": _s(32, U16),
    "BODY": _s(64, F32), "PX": _s(80, F32), "S1": _s(64, F32), "S2": _s(64, F32), "S3": _s(64, F32), "S4": _s(64, F32), "SI": _s(64, I32),
    "NF": _s(328, B16), "DIS": _s(328, B16), "H": _s(328, B16), "NFD": _s(320, B16), "MV": _s(320, B16), "JB": _s(240, B16),
    "H1": _s(320, B16), "H2": _s(320, B16), "H3": _s(320, B16), "H4": _s(320, B16), "D0": _s(320, B16), "KP": _s(400, B16),
    "U": _s(320, F32), "LF": _s(320, F32), "CE": _s(320, F32),
    "G1": _s(320, F32), "G2": _s(320, F32), "G3": _s(320, F32), "G4": _s(320, F32), "G5": _s(320, F32),
    "GI": _s(256, I32),
}
SCRATCH.update({"P%d" % b: ("psum", [128, 512], F32) for b in range(8)})
ALIAS = {"AB0": ("N2", 0), "AB1": ("N2", 1024), "AB2": ("N2", 2048), "TS": ("N2", 3072), "D20": ("N2", 0), "D21": ("T0", 0),
         "J0": ("J", 0), "J1": ("J", 1536), "J2": ("J", 3072), "J3": ("J", 4608), "J4": ("J", 6144),
         "ZF": ("W2", 0), "XR": ("W2", 144), "BLKF": ("W2", 288), "WR": ("W2", 416), "Z0": ("W2", 1280), "PF2": ("W2", 3072),
         "Z1": ("R", 0), "Y": ("R", 3200), "PF": ("PS", 0), "SW": ("PS", 1024), "YF": ("CL0", 0), "KN": ("PT", 0)}
SEMAPHORES = ["qv", "qs", "qp", "qg"] + ["d%d" % i for i in range(110)] + ["r%d" % i for i in range(8)] + ["l%d" % i for i in range(8)]

CYC, GATHER, SCATTER, PECYC, WAKE, DMA0, DMARATE, FAR0, FARRATE = 0.9e-3, 1.4, 3.0, 0.5e-3, 0.06, 1.6, 300e3, 2.8, 25e3
SIZE = {F32: 4, B16: 2, I32: 4, U16: 2}


def rank_program(g, core, T, topo):
    rank = T.rank_of(core)
    if rank is None:
        return
    Q = {"v": g.vector, "s": g.scalar, "p": g.tensor, "g": g, "y": g.sync}
    nodes, seen, nd = [], {}, [0]

    def X(name, lo, hi, step=1, rows=None):
        name, o = ALIAS.get(name, (name, 0))
        lo, hi = lo + o, hi + o
        pm, ps = (0xFFFF, slice(None)) if rows is None else (1 << rows, slice(rows, 128, 16))
        return (T[name][ps, slice(lo, hi, step) if step != 1 else slice(lo, hi)], [(name, pm, lo, hi)], None, len(range(lo, hi, step)), name)

    def RV(name, lo, hi, step=1):
        name, o = ALIAS.get(name, (name, 0))
        cols = range(lo + o, hi + o, step)
        end = cols[0] - step
        return (T[name][:, slice(cols[-1], end if end >= 0 else None, -step)], [(name, 0xFFFF, lo + o, hi + o)], None, len(cols), name)

    def X3(name, a, b, lo, hi):
        w = SCRATCH[name][1][2]
        return (T[name][:, a:b, lo:hi], [(name, 0xFFFF, k * w + lo, k * w + hi) for k in range(a, b)], None, (b - a) * (hi - lo), name)

    def IN(win, off):
        return (win[0].indirect(off[0]), win[1], off[1], 16 * off[3], win[4])

    def HB(ap_):
        return (ap_, [], None, 0, None)

    def record(q, fn, reads, writes, busy, late, sem=None, inc=1, after=()):
        deps = set(after)
        for regs, isw in ((reads, False), (writes, True)):
            for (nm, pm, lo, hi) in regs:
                ps = SCRATCH[nm][0] == "psum"
                for (k, ow, opm, olo, ohi) in seen.get(nm, []):
                    same = nodes[k]["q"] == q and sem is None and nodes[k]["sem"] is None
                    if (ps and (q == "p" or not same)) or ((pm & opm) and lo < ohi and olo < hi and (ow or isw)):
                        deps.add(k)
        nodes.append({"q": q, "fn": fn, "deps": deps, "busy": busy, "late": late, "sem": sem, "inc": inc})
        for regs, isw in ((reads, False), (writes, True)):
            for (nm, pm, lo, hi) in regs:
                seen.setdefault(nm, []).append((len(nodes) - 1, isw, pm, lo, hi))
        return len(nodes) - 1

    def op(q, fn, out, ins, rate=None, more=None, busy=None):
        aps = [i for i in ins if isinstance(i, tuple)]
        reads = [x for i in aps for x in i[1] + (i[2] or [])] + (out[2] or [])
        if busy is None:
            if out[2]:
                busy = 0.06 + out[3] * SCATTER * CYC
            elif aps and aps[0][2]:
                busy = 0.06 + out[3] * GATHER * CYC
            else:
                rate = rate or (0.5 if all(SIZE[SCRATCH[i[4]][2]] == 2 for i in aps + [out] if i[3] > 1) else 1)
                busy = max(64, out[3] * rate) * CYC
        record(q, fn, reads, out[1] + (more[1] if more else []), busy, busy)

    def ap(x):
        return x[0] if isinstance(x, tuple) else x

    def dma(out, in_, q="y"):
        sem = "d%d" % nd[0]
        nd[0] += 1
        side = out if out[4] else in_
        move = (128 if side[1][0][1] == 0xFFFF else 8) * side[3] * SIZE[SCRATCH[side[4]][2]] / DMARATE
        record(q, lambda: Q[q].dma_start(out[0], in_[0]), in_[1], out[1], max(0.1, move) if q == "y" else 0.1, DMA0 + move, sem, 16)

    def cp(o, i): op("v", lambda: g.vector.tensor_copy(o[0], i[0]), o, [i])
    def ms(o, c): op("v", lambda: g.vector.memset(o[0], c), o, [])

    def tt(o, a, b, f):
        op("v", lambda: g.vector.tensor_tensor(o[0], a[0], b[0], f), o, [a, b], 2 if SCRATCH[a[4]][0] == SCRATCH[b[4]][0] else 1)

    def ts(o, a, s1, f1, s2=None, f2=None):
        if f2 is None:
            op("v", lambda: g.vector.tensor_scalar(o[0], a[0], ap(s1), None, f1), o, [a, s1])
        else:
            op("v", lambda: g.vector.tensor_scalar(o[0], a[0], ap(s1), ap(s2), f1, f2), o, [a, s1, s2])

    def scan(o, a, b, ini, f0, f1): op("v", lambda: g.vector.tensor_tensor_scan(o[0], a[0], b[0], ap(ini), f0, f1), o, [a, b, ini])
    def tr(o, i): op("v", lambda: g.vector.transpose(o[0], i[0]), o, [i])

    def act(o, i, bias=0.0, scale=1.0, fn=AF.Identity, acc=None):
        if fn == AF.Silu:
            op("s", lambda: g.scalar.activation(o[0], i[0], fn), o, [i])
        elif acc is None:
            op("s", lambda: g.scalar.activation(o[0], i[0], fn, bias=ap(bias), scale=ap(scale)), o, [i, bias, scale], 1)
        else:
            op("s", lambda: g.scalar.activation(o[0], i[0], fn, accum_out=acc[0]), o, [i], 1, acc)

    def mm(o, l, r, start=True, stop=True):
        op("p", lambda: g.tensor.matmul(o[0], l[0], r[0], start, stop), o, [l, r],
           busy=max(64, r[3]) * PECYC * (4 if SCRATCH[r[4]][2] == F32 else 1))

    def mms(o, terms):
        for x, (m_, r_) in enumerate(terms):
            mm(o, mat(m_), r_, x == 0, x == len(terms) - 1)

    def iota(o, pat, base, cm, fl=True):
        if fl:
            op("g", lambda: g.iota(o[0], pat, base, cm, allow_small_or_imprecise_dtypes=True), o, [], busy=0.13 + 2 * o[3] * CYC)
        else:
            op("g", lambda: g.iota(o[0], pat, base, cm), o, [], busy=0.13 + 2 * o[3] * CYC)

    def aff(o, i, pat, f, base, cm):
        op("g", lambda: g.affine_select(o[0], i[0], pat, f, 0.0, base, cm), o, [i], busy=0.17 + 2 * o[3] * CYC)

    def const(name, lo, hi, v):
        for a in range(lo, hi, 300):
            iota(X(name, a, min(hi, a + 300)), [[0, min(hi, a + 300) - a]], v, 0)

    def lin(q, o, i, scale, bias):
        if q == "s":
            act(o, i, bias=bias, scale=scale)
        else:
            ts(o, i, scale, OP.mult, bias, OP.add)

    def gat(q, o, win, off):
        if q == "s":
            act(o, IN(win, off))
        else:
            cp(o, IN(win, off))

    def common(src, dsts):
        e = [k for k in topo.engines(src, dsts[0]) if all(k in topo.engines(src, d) for d in dsts)]
        n = 1
        while 2 * n <= min(len(e), 8):
            n *= 2
        return e[-n:]

    def peer(r, d):
        return T.cores[(r + d) % NR]

    def send(k, src, dsts):
        ds = [d for d, _, _ in dsts]
        e = common(core, [peer(rank, d) for d in ds])
        per = len(e) // len(dsts)
        trs = []
        for x, (d, reg, rs) in enumerate(dsts):
            rid, pid, _ = topo.addr(peer(rank, d))
            trs.append((rid, pid, sum(1 << b for b in e[x * per:(x + 1) * per]), reg, rs))

        def issue():
            if len(trs) == 1:
                rid, pid, mk, reg, rs = trs[0]
                g.remote_dma(reg[0], src[0], T.sem["r%d" % rs], T.sem["l%d" % k], pid, rid, mk)
            else:
                g.remote_dma_fused([RemoteDMATransfer(dst_ids=[DstId(rid=rid, pnc=pid)], dma_engine_mask=mk, remote_sem=T.sem["r%d" % rs],
                                                      src=src[0], dst=reg[0]) for rid, pid, mk, reg, rs in trs], local_sem=T.sem["l%d" % k])
        first = 2.0 if k == 0 else 0.0
        me = record("g", issue, src[1], [], 0.3 + first, first + FAR0 + 256 * src[3] / per / FARRATE, "l%d" % k, per * len(dsts))
        for d, reg, rs in dsts:
            sr = (rank - d) % NR
            record(None, None, [], reg[1], 0.0, 0.0, "r%d" % rs, len(common(T.cores[sr], [peer(sr, x) for x in ds])) // len(ds), [me])

    def sec(name, r, j, lo=0, hi=None, rows=None):
        return X(name + str(r), 16 + 1024 * j + lo, 16 + 1024 * j + (NP[r] if hi is None else hi), rows=rows)

    DIST = {3: 1, 4: 3}

    def col(k): return X("COL", k, k + 1)
    def mat(name): return X(name, 0, 128)
    WSEG = {15: 0, 20: 16, 3: 36, 4: 40, 1: 44}
    pe = [0]

    def small():
        pe[0] += 1
        return "P%d" % (2 + pe[0] % 2)

    def carry(*terms):
        c_ = X(small(), 0, terms[0][1][3])
        mms(c_, terms)
        return c_

    def pick(sel, src, k, bank=None):
        b = X(bank or small(), 0, k)
        for i in range(16):
            mm(b, X(sel, 15 - i, 143 - i), src(i), i == 0, i == 15)
        return b

    def half(m, u=0): return X3("PD", 0, m // 16, 16 * u, 16 * u + 16)

    def fwd(o, a, b, f1, r, shift):
        m, h = NL[r] // 16, REACH[r]
        scan(o(0, m), a(0, m), b(0, m), 0.0, OP.mult, f1)
        scan(o(0, h), a(0, h), b(0, h), carry((shift, o(m - 1, m))), OP.mult, f1)

    def bwd(o, b, f1, r, shift):
        m, h = NL[r] // 16, REACH[r]
        scan(RV(o, 0, m), RV("NF", 2, m + 2), RV(b, 0, m), 0.0, OP.mult, f1)
        scan(RV(o, m - h, m), RV("NF", m - h + 2, m + 2), RV(b, m - h, m), carry((shift, X(o, 0, 1))), OP.mult, f1)

    def at(name, o=0): return lambda lo, hi: X(name, lo + o, hi + o)

    def columns(r, lo, hi):
        m, ls, w = NL[r] // 16, X("LS%d" % r, lo, hi), hi - lo
        ts(X("SI", 0, w), ls, -(m - 1) / 2, OP.add, 1.0 / m, OP.mult)
        ts(X("S3", 0, w), ls, 16.0, OP.mult, 0.25, OP.add)
        ts(X("S2", 0, w), X("SI", 0, w), 15.0, OP.min, -(16.0 * m - 1), OP.mult)
        tt(X("S2", 0, w), X("S2", 0, w), X("S3", 0, w), OP.add)
        cp(X("LC%d" % r, lo, hi), X("S2", 0, w))

    ms(X("G5", 0, 240), 0.0)
    dma(X("TP", 0, 768), HB(T.form[:, :]))
    dma(X("RB", 0, 48), HB(T.runs[:, :]), "s")
    dma(X("E", 0, 3840, rows=0), X("G5", 0, 240), "s")
    dma(X("CB", 0, 240), HB(T.calls[:, :]), "s")
    for x, j in enumerate((3, 4, 0, 1, 2)):
        for h in range(2):
            dma(X("J%d" % j, 768 * h, 768 * h + 768), HB(T.jump[:, 3840 * h + 768 * j:3840 * h + 768 * j + 768]))
    iota(X("PI", 0, 1), [[0, 1]], 0, 1, False)
    iota(X("XR", 0, 144), [[1, 144]], 0, 0)
    iota(X("PX", 0, 80), [[16, 80]], 0, 0)
    iota(X("GM", 0, 128), [[16, 8], [0, 16]], 0, 0)
    iota(X("PF", 0, 768), [[1, 48], [48, 16]], 33, 0)
    ts(X("PI", 1, 2), X("PI", 0, 1), 15, OP.bitwise_and)
    ts(X("PI", 2, 3), X("PI", 0, 1), 16, OP.bitwise_and)
    ms(X("ZB", 0, 320), 0.0)
    cp(X("COL", 0, 3), X("PI", 0, 3))
    tt(col(5), col(0), col(1), OP.subtract)
    ts(col(3), col(5), 15.0, OP.add)
    ts(col(4), col(1), 0.0, OP.is_equal)
    ts(col(7), col(1), float(L_CLONE), OP.is_equal)
    ts(col(8), col(7), -1.0, OP.mult)
    ts(col(6), col(1), float(L_COUNT), OP.is_equal, col(8), OP.add)
    ts(X("PX", 0, 80), X("PX", 0, 80), col(1), OP.add)
    ts(X("BODY", 0, 64), X("PX", 0, 64), 0.25, OP.add)
    for nm, c_ in (("ZT", col(4)), ("ZF", col(4)), ("ZS", 1.0 / 16), ("ZC", col(7)), ("ZN", col(8)), ("ZQ", col(6))):
        ts(X(nm, 0, 144), X("XR", 0, 144), col(3), OP.is_equal, c_, OP.mult)
    for nm, c_ in (("IDN", 1.0), ("N16", -16.0), ("IDF", 1.0), ("NB", -BIG), ("NI", -1.0), ("M127", -127.0 / 128), ("K1024", 1024.0),
                   ("K33", 33.0), ("NKF", -1024.0)):
        ts(mat(nm), X("XR", 0, 128), col(0), OP.is_equal, c_, OP.mult)
    ts(mat("BLKF"), mat("GM"), col(5), OP.is_equal, -1.0, OP.mult)
    ts(mat("BLK"), mat("GM"), col(5), OP.is_equal)
    aff(mat("NTF"), mat("BLKF"), [[1, 128]], OP.is_gt, 0, -1)
    aff(mat("SHD"), mat("BLK"), [[1, 128]], OP.is_equal, -1, -1)
    aff(mat("SHU"), mat("BLK"), [[1, 128]], OP.is_equal, 1, -1)
    aff(mat("TRI"), mat("BLK"), [[1, 128]], OP.is_gt, 0, -1)
    cp(mat("SHDF"), mat("SHD"))
    cp(mat("SHUF"), mat("SHU"))
    ts(mat("S127"), mat("SHU"), -127.0 / 128, OP.mult)
    ts(X("K16", 0, 1), col(4), 16.0, OP.add)
    for M, o in WSEG.items():
        iota(X("WR", 16 * o, 16 * (o + M)), [[1, 16], [32, M]], 0, 0)
    for lo, hi in ((15, 16), (39, 40), (45, 48)):
        iota(X("WR", 16 * lo, 16 * hi), [[0, 16 * (hi - lo)]], 0, 0)
    ts(X("WO", 0, 48), pick("ZF", lambda i: X("WR", i, 768, 16), 48, "P1"), col(2), OP.add, 0.25, OP.add)
    iota(X("CX", 0, 320), [[1, 320]], 0, 0)
    for nm, w, v_ in (("K32", 400, 32), ("ONE", 320, 1), ("DIS", 8, 0), ("NF", 8, 1), ("KM", 400, -int(MAG) - 33)):
        iota(X(nm, 0, w), [[0, w]], v_, 0)
    ms(X("C85", 0, 320), -8.5 / 16)
    for r in range(2):
        ts(col(9 + r), col(1), NL[r] / 16, OP.mult)
        ts(col(11 + r), col(1), -NL[r] / 16, OP.mult, float(NL[r]), OP.add)
    for j in range(5):
        ms(sec("T", 0, j, 768, 1024), 0.0)
    for nm, lo, hi, v_ in (("T0", 0, 16, 0), ("T1", 0, 16, 0), ("A", 3840, 3856, 0), ("A", 5120, 5136, 0), ("NQ", 5120, 5136, 0),
                           ("E", 3840, 3856, 5120), ("E", 5120, 5136, 0), ("FV", 1280, 1296, 0), ("CL0", 0, 16, 0), ("CL1", 0, 16, 0),
                           ("R", 1536, 5136, 0)):
        const(nm, lo, hi, v_)
    for a in range(0, 1536, 512):
        ms(X("R", a, a + 512), 0.0)
    ts(X("S2", 0, 16), X("XR", 0, 16), col(1), OP.is_equal)
    for i in range(16):
        ts(X("BC", 128 * i, 128 * i + 128), mat("BLK"), X("S2", i, i + 1), OP.mult)

    def arguments(r):
        n, k = NP[r], NP[r] // 16
        b = pick("ZT", lambda i: X("FV", i, n, 16), k)
        ts(X("S1", 0, k), b, 0.5, OP.is_gt, 768.0, OP.mult)
        tt(X("S1", 0, k), X("S1", 0, k), X("BODY", 0, k), OP.add)
        cp(X("AO", 0, k), X("S1", 0, k))
        h = n // 2
        for x, j in enumerate((3, 4, 0, 1, 2)):
            ab = "AB%d" % (x % 3)
            base = ("TS", (j - 3) * 1024) if j >= 3 else ("T%d" % r, 16 + j * 1024)
            for lo in (0, h):
                lin(ARGQ[r][x], X(ab, lo, lo + h), IN(X("J%d" % j, 0, 1536), X("AO", lo // 16, (lo + h) // 16)), -1.0, 15.0)
                ps = X("P%d" % (6 + lo // h), 0, h)
                mms(ps, [("IDN", X("FV", lo, lo + h)), ("N16", X(ab, lo, lo + h))])
                tt(X(base[0], base[1] + lo, base[1] + lo + h), X(ab, lo, lo + h), ps, OP.max)
            if j >= 3:
                send(4 * r + j - 3, X("TS", base[1], base[1] + n), [(DIST[j], sec("T", r, j), 4 * r + j - 3)])

    def pieces(r):
        w = (30, 32)[r]
        return [(a, a + w) for a in range(0, NL[r] // 16, w)]

    def blocks(r, x, a, b, sel, bank="P0", last=True):
        if x % 2 == 1:
            a = 2 * a - b
            for i in range(16):
                mm(X(bank, a, b), X(sel, 15 - i, 143 - i), X("NQ", 16 * a + i, 16 * b, 16), False, last and i == 15 and b == NL[r] // 16)

    def dissent(r):
        m, t_ = NL[r] // 16, X("T%d" % r, 0, 5136)
        mm(X("P0", 0, m), mat("IDN"), X("C85", 0, m), True, False)
        for x, (a, b) in enumerate(pieces(r)):
            gat("s", X("A", 16 * a, 16 * b), t_, X("UW", a, b))
            tt(X("NQ", 16 * a, 16 * b), IN(t_, X("LW", a, b)), X("A", 16 * a, 16 * b), OP.not_equal)
            blocks(r, x, a, b, "ZS")

    def ends(m):
        cp(X("NF", m + 1, m + 2), carry(("SHU", X("NF", 1, 2))))

    def splits(r):
        n, m, np_, h = NL[r], NL[r] // 16, NP[r], REACH[r]
        pc, dis, nfd, mv, x_ = X("P0", 0, m), X("DIS", 1, m + 1), X("NFD", 0, m), X("MV", 0, m), X("P1", 0, m)
        act(X("KN", 0, m), X("CX", 0, m), bias=col(11 + r), scale=-1.0)
        mm(X("P4", 0, m), mat("IDF"), X("KN", 0, m), True, False)
        mm(X("P5", 0, m), mat("IDF"), X("U", 0, m), True, False)
        ts(dis, pc, 0.0, OP.is_gt)
        scan(X("H", 1, m + 1), X("NF", 1, m + 1), dis, 0.0, OP.mult, OP.max)
        scan(X("H", 0, h + 1), X("NF", 0, h + 1), X("DIS", 0, h + 1), carry(("SHD", X("H", m, m + 1))), OP.mult, OP.max)
        tt(nfd, pc, X("H", 0, m), OP.is_le)
        scan(X("H1", 0, m), nfd, X("ONE", 0, m), 0.0, OP.add, OP.subtract)
        ts(x_, X("H1", 0, m), carry(("TRI", X("H1", m - 1, m)), ("BLK", X("K16", 0, 1))), OP.add, 0.0, OP.max)
        tt(X("H4", 0, m), x_, dis, OP.mult)
        bwd("H2", "H4", OP.max, r, "SHU")
        dma(X("NQ", 0, n, rows=L_CLONE), X("H2", 0, m))
        if r == 1:
            dma(X("NQ", 0, n, rows=L_COUNT), X("CN", 0, m))
        gat("s", sec("CL", r, 0), X("NQ", 0, n + 16 * r), X("LS%d" % r, 0, np_ // 16))
        send(4 * r + 2, sec("CL", r, 0), [(1, sec("CL", r, 3), 4 * r + 2), (3, sec("CL", r, 4), 4 * r + 3)])
        for j in (1, 2):
            dma(sec("CL", r, j, rows=L_CLONE), sec("CL", r, 0, rows=L_CLONE))
        tt(mv, x_, dis, OP.min)
        mm(X("P5", 0, m), mat("NB"), nfd, False, True)
        mm(X("P4", 0, m), mat("NB"), nfd, False, True)
        fwd(at("G1"), at("NF", 1), at("P5"), OP.max, r, "SHDF")
        bwd("G2", "P4", OP.max, r, "SHUF")
        dma(X("R", 0, n, rows=L_FIRST), X("G2", 0, m))
        act(X("P7", 0, m), mv, scale=BIG)
        mms(X("P4", 0, m), [("IDF", X("LF", 0, m)), ("NB", mv)])
        tt(X("G1", 0, m), X("P7", 0, m), X("G1", 0, m), OP.min)
        tt(X("G3", 0, m), X("P4", 0, m), X("G1", 0, m), OP.max)
        ts(X("NW", 0, m), X("G3", 0, m), -17.0, OP.add)
        mm(X("P6", 0, m), mat("IDN"), X("NF", 2, m + 2), True, False)
        mm(X("P6", 0, m - 1), mat("M127"), X("MV", 1, m), False, False)
        mm(X("P6", m - 1, m), mat("S127"), X("MV", 0, 1), False, True)
        act(X("H3", 0, m), mv, scale=127.0, bias=1.0)
        tt(X("D0", 0, m), X("P6", 0, m), X("H3", 0, m), OP.mult)
        mms(X("P5", 0, m), [("K1024", mv), ("K33", mv), ("NI", X("H4", 0, m))] + [("CNT", mv)] * r)
        tt(X("G4", 0, m), X("P5", 0, m), X("CE", 0, m), OP.max)
        dma(X("R", 0, n, rows=L_CALLEE), X("G4", 0, m))
        if r == 0:
            dma(X("R", 0, n, rows=L_LEAD), X("G3", 0, m))
            ts(col(13), carry(("BLK", X("H1", m - 1, m))), -1.0, OP.mult, 256.0, OP.min)
            ts(mat("CNT"), mat("IDN"), col(13), OP.mult)
            ts(X("CN", 0, 320), X("ONE", 0, 320), col(13), OP.mult)
            for j in (1, 2):
                dma(sec("CL", 1, j, rows=L_COUNT), X("CN", 0, 64))

    def clone_list(r):
        n, np_, k = NL[r], NP[r], NP[r] // 16
        b = pick("ZC", lambda i: X("CL%d" % r, 16 + i, 16 + np_, 16), k)
        ts(X("S1", 0, k), b, 0.5, OP.is_lt)
        tt(X("S1", 0, k), X("S1", 0, k), X("PX", 0, k), OP.mult)
        tt(X("S1", 0, k), X("S1", 0, k), b, OP.subtract)
        ts(X("SO", 0, k), X("S1", 0, k), 256.25, OP.add)
        const("SW", 0, 256, 32)
        act(X("PF", 0, np_), IN(X("R", 0, n + 16), X("LS%d" % r, 0, k)), bias=32.0)
        for lo in range(0, k, 16):
            act(IN(X("SW", 0, 1288), X("SO", lo, lo + 16)), X("PF", 16 * lo, 16 * lo + 256), fn=AF.Silu)
        for f, lane in enumerate((L_FIRST, L_CALLEE)[:2 - r]):
            for u in range(2):
                dma(X3("FD", f, f + 1, 16 * u, 16 * u + 16), X("SW", 0, 256, rows=lane))
        tr(X("PT2", 0, 64 - 32 * r), X3("FD", 0, 2 - r, 0, 32))
        ts(X("S4", 0, 16), IN(X("PT2", 0, 32), X("WO", 44, 45)), -1.0, OP.mult, n + 32.25, OP.add)
        cp(X("LS%d" % r, k, k + 16), X("S4", 0, 16))
        columns(r, k, k + 16)
        if r == 0:
            ts(X("BODY", 48, 64), IN(X("PT2", 32, 64), X("WO", 44, 45)), -64.75, OP.add)

    def tally(r):
        n, m, d2 = NL[r], NL[r] // 16, "D2%d" % r
        for a, b in pieces(r):
            tt(X(d2, 16 * a, 16 * b), IN(X("T%d" % r, 0, 5136), X("NW", a, b)), X("A", 16 * a, 16 * b), OP.not_equal)
        for x, i in enumerate([y for z in range(8) for y in (15 - z, 7 - z)] + [7]):
            lo = m - REACH[r] if x == 16 else 0
            pb = "P%d" % (6 + x % 2)
            mm(X(pb, lo, m), X("BC", 128 * i, 128 * i + 128), X("D0", lo, m))
            scan(RV("E", i * m + lo, i * m + m), RV(pb, lo, m), RV(d2, 16 * lo + i, n, 16),
                 0.0 if x < 2 else X("E", i * m + m, i * m + m + 1), OP.mult, OP.add)

    def formals(r):
        n, np_, k = NL[r], NP[r], NP[r] // 16
        if FLAGQ[r] == "s":
            act(X("TP", 0, np_), IN(X("E", 0, n + 16), X("LS%d" % r, 0, k)), bias=64.0, scale=-64.0, fn=AF.Relu)
        else:
            ts(X("TP", 0, np_), IN(X("E", 0, n + 16), X("LS%d" % r, 0, k)), 0.9, OP.is_lt, 16.0, OP.mult)
        cp(X("GI", 0, 256), IN(X("E", 0, n + 16), X("LS%d" % r, k, k + 16)))
        ts(X("GI", 0, 256), X("GI", 0, 256), 127, OP.bitwise_and)
        ts(X("TP", np_, np_ + 256), X("GI", 0, 256), 0.5, OP.is_lt, 16.0, OP.mult)
        for lo in range(0, k + 16, 32):
            hi = min(k + 16, lo + 32)
            tt(X("FV", 16 * lo, 16 * hi), IN(X("A", 0, n + 16), X("LC%d" % r, lo, hi)), X("TP", 16 * lo, 16 * hi), OP.min)

    def places(r):
        n, m = NL[r], NL[r] // 16
        mm(X("P0", 0, m), mat("IDN"), X("ZB", 0, m), True, False)
        mm(X("P4", 0, m), mat("IDN"), X("ZB" if r else "JB", 0, m), True, False)
        for x, (a, b) in enumerate(pieces(r)):
            gat(LOOKQ[r][x], X("NQ", 16 * a, 16 * b), X("CL%d" % r, 0, 5136), X("UW", a, b))
            blocks(r, x, a, b, "ZN")
            blocks(r, x, a, b, "ZQ" if r else "ZN", "P4", False)
        pc, om, mv, px = X("P0", 0, m), X("P1", 1, m + 1), X("MV", 0, m), X("P5", 0, m)
        act(px, mv, scale=1024.0, bias=-512.0)
        ms(X("P1", 0, 1), 0.0)
        ts(om, pc, -0.5, OP.is_lt, 1.0, OP.add)
        act(X("H3", 0, m), pc, fn=AF.Sign, acc=col(15))
        mm(X("P4", 0, m), mat("NB"), X("H3", 0, m), False, True)
        act(X("G1", 0, m), X("P4", 0, m), bias=1057.25 - BIG)
        dma(X("R", 0, n, rows=L_COPY), X("G1", 0, m))
        tt(X("H1", 0, m), om, mv, OP.mult)
        tt(X("NFD", 0, m), om, X("H1", 0, m), OP.subtract)
        fwd(at("H"), at("NF", 1), at("H1"), OP.subtract, r, "SHD")
        bwd("H2", "NFD", OP.add, r, "SHU")
        scan(X("G2", 0, m), X("P1", 0, m), X("ZB", 0, m), carry(("NTF", col(15)), ("IDF", col(9 + r))), OP.add, OP.add)
        tt(px, px, X("H2", 0, m), OP.min)
        tt(px, px, X("H", 0, m), OP.max)
        for u in range(2):
            tt(half(m, u), px, X("G2", 0, m), OP.add)
        tr(X("PT", 0, 2 * m), X3("PD", 0, m // 16, 0, 32))
        cp(X("PW", 0, m), IN(X("PT", 0, 2 * m), X("WO", WSEG[m // 16], WSEG[m // 16] + m // 16)))

    def window(w, r, lane):
        o = 7 if lane == L_COPY else 8
        return X(w, o, o + NL[r + 1], rows=lane)

    def scatter(q, r, lo, hi, parts):
        w = (hi - lo) // parts
        for a in range(lo, hi, w):
            if q == "s":
                act(IN(X("W1", 8, 8 + NL[r + 1]), X("PW", a // 16, (a + w) // 16)), X("R", a, a + w), fn=AF.Silu)
            else:
                ts(IN(X("W2", 8, 8 + NL[r + 1]), X("PW", a // 16, (a + w) // 16)), X("R", a, a + w), 1.0, OP.mult, -MAG - 65.0, OP.add)

    act(X("FV", 0, 768), X("TP", 0, 768), scale=-1.0, bias=15.0)
    arguments(0)
    m = 240
    cp(X("S4", 0, 48), X("RB", 0, 48))
    scan(X("S3", 0, 48), X("ZB", 0, 48), X("S4", 0, 48), 0.0, OP.add, OP.subtract)
    c_ = carry(("NTF", X("S3", 47, 48)))
    tt(X("S4", 0, 48), X("S3", 0, 48), X("S4", 0, 48), OP.add)
    ts(X("SO", 0, 48), X("S4", 0, 48), -1.0, OP.mult, c_, OP.add)
    for u in range(2):
        ts(X3("LD", 0, 3, 16 * u, 16 * u + 16), X("S4", 0, 48), -1.0, OP.mult, c_, OP.add)
    for h in range(2):
        act(IN(X("E", 0, 3840), X("SO", 24 * h, 24 * h + 24)), X("PF", 384 * h, 384 * h + 384), fn=AF.Silu)
    dma(X("G5", 0, m), X("E", 0, 3840, rows=0))
    ts(X("GI", 0, m), X("CB", 0, m), -383.5, OP.add, 1.0 / 768, OP.mult)
    ts(X("G3", 0, m), X("CB", 0, m), 33.0, OP.add)
    ts(X("P5", 0, m), X("GI", 0, m), 256.0, OP.mult, 0.25, OP.add)
    tt(X("U", 0, m), X("P5", 0, m), X("G3", 0, m), OP.add)
    ts(X("UW", 0, m), X("U", 0, m), -17.0, OP.add)
    ts(X("JB", 0, m), X("GI", 0, m), 1024.0, OP.mult)
    ts(X("NF", 1, m + 1), X("G5", 0, m), 1.0, OP.is_lt)
    ends(m)
    mms(X("P4", 0, m), [("IDF", X("U", 0, m)), ("NB", X("NF", 1, m + 1))])
    fwd(at("LF"), at("NF", 1), at("P4"), OP.max, 0, "SHDF")
    ts(X("LW", 0, m), X("LF", 0, m), -17.0, OP.add)
    fwd(at("CE"), at("NF", 1), at("G5"), OP.max, 0, "SHDF")
    tr(X("PT2", 0, 96), X3("LD", 0, 3, 0, 32))
    cp(X("LS0", 0, 48), IN(X("PT2", 0, 96), X("WO", 36, 39)))
    columns(0, 0, 48)
    dma(X("R", 0, 3840, rows=L_SITE), X("G3", 0, m))
    dma(X("R", 0, 3840, rows=L_CALL), X("U", 0, m))
    FIELDS = (L_CALL, L_COPY, L_LEAD, L_SITE, L_CALLEE)
    for lane in FIELDS:
        dma(window("W1", 0, lane), X("K32", 0, 320))
    for nm, lo, hi in (("CL0", 784, 3088), ("CL0", 3856, 4112), ("CL0", 4880, 5136), ("CL1", 1040, 3088)):
        dma(X(nm, lo, hi), X("T0", 2816, 2816 + hi - lo))

    dissent(0)
    splits(0)
    clone_list(0)
    tally(0)
    places(0)
    formals(0)
    scatter("s", 0, 0, 3840, PARTS)
    act(X("G2", 0, m), half(m))
    dma(X("E", 0, 3840, rows=0), X("G2", 0, m))
    arguments(1)
    m = 320
    z = [X("Z0", f * m, f * m + m) for f in range(5)]
    for f, lane in enumerate(FIELDS):
        dma(z[f], window("W1", 0, lane), "ys"[f % 2])
    cp(X("TMP", 0, 3), carry(("SHDF", X("Z0", 3 * m - 1, 5 * m, m))))
    tt(X("U", 0, m), z[0], z[1], OP.max)
    ts(X("UW", 0, m), X("U", 0, m), -17.0, OP.add)
    ts(X("KP", 0, m), z[1], 100.0, OP.is_gt)
    scan(X("LF", 0, m), X("KP", 0, m), z[2], X("TMP", 0, 1), OP.mult, OP.max)
    ts(X("LW", 0, m), X("LF", 0, m), -17.0, OP.add)
    tt(X("NF", 1, m + 1), X("U", 0, m), X("LF", 0, m), OP.not_equal)
    ends(m)
    scan(X("G3", 0, m), X("KP", 0, m), z[3], X("TMP", 1, 2), OP.mult, OP.max)
    dma(X("R", 0, 5120, rows=L_SITE), X("G3", 0, m))
    scan(X("CE", 0, m), X("KP", 0, m), z[4], X("TMP", 2, 3), OP.mult, OP.max)
    act(X("G4", 0, m), X("U", 0, m), scale=1.0 / 1024, bias=-33.25 / 1024 - 0.4995)
    act(X("G4", 0, m), X("G4", 0, m), bias=MAG)
    act(X("G4", 0, m), X("G4", 0, m), bias=-MAG, fn=AF.Relu)
    mms(X("P4", 0, m), [("IDF", X("U", 0, m)), ("NKF", X("G4", 0, m))])
    act(X("G5", 0, m), X("P4", 0, m))
    dma(X("R", 0, 5120, rows=L_CALL), X("G5", 0, m))
    gat("s", X("PF2", 0, 1024), X("E", 0, 3856), X("LS0", 0, 64))
    for u in range(2):
        dma(X3("LD", 0, 4, 16 * u, 16 * u + 16), X("PF2", 0, 1024, rows=0))
    tr(X("PT2", 0, 128), X3("LD", 0, 4, 0, 32))
    cp(X("LS1", 0, 64), IN(X("PT2", 0, 128), X("WO", 40, 44)))
    columns(1, 0, 64)
    LAST = (L_COPY, L_CALL, L_CALLEE, L_SITE)
    for lane in LAST:
        dma(window("W1", 1, lane), X("K32", 0, 400))
        dma(window("W2", 1, lane), X("KM", 0, 400))

    dissent(1)
    splits(1)
    clone_list(1)
    tally(1)
    places(1)
    formals(1)
    ts(X("TMP", 4, 5), col(13), -1.0, OP.mult, 256.0, OP.add)
    ts(X("TMP", 5, 6), col(13), 767.5, OP.add)
    ts(X("S1", 0, 32), X("PX", 48, 80), X("TMP", 5, 6), OP.is_ge, X("TMP", 4, 5), OP.mult)
    tt(X("S1", 0, 32), X("S1", 0, 32), X("PX", 48, 80), OP.add)
    ts(X("YO", 0, 32), X("S1", 0, 32), 1280.0, OP.min)
    ts(X("YF", 0, 768), X("FV", 0, 768), -1.0, OP.mult, 15.0, OP.add)
    act(X("YF", 768, 1280), IN(X("FV", 0, 1296), X("YO", 0, 32)), scale=-1.0, bias=15.0)
    dma(HB(T.yform[:, :]), X("YF", 0, 1280))
    scatter("v", 1, 0, VSHARE, 2)
    scatter("s", 1, VSHARE, 5120, 2)
    m = 400
    bank = [X(b, 0, m) for b in ("P0", "P1", "P4", "P5")]
    for f, lane in enumerate(LAST):
        dma(X("Z1", 2 * f * m, (2 * f + 1) * m), window("W1", 1, lane), "s")
        dma(X("Z1", (2 * f + 1) * m, (2 * f + 2) * m), window("W2", 1, lane))
    y = [bank[0]] + [X("Y", f * m, f * m + m) for f in range(4)]
    for f in range(4):
        act(bank[f], X("Z1", 2 * f * m, (2 * f + 1) * m), bias=MAG)
        tt(y[f], bank[f], X("Z1", (2 * f + 1) * m, (2 * f + 2) * m), OP.add)
    ts(X("KP", 0, m), y[0], 0.0, OP.is_le, -BIG, OP.mult)
    tt(y[1], y[0], y[1], OP.max)
    dma(HB(T.ycaller[:, :]), y[1])
    for f, out, q in ((2, T.ycallee, "s"), (3, T.ysite, "y")):
        o = y[4] if f == 2 else X("Z1", 0, m)
        scan(o, X("KP", 0, m), y[f], carry(("SHDF", X("Y", f * m - 1, f * m))), OP.add, OP.max)
        dma(HB(out[:, :]), o, q)

    def plan(before, gap, rank_):
        users = [[] for _ in nodes]
        for k, ds in enumerate(before):
            for d in ds:
                users[d].append(k)
        left = [len(ds) for ds in before]
        can = [gap(None, k) for k in range(len(nodes))]
        free = {q: 0.0 for q in list(Q) + [None]}
        ready = {q: [k for k in range(len(nodes)) if left[k] == 0 and nodes[k]["q"] == q] for q in free}
        order, start = [], [0.0] * len(nodes)
        while len(order) < len(nodes):
            soon, first = min((max(can[k], free[q]) + nodes[k]["busy"], k) for q in ready for k in ready[q])
            q = nodes[first]["q"]
            k = max([x for x in ready[q] if x == first or can[x] < soon], key=lambda x: (rank_[x], -x))
            start[k] = max(can[k], free[q])
            free[q] = start[k] + nodes[k]["busy"]
            ready[q].remove(k)
            order.append(k)
            for u in users[k]:
                can[u] = max(can[u], start[k] + gap(k, u))
                left[u] -= 1
                if left[u] == 0:
                    ready[nodes[u]["q"]].append(u)
        return order, start

    def wake(a, b): return 0.0 if nodes[a]["q"] == nodes[b]["q"] == "p" else WAKE
    def ahead(d, k): return 0.0 if d is None else nodes[d]["late"] + wake(d, k)
    def back(u, k): return nodes[k]["late"] - nodes[k]["busy"] + (0.0 if u is None else nodes[u]["busy"] + wake(u, k))

    deps = [sorted(x["deps"]) for x in nodes]
    after = [[] for _ in nodes]
    way = [0.0] * len(nodes)
    for k in range(len(nodes) - 1, -1, -1):
        way[k] += nodes[k]["late"]
        for d in deps[k]:
            way[d] = max(way[d], way[k] + WAKE)
            after[d].append(k)
    best = None
    for _ in range(PASSES):
        order, start = plan(deps, ahead, way)
        end = [start[k] + nodes[k]["late"] for k in range(len(nodes))]
        if best is None or max(end) < best[0]:
            best = (max(end), order)
        way = [t + nodes[k]["busy"] for k, t in enumerate(plan(after, back, end)[1])]
    count = {q: 0 for q in Q}
    waited = {q: {} for q in Q}
    token = {}
    for k in best[1]:
        x = nodes[k]
        q = x["q"]
        if x["sem"] is None:
            count[q] += 1
            token[k] = ("q" + q, count[q])
        else:
            token[k] = (x["sem"], x["inc"])
        if q is None:
            continue
        need = {}
        for d in x["deps"]:
            if not (q == "p" and nodes[d]["q"] == "p"):
                need[token[d][0]] = max(need.get(token[d][0], 0), token[d][1])
        for s_, v_ in need.items():
            if waited[q].get(s_, 0) < v_:
                Q[q].wait_ge(T.sem[s_], v_)
                waited[q][s_] = v_
        call = x["fn"]()
        if call is not None:
            call.then_inc(T.sem[token[k][0]], x["inc"])
    final = {}
    for s_, v_ in token.values():
        final[s_] = max(final.get(s_, 0), v_)
    for s_, v_ in final.items():
        if all(waited[q].get(s_, 0) < v_ for q in Q):
            g.sync.wait_ge(T.sem[s_], v_)
